import numpy as np, ml_dtypes
CORES = [2,3,42,43,82,83,122,123]
N = 8
BF = ml_dtypes.bfloat16
S, CAP, WC, NB, RO, OC, SHO = 192, 32, 4096, 128, 3, 3, 5
MU = (61, 173, 89, 347)
FC, L = 16 * NB, N * CAP
KB = (np.arange(16)[:, None] >> np.arange(4)) & 1
def cells(x):
    p = [(x[..., e, :, None] >> 2) + KB[:, e] for e in range(4)]
    w = [np.where(KB[:, e] == 1, x[..., e, :, None] & 3, 4 - (x[..., e, :, None] & 3)) for e in range(4)]
    i = (((p[0] * (2 * p[1] + 1)) >> 2) + MU[0] * p[2] + MU[1] * p[3]) & (WC - 1)
    b = (((p[2] * (2 * p[3] + 1)) >> 2) + MU[2] * p[0] + MU[3] * p[1]) & (NB - 1)
    return i, b, w[0] * w[1] * w[2] * w[3]
def parts(rng):
    cf = rng.integers(0, 237, (N, 8, 1, WC)) + rng.integers(0, 4, (N, 8, 16, WC))
    ft = rng.integers(0, 256, (N, 8, 16, FC)); ft[:, ::2, :4] = 96 + (ft[:, ::2, :4] >> 2)
    tg = rng.integers(0, 256, (N, 8, 16, S)); x = rng.integers(0, 256, (N, 8, 4, S))
    fav = rng.integers(0, N, (N, 8, 1)); hit = rng.random((N, 8, S)) < rng.choice(np.array([0.0, 0.1, 0.3, 0.5]), (N, 8, 1))
    x[:, :, OC] = np.where(hit, (fav << SHO) + (x[:, :, OC] & ((1 << SHO) - 1)), x[:, :, OC])
    return cf, ft, tg, x
def pack(cf, ft, tg, x):
    b = lambda v, n: np.ascontiguousarray(v.reshape(N, 128, n)).astype(np.float32).astype(BF)
    return {"cf": b(cf, WC), "ft": b(ft, FC), "tg": b(tg, S), "x0": np.ascontiguousarray(x.reshape(N, 32, S)).astype(np.int32)}
def setup_inputs(rng):
    return pack(*parts(rng))
def setup_inputs_spread(rng):
    cf, ft, tg, x = parts(rng)
    cf = np.where(rng.random((N, 8, 1, WC)) < 0.5, rng.integers(0, 241, cf.shape), (241 * rng.random(cf.shape) ** 4).astype(np.int64))
    v = np.minimum(np.exp2(8 * rng.random(ft.shape)).astype(np.int64) - 1, 255); ft = np.where(rng.random((N, 8, 1, FC)) < 0.5, v, 255 - v)
    v = np.minimum(np.exp2(8 * rng.random(tg.shape)).astype(np.int64) - 1, 255); tg = np.where(rng.random((N, 8, 1, S)) < 0.5, v, 255 - v)
    v = np.minimum((256 * rng.random(x.shape) ** 2).astype(np.int64), 255); x = np.where(rng.random((N, 8, 4, 1)) < 0.5, v, 255 - v)
    return pack(cf, ft, tg, x)
def setup_inputs_ends(rng):
    e = lambda top, *shape: top * rng.integers(0, 2, shape)
    cf = e(240, N, 8, 16, WC); kind = rng.integers(0, 4, (N, 8, 1, NB, 1)); fv = e(255, N, 8, 16, NB, 16)
    fv = np.ascontiguousarray(np.where(kind == 0, 0, np.where(kind == 1, 255, fv)))
    rec = rng.integers(0, 3, (N, 8, 1, S)); tg = np.where(rec == 0, 0, np.where(rec == 1, 255, e(255, N, 8, 16, S)))
    x = e(255, N, 8, 4, S); x[:, :, OC] = np.where(rng.random((N, 8, S)) < 0.2, rng.integers(0, 256, (N, 8, S)), x[:, :, OC])
    z = np.zeros((4, 1), np.int64); z[OC] = 255; zi, zb, zw = cells(z); live = zw[0] > 0; zi = zi[0][live]; zb = zb[0][live]
    tb = cells(np.full((4, 1), 255))[1][0]; r = N - 1
    for g in range(8):
        for turn in ((0, 1) if g % 2 else (1, 0)):
            if turn == 0: cf[r, g][:, zi] = 0; cf[r, g][15, zi] = 240; fv[r, g][:, zb] = 255; fv[r, g][:, zb, 15] = 0
            else: fv[r, g][:, tb] = 255
    x[0, :, :, 0] = z[:, 0]; tg[0, :, :, 0] = 255; x[0, :, :, 1] = 255; tg[0, :, :, 1] = 0
    x[r, 7, OC, rng.permutation(S)[:CAP + 4]] = 255
    h = int(np.flatnonzero((x[r, 7, OC] >> SHO) == r)[CAP - 1]); x[r, 7, :, h] = 255; tg[r, 7, :, h] = 0
    return pack(cf, fv, tg, x)
def setup_inputs_corners(rng):
    cf, ft, tg, x = parts(rng)
    mode = rng.integers(0, 4, (N, 8, 1, S)); low = np.where(mode == 0, 0, np.where(mode == 1, 2, np.where(mode == 2, 3, x & 3)))
    hi = np.where(rng.random(x.shape) < 0.3, 252 * rng.integers(0, 2, x.shape), x - (x & 3)); x = hi + low
    own = np.zeros((N, 8, S), np.int64)
    for q in range(N):
        for g in range(8):
            o = int(rng.integers(0, N)); n = int(rng.choice(np.array([0, 1, CAP - 1, CAP, CAP + 1, S])))
            if q == 0: o = 1 + g % (N - 1); n = (CAP, CAP + 1, S, CAP - 1, 1, 0, CAP, CAP + 1)[g]
            own[q, g] = rng.permutation(np.concatenate([np.full(n, o), (o + rng.integers(1, N, S - n)) % N]))
    x[:, :, OC] = (own << SHO) + (hi[:, :, OC] & ((1 << SHO) - 1)) + low[:, :, OC]
    few = np.array([0, 1, 254, 255]); v = rng.choice(np.array([119, 120, 121, 127, 128, 129, 135, 136, 137]), (8, 16))
    v[5, 4:] = rng.choice(np.array([0, 1, 100, 254, 255]), 12)
    for g in (1, 3, 5, 7):
        ft[:, g, :4] = v[g, :4, None]; ft[:, g, 4:] = v[5, 4:, None] if g == 5 else rng.choice(few, (N, 12, FC))
        tg[:, g, :4] = v[g, :4, None] + rng.integers(-1, 2, (N, 4, S)); tg[:, g, 4:] = rng.choice(few, (N, 12, S))
    tg[:, 5] = np.where(rng.random((N, 1, S)) < 0.25, v[5][:, None], tg[:, 5])
    for o in range(N):
        two = np.flatnonzero(own[0, 5] == o)[:2]
        if len(two) == 2: x[0, 5, :, two[1]] = x[0, 5, :, two[0]]; tg[0, 5, :, two[0]] = v[5]; tg[0, 5, :, two[1]] = 255
    return pack(cf, ft, tg, x)
def setup_inputs_crowd(rng):
    cf, ft, tg, x = parts(rng); turn = int(rng.integers(0, N)); e = (OC + 1) % 4
    for g in range(8):
        o = (g + turn) % N
        for again in range(64):
            pt = 4 * rng.integers(0, 64, 4); pt[OC] = (o << SHO) + 4 * rng.integers(0, 1 << (SHO - 2))
            two = np.stack([pt, pt], axis=1); two[e, 1] = (two[e, 1] + 64) & 255; zi, zb, zw = cells(two)
            if zi[0, 0] != zi[1, 0] and zb[0, 0] != zb[1, 0]: break
        v = pt[None, :, None] + rng.integers(0, 3, (N, 4, S))
        if g == 1: v[N - 1, e, CAP - 1] = (v[N - 1, e, CAP - 1] + 64) & 255
        if g == 5: v[0, e, 0] = (v[0, e, 0] + 64) & 255
        if g % 4 == 2: v[:, e] = (v[:, e] + 64 * rng.integers(0, 3, (N, S))) & 255
        if g % 4 == 3: v[:, :, 1::2] = x[:, g, :, 1::2]
        x[:, g] = v
    return pack(cf, ft, tg, x)
def setup_inputs_calm(rng):
    cf, ft, tg, x = parts(rng)
    cf = 235 * rng.integers(0, 2, (N, 8, 1, WC)) + rng.integers(0, 6, (N, 8, 16, WC))
    step = 128 + (np.arange(8)[:, None] & 3) * (1 - 2 * rng.integers(0, 2, (8, 4)))
    ft[:, :, :4] = step[None, :, :, None]; tg[:, :, :4] = step[None, :, :, None]
    ft[:, 1::2, 4:] = rng.choice(np.array([0, 1, 2, 3, 252, 253, 254, 255]), (N, 4, 12, FC))
    tg[:, :, 4:] = 255 * rng.integers(0, 2, (N, 8, 12, S))
    for g in (0, 4):
        low = rng.integers(0, 2 if g == 0 else 1, (N, 16, WC)); low[:, 0] = 0
        cf[:, g] = np.where(rng.random((N, 1, WC)) < 0.5, low, cf[:, g]); tg[:, g, 4:] = np.where(rng.random((N, 1, S)) < 0.5, 0, tg[:, g, 4:])
        if g == 0: x[0, g, :, 0] = x[0, g, :, 0] - (x[0, g, :, 0] & 3)
        i, b, w = cells(x[0, g, :, :1]); tg[0, g, 4:, 0] = 0
        cf[int(x[0, g, OC, 0]) >> SHO, g, :, int(i[0, np.argmax(w[0])])] = 0 if g == 4 else (np.arange(16) >= int(rng.integers(1, 16))).astype(np.int64)
    for q, g in ((0, 3), (N - 1, 6)):
        o = (q + 1 + int(rng.integers(0, N - 1))) % N; r = (x[q, g, OC] - (o << SHO)) & 255
        r = np.where((r < (1 << SHO) + 12) | (r >= 244), (r + 128) & 255, r)
        s = rng.permutation(S)[:8]; r[s] = (1 << SHO) - 1 if step[g, OC] > 128 else 0
        x[q, g, OC] = ((o << SHO) + r) & 255; tg[q, g, 4:, s] = 255
    return pack(cf, ft, tg, x)
def check_inputs(d):
    bad = []
    for k, top in (("cf", 240), ("ft", 255), ("tg", 255), ("x0", 255)):
        v = np.asarray(d[k]).astype(np.float64)
        if not (np.min(v) >= 0 and np.max(v) <= top): bad.append("range of " + k)
        if np.any(v != np.floor(v)): bad.append("whole numbers of " + k)
    return bad
def firsts(lanes, key):
    return lanes[np.unique(key[lanes], return_index=True)[1]]
def reference(cf, ft, tg, x0):
    C = cf.astype(np.float32).astype(np.int64).reshape(N, 8, 16, WC); F = ft.astype(np.float32).astype(np.int64).reshape(N, 8, 16, FC)
    t = tg.astype(np.float32).astype(np.int64).reshape(N, 8, 16, S); x = x0.astype(np.int64).reshape(N, 8, 4, S); ys = np.zeros((N, 8, 16, S), np.int64)
    for rnd in range(RO):
        own = x[:, :, OC] >> SHO
        h = (own[:, :, None, :] == np.arange(N)[:, None]).astype(np.int64)
        place = np.take_along_axis(np.add.accumulate(h, axis=3) - h, own[:, :, None, :], 2)[:, :, 0]
        q, g, s = np.nonzero(place < CAP); o = own[q, g, s]; l = CAP * q + place[q, g, s]
        X = np.zeros((N, 8, 4, L), np.int64); T = np.zeros((N, 8, 16, L), np.int64); live = np.zeros((N, 8, L), bool)
        X[o, g, :, l] = x[q, g, :, s]; T[o, g, :, l] = t[q, g, :, s]; live[o, g, l] = True
        i, b, w = cells(X)
        m = np.argmax(np.take_along_axis(C, i.reshape(N, 8, 1, L * 16), 3), axis=2).reshape(N, 8, L, 16)
        v = np.take_along_axis(F, (16 * b + m).reshape(N, 8, 1, L * 16), 3).reshape(N, 8, 16, L, 16)
        y = np.sum(v * w[:, :, None], axis=4) >> 8
        sg = np.sign(T - y)
        k = np.argmax(w, axis=3)[..., None]
        ci, cb, cm = [np.take_along_axis(z, k, 3)[..., 0] for z in (i, b, m)]; fc = 16 * cb + cm
        u = np.take_along_axis(F, (16 * cb[..., None] + np.arange(16)).reshape(N, 8, 1, L * 16), 3).reshape(N, 8, 16, L, 16)
        up = np.sign(np.sum(sg[..., None] * u, axis=2))
        for r in range(N):
            for a in range(8):
                lanes = np.flatnonzero(live[r, a])
                win = firsts(lanes, ci[r, a]); C[r, a][:, ci[r, a, win]] += up[r, a, win].T
                win = firsts(lanes, fc[r, a]); at = fc[r, a, win]; F[r, a][:, at] = np.clip(F[r, a][:, at] + sg[r, a][:, win], 0, 255)
        back = y[o, g, :, l]
        ys[q, g, :, s] += back
        x[q, g, :, s] = (x[q, g, :, s] + np.clip(back[:, :4] - 128, -8, 8)) & 255
    yc = np.sum(C * (np.arange(16) + 1)[:, None], axis=2)
    return {"yc": yc.astype(np.float32), "yf": F.reshape(N, 128, FC).astype(np.float32).astype(BF), "ys": ys.reshape(N, 128, S).astype(np.float32), "yx": x.reshape(N, 32, S).astype(np.float32)}

@@ -1,0 +1,735 @@
+import numpy as np
+from concourse.bass import DstId, RemoteDMATransfer
+from concourse.mybir import dt, AluOpType, AxisListType, ActivationFunctionType
+A = AluOpType
+AF = ActivationFunctionType
+N, S, CAP, RO = 8, 192, 32, 3
+B0 = 160.0
+OFF = (0, 61, 173, 234)
+BOFF = (0, 89, 91, 52)
+NP = 11
+TAG = [""]
+CY, GA, SCA, WAKE, SENT, LAND, SLACK = 1.04e-3, 1.6, 3.8, 0.09, 3.1, 0.9, 0.15
+SPLIT = (4, 2)
+EVAC, MZG, MGV, EQV, MBS, VECQ = "sv", 6, 24, 8, 4, "gss"
+TRIES, ORDER = 1200, []
+bf, f32, i32, u16, f16 = "bfloat16", "float32", "int32", "uint16", "float16"
+CB = ["Z1", "Z2", "Z3", "Zm", "orep", "xrep", "pow", "big", "pen", "cnt", "ycw", "I64", "In"]
+CH = ["ZA", "b0", "b1", "b2", "b3", "b4", "b5", "b6", "b7", "b8", "Ih"]
+SB = {
+    "C": ([128, 4608], bf), "Fr": ([128, 2304], bf), "Fp": ([128, 2304], bf), "M": ([128, 4864], bf), "YC": ([128, 4608], f32),
+    "X": ([128, S], i32), "tgr": ([128, S], bf), "tgc": ([128, S], bf), "st": ([128, S], i32), "ob": ([128, S], bf), "xb": ([128, S], bf),
+    "h": ([128, S], bf), "cum": ([128, S], bf), "val": ([128, S], bf), "Fh": ([128, S], bf), "lim": ([128, S], bf),
+    "yg": ([128, RO, S], bf), "sg": ([128, RO, S], bf), "ysO": ([128, S], f32), "xO": ([128, S], f32),
+    "SF": ([128, N * S], bf), "ST": ([128, N * S], bf), "RY": ([128, N * S], bf), "slot": ([128, 12], u16),
+    "RF0": ([128, 256], bf), "RF1": ([128, 256], bf), "RF2": ([128, 256], bf),
+    "RT0": ([128, 256], bf), "RT1": ([128, 256], bf), "RT2": ([128, 256], bf),
+    "yb0": ([128, 256], bf), "yb1": ([128, 256], bf), "yb2": ([128, 256], bf),
+    "ones": ([128, 256], bf), "Z": ([128, 512], bf), "IW": ([128, 136], bf), "BD": ([128, 128], bf), "BDt": ([128, 128], bf),
+    "cb": ([128, len(CB), 144], bf), "ch": ([128, len(CH), 144], f16), "MB": ([128, NP - 1, 144], bf),
+    "VEC": ([128, 4, NP * 16], bf), "comb": ([128, 144], bf), "PAT": ([128, NP - 1, 16], bf),
+    "pc": ([128, 2], i32), "col": ([128, 16], f32), "J": ([128, 16], f32), "RM": ([128, 16], f32), "two": ([128, 16], f32), "pw": ([128, 16], f32),
+    "RST": ([128, 256], bf), "trash": ([128, 32], f32), "IOTA": ([128, 2048], i32),
+    "SC": ([128, 4096], f32), "E": ([128, 256], i32), "R2": ([128, 2, 128], bf), "T2": ([128, 256], bf),
+    "hv": ([128, 64], f32), "hp": ([128, 64], f32), "hi": ([128, 64], i32), "ML": ([128, 64], u16),
+    "bv": ([128, 64], f32), "bp": ([128, 64], f32), "bi": ([128, 64], i32), "BB": ([128, 256], bf),
+    "fv": ([128, 256], f32), "fi": ([128, 256], i32), "Q": ([128, 256], f16),
+    "Mo": ([128, 1024], bf), "FL": ([128, 256], u16), "VG": ([128, 4096], bf),
+    "VW0": ([128, 64, 4, 4], f16), "VW1": ([128, 64, 4, 4], f16), "VW2": ([128, 64, 4, 4], f16), "VW3": ([128, 64, 4, 4], f16), "Wab": ([128, 1024], bf), "acc": ([128, 256], f32),
+    "KS": ([128, 32], f32), "KY": ([128, 32], f32), "KL": ([128, 32], u16), "BI": ([128, 16], i32), "AI": ([128, 32], i32), "y16": ([128, 256], f16), "BL": ([128, 16], u16), "dd": ([128, 16], f32), "KN": ([128, 16], f32), "GM": ([128, 8], f32),
+    "KR": ([128, 512], f16), "EQ0": ([128, 16, 128], bf), "EQ1": ([128, 16, 128], bf), "LS": ([128, 512], bf),
+    "bad": ([128, 32], f32), "OL": ([128, 32], u16),
+    "Ms": ([128, 256], bf), "Co": ([128, 256], bf), "Fo": ([128, 256], bf), "Cn": ([128, 256], bf), "Fn": ([128, 256], bf),
+    "UG": ([128, 4096], bf), "PR": ([128, 4096], bf), "TR": ([128, 256], bf), "TB": ([128, 256], bf), "Mn": ([128, 256], bf),
+    "sn": ([128, 256], f32), "e16": ([128, 16], i32), "ycn": ([128, 256], f32),
+}
+SCRATCH = {k: ("sbuf", v[0], v[1]) for k, v in SB.items()}
+SCRATCH["P01"] = ("psum", [128, 64, 4, 4], f32)
+for _k in range(2, 8):
+    SCRATCH["P%d" % _k] = ("psum", [128, 512], f32)
+SEMAPHORES = (["cv", "ct", "cs", "cg", "dx", "dc0", "dc1", "dc2", "dc3", "df", "dtg", "dm0", "dm1", "dm2", "out"]
+              + [p + str(r) for p in ("af", "at", "ay", "lf", "lt", "ly") for r in range(RO)])
+
+
+def plan(topo, cores, src):
+    k = cores.index(src)
+    turn = cores[k + 1:] + cores[:k]
+    far = [d for d in turn if topo.chip(d) != topo.chip(src)]
+    near = [d for d in turn if topo.chip(d) == topo.chip(src)]
+    pool = list(topo.engines(src, far[0]))
+    calls = []
+    for n in SPLIT:
+        part, far = far[:n], far[n:]
+        w = len(pool) // n
+        calls.append({d: pool[w * j:w * j + w] for j, d in enumerate(part)})
+    calls[0][near[0]] = [e for e in topo.engines(src, near[0]) if e not in pool]
+    return calls
+
+
+def patterns():
+    p = {}
+
+    def put(k, row, c, v):
+        p[(row, 16 * k + c)] = float(v)
+    for x in range(4):
+        c, lo, hi = 4 * x + 3, x & 1, x >> 1
+        for k, ru, rv in ((0, 0, 1), (3, 2, 3)):
+            put(k, ru, c, 1); put(k, 12, c, lo - B0)
+            put(k + 1, rv, c, 2); put(k + 1, 12, c, -2 * B0); put(k + 1, 13, c, 2 * hi + 1)
+        put(2, 2, c, 244); put(2, 3, c, 692); put(2, 12, c, 14080)
+        put(5, 0, c, 356); put(5, 1, c, 364)
+        put(9, x, c, 128)
+        for base, eu, ev in ((0, 0, 1), (4, 2, 3)):
+            su, sv = (1 if lo else -1), (1 if hi else -1)
+            put(6, 4 + eu, base + x, 4 * su); put(6, eu, base + x, -16 * su); put(6, 12, base + x, 16 * B0 * su + (0 if lo else 16))
+            put(7, 4 + ev, base + x, sv); put(7, ev, base + x, -4 * sv); put(7, 12, base + x, 4 * B0 * sv + (0 if hi else 4))
+    for role, ru, rv in ((8, 8, 9), (9, 10, 11)):
+        up = 1 if role == 8 else 32
+        put(6, ru, role, up); put(6, 12, role, -B0 * up)
+        put(7, rv, role, 2); put(7, 12, role, -2 * B0); put(7, 13, role, 1)
+    put(6, 12, 12, 4); put(7, 12, 12, 1)
+    put(8, 10, 8, 244); put(8, 11, 8, 692); put(8, 12, 8, 14080); put(8, 8, 9, 356 * 32); put(8, 9, 9, 364 * 32)
+    runs = []
+    by = {}
+    for (row, c), v in sorted(p.items()):
+        by.setdefault((row, v), []).append(c)
+    for (row, v), cs in by.items():
+        while cs:
+            best = [cs[0]]
+            for c2 in cs[1:]:
+                st, run = c2 - cs[0], [cs[0]]
+                while run[-1] + st in cs:
+                    run.append(run[-1] + st)
+                if len(run) > len(best):
+                    best = run
+            st = best[1] - best[0] if len(best) > 1 else 1
+            runs.append((row // 4, slice(row % 4, row % 4 + 1), slice(best[0], best[-1] + 1, st), len(best), v))
+            cs = [c for c in cs if c not in best]
+    c0 = 16 * (NP - 1)
+    for q, vals in enumerate(((0.25, B0, -0.375), (1.0, 0, 0), (0.25, B0, -0.125), (0, 1.0, 0))):
+        for j, v in enumerate(vals):
+            if v:
+                runs.append((q, slice(0, 4), slice(c0 + j, c0 + j + 1), 4, float(v)))
+    return runs
+
+
+def rank_program(g, core, T, topo):
+    me = T.rank_of(core)
+    if me is None:
+        return
+    cores = list(T.cores)
+    V, P, Sc, Y = g.vector, g.tensor, g.scalar, g.sync
+    Qs = {"v": V, "t": P, "s": Sc, "g": g, "y": Y}
+    total, clock, snap = {}, {q: {} for q in Qs}, {}
+    wr, rd, bank = {}, {}, {}
+
+    def need(q, ev):
+        sem, val = ev
+        if sem[0] == "d":
+            val = total[sem]
+        if clock[q].get(sem, 0) >= val:
+            return
+        Qs[q].wait_ge(T.sem[sem], val)
+        clock[q][sem] = val
+        for k, v in snap.get((sem, val), {}).items():
+            if clock[q].get(k, 0) < v:
+                clock[q][k] = v
+
+    def deps(q, r, w, x):
+        evs = {}
+
+        def add(ev):
+            if ev and evs.get(ev[0], 0) < ev[1]:
+                evs[ev[0]] = ev[1]
+        for k in r:
+            add(wr.get(k))
+        for k in w:
+            add(wr.get(k))
+            for ev in rd.get(k, {}).items():
+                add(ev)
+        for b in x:
+            for q2, ev in bank.get(b, {}).items():
+                if q2 != q:
+                    add(ev)
+        for ev in evs.items():
+            need(q, ev)
+
+    def done(q, ev, r, w, x):
+        snap[ev] = dict(clock[q])
+        for k in r:
+            rd.setdefault(k, {})[ev[0]] = ev[1]
+        for k in w:
+            wr[k] = ev
+            rd[k] = {}
+        for b in x:
+            bank.setdefault(b, {})[q] = ev
+
+    ops = []
+
+    def size(ap):
+        n = 1
+        for d in ap.shape[1:]:
+            n *= d
+        return n
+
+    def cost(n, k):
+        if k == "g":
+            return 0.05 + n * GA * CY
+        if k == "s":
+            return 0.05 + n * SCA * CY
+        return 0.03 + max(64, n * k) * CY
+
+    def op(q, fn, r=(), w=(), c=0.1, o=(), lat=0.0, kind="c", extra=None):
+        x = sorted({int(k[1]) for k in list(r) + list(w) + list(o) if k[0] == "#"})
+        ops.append(dict(q=q, fn=fn, r=list(r), w=list(w), x=x, o=list(o), c=c, lat=lat, kind=kind, extra=extra, tag=TAG[0]))
+
+    def dma(q, out, in_, sem, r=(), w=(), lat=2.2):
+        op(q, lambda: Qs[q].dma_start(out, in_), r, w, 0.1, (), lat, "d", sem)
+
+    def mm(items, r, w, o=()):
+        def fn():
+            for it in items:
+                i = P.matmul(*it)
+            return i
+        op("t", fn, r, w, sum(0.005 + max(64, size(it[2])) * CY for it in items), o, 0.1)
+
+    def group(out, pairs, start=True, stop=True):
+        return [(out, l, rr, start and k == 0, stop and k == len(pairs) - 1) for k, (l, rr) in enumerate(pairs)]
+
+    def ts(out, in0, s1, s2, op0, op1=None, r=(), w=(), k=1):
+        if op1 is None:
+            op("v", lambda: V.tensor_scalar(out, in0, s1, None, op0), r, w, cost(size(out), k))
+        else:
+            op("v", lambda: V.tensor_scalar(out, in0, s1, s2, op0, op1), r, w, cost(size(out), k))
+
+    def tt(out, a, b, o, r=(), w=()):
+        ps = any(k[0] == "#" for k in list(r) + list(w))
+        op("v", lambda: V.tensor_tensor(out, a, b, o), r, w, cost(size(b), 1 if ps else 2))
+
+    def cp(out, a, r=(), w=(), k=1):
+        op("v", lambda: V.tensor_copy(out, a), r, w, cost(size(a if k == "s" else out), k))
+
+    def ms(out, k, r=(), w=()):
+        op("v", lambda: V.memset(out, k), r, w, cost(size(out), 0.5))
+
+    def scan(out, d0, d1, init, o0, o1, r, w, k=1):
+        op("v", lambda: V.tensor_tensor_scan(out, d0, d1, init, o0, o1), r, w, cost(size(out), k))
+
+    def act(out, a, fn=AF.Copy, r=(), w=(), k=1, **kw):
+        op("s", lambda: Sc.activation(out, a, fn, **kw), r, w, cost(size(out), k))
+
+    plans = {c: plan(topo, cores, c) for c in cores}
+    arrive = sum(len(call.get(core, ())) for c in cores for call in plans[c])
+    leave = sum(len(e) for call in plans[core] for e in call.values())
+
+    def send(kind, rnd, src, dst, r, w, landed):
+        ls = "l%s%d" % (kind, rnd)
+
+        def fn():
+            for call in plans[core]:
+                trs = []
+                for d, engines in call.items():
+                    rid, pid, _ = topo.addr(d)
+                    trs.append(RemoteDMATransfer(dst_ids=[DstId(rid=rid, pnc=pid)], dma_engine_mask=sum(1 << e for e in engines),
+                                                 remote_sem=T.sem["a%s%d" % (kind, rnd)], src=src(cores.index(d)), dst=dst))
+                g.remote_dma_fused(trs, local_sem=T.sem[ls])
+        op("g", fn, r, w, 0.6 * len(SPLIT), ["eng"], SENT, "r", (ls, landed))
+
+    def emit(e):
+        q = e["q"]
+        TAG[0] = e["tag"]
+        deps(q, e["r"], e["w"], e["x"])
+        if q == "g" and e["kind"] == "c" and "cg" in total:
+            need(q, ("cg", total["cg"]))
+        if e["kind"] == "r":
+            ls, landed = e["extra"]
+            e["fn"]()
+            total[ls] = leave
+            total["a" + ls[1:]] = arrive
+            wr[landed] = ("a" + ls[1:], arrive)
+            ev = (ls, leave)
+        else:
+            sem, n = (e["extra"], 16) if e["kind"] == "d" else ("c" + q, 1)
+            total[sem] = total.get(sem, 0) + n
+            e["fn"]().then_inc(T.sem[sem], n)
+            ev = (sem, total[sem])
+        done(q, ev, e["r"], e["w"], e["x"])
+
+    def schedule(bias):
+        n = len(ops)
+        pre = [dict() for _ in range(n)]
+        lw, lr, lo = {}, {}, {}
+        for i, e in enumerate(ops):
+            def edge(j, d):
+                if j != i and pre[i].get(j, -1.0) < d:
+                    pre[i][j] = d
+            for k in e["r"] + e["w"]:
+                if k in lw:
+                    edge(*lw[k])
+            for k in e["w"]:
+                for j in lr.get(k, ()):
+                    edge(j, ops[j]["lat"] + WAKE)
+            for k in e["o"]:
+                if k in lo:
+                    edge(lo[k], 0.0)
+                lo[k] = i
+            for k in e["r"]:
+                lr.setdefault(k, []).append(i)
+            for k in e["w"]:
+                lw[k] = (i, e["lat"] + WAKE)
+                lr[k] = []
+            if e["kind"] == "r":
+                lw[e["extra"][1]] = (i, e["lat"] + LAND)
+        post = [[] for _ in range(n)]
+        for i in range(n):
+            for j, d in pre[i].items():
+                post[j].append((i, d))
+        level = [0.0] * n
+        for i in range(n - 1, -1, -1):
+            level[i] = ops[i]["c"] + max([ops[i]["lat"]] + [d + level[j] for j, d in post[i]])
+        left = [len(p) for p in pre]
+        ready = [0.0] * n
+        free = {q: 0.0 for q in Qs}
+        held = {}
+        avail = [i for i in range(n) if not left[i]]
+        order = []
+        while avail:
+            st = {}
+            for i in avail:
+                e = ops[i]
+                t = max(ready[i], free[e["q"]])
+                for b in e["x"]:
+                    for q2, t2 in held.get(b, {}).items():
+                        if q2 != e["q"] and t2 > t:
+                            t = t2
+                st[i] = t
+            first = min(avail, key=lambda i: st[i])
+            q = ops[first]["q"]
+            near = [i for i in avail if ops[i]["q"] == q and st[i] <= st[first] + SLACK * ops[first]["c"] + 0.02]
+            i = max(near, key=lambda i: (level[i] + bias.get(ops[i]["tag"] + q, 0.0), -i))
+            e = ops[i]
+            end = st[i] + e["c"]
+            free[q] = end
+            for b in e["x"]:
+                held.setdefault(b, {})[q] = end + e["lat"] + WAKE
+            order.append(i)
+            avail.remove(i)
+            for j, d in post[i]:
+                ready[j] = max(ready[j], end + d)
+                left[j] -= 1
+                if not left[j]:
+                    avail.append(j)
+        return max(ready + list(free.values())), order
+
+    cb = lambda n, a=0: T.cb[:, CB.index(n), a:a + 128]
+    ch = lambda n, a=0: T.ch[:, CH.index(n), a:a + 128]
+    I = T.IW[:, 8:136]
+    col = lambda j: T.col[:, j:j + 1]
+    RM = lambda j: T.RM[:, j:j + 1]
+    RC, LT8, INIT, Z1C, OC, LT4, R1, ZAC, SUB, THR, S1, S2 = range(12)
+    P01 = T.P01
+    now = [0]
+
+    def tag(s):
+        TAG[0] = s + str(now[0])
+
+    def pk(b, lo=0, hi=512):
+        return ["#%d_%d" % (b, j) for j in range(lo // 16, (hi + 15) // 16)]
+
+    def ps(b, lo=0, hi=512):
+        return P01[:, 32 * b + lo // 16:32 * b + hi // 16] if b < 2 else T["P%d" % b][:, lo:hi]
+
+    tag("c0")
+    ms(T.X[:], 0, w=["X0"])
+    ms(T.ones[:], 1.0, w=["ones"])
+    for k in range(4):
+        dma("y", T.C[:, 1024 * k:1024 * k + 1024], T.cf[:, 1024 * k:1024 * k + 1024], "dc%d" % k, w=["C%d" % k], lat=2.9 + k)
+    for e in range(4):
+        dma("ys"[e // 2], T.X[e:128:16, :], T.x0[e:32:4, :], "dx", r=["X0"], w=["X%d" % (e + 1)])
+    dma("s", T.tgr[:], T.tg[:], "dtg", w=["tgr"])
+    dma("y", T.Fr[:, 0:2048], T.ft[:], "df", r=["C3"], w=["Fr"], lat=3.5)
+    op("g", lambda: g.affine_select(T.IW[:], T.ones[:, 0:136], [[-1, 136]], A.is_equal, 0.0, 8, 1), ["ones"], ["IW"], 0.45)
+    op("g", lambda: g.iota(T.pc[:, 0:1], [[0, 1]], 0, 1), [], ["pc"], 0.14)
+    op("g", lambda: g.iota(T.J[:], [[1, 16]], 0, 0, allow_small_or_imprecise_dtypes=True), [], ["J"], 0.17)
+    op("g", lambda: g.affine_select(T.BDt[:], T.ones[:, 0:128], [[-16, 8], [0, 16]], A.is_ge, 0.0, 0, 1), ["ones"], ["BDt"], 0.44)
+    op("g", lambda: g.affine_select(T.BD[:], T.BDt[:], [[16, 8], [0, 16]], A.is_ge, 0.0, 15, -1), ["BDt"], ["BD"], 0.44)
+    op("g", lambda: g.iota(T.trash[:], [[-2304, 2], [16, 16]], 4352, 0, allow_small_or_imprecise_dtypes=True), [], ["trash"], 0.2)
+    for k in range(4):
+        op("g", lambda k=k: g.iota(T.IOTA[:, 512 * k:512 * k + 512], [[1, 512]], 512 * k, 0), [], ["IOTA%d" % k], 1.2)
+    ms(T.VEC[:], 0.0, w=["VEC"])
+    ms(T.Z[:], 0.0, w=["Z"])
+    ms(T.comb[:], 0.0, w=["comb"])
+    ms(T.RST[:], 0.0625, w=["RST"])
+    ms(T.cb[:, 0:4, :], 0.0, w=["cbz"])
+    ms(T.two[:], 2.0, w=["two"])
+    for q in range(4):
+        ms(T.comb[32 * q:32 * q + 1, 4 * q + 3:128:16], 1.0, r=["comb"], w=["comb%d" % q])
+    ms(T.RST[:, 0:256:16], -1024.0, w=["RST"])
+    vk = []
+    for k, (q, rows, cols, n, v) in enumerate(patterns()):
+        out = T.VEC[32 * q:32 * q + 1, rows, cols]
+        vk.append("vec%d" % k)
+        if VECQ[k % len(VECQ)] == "v":
+            ms(out, v, r=["VEC"], w=[vk[-1]])
+        elif VECQ[k % len(VECQ)] == "g" and v == int(v):
+            op("g", lambda out=out, n=n, v=v: g.iota(out, [[0, n]], int(v), 0, allow_small_or_imprecise_dtypes=True), ["VEC"], [vk[-1]], 0.15)
+        else:
+            act(out, T.ones[32 * q:32 * q + 1, 0:n], r=["VEC", "ones"], w=[vk[-1]], scale=v)
+    mm(group(ps(5, 0, NP * 16), [(T.comb[:, 3 - k:131 - k], T.VEC[:, k, :]) for k in range(4)]),
+       vk + ["comb%d" % q for q in range(4)], pk(5, 0, NP * 16))
+    tag("c1")
+    b15 = T.BD[:, 15:128:16]
+    ts(T.pc[:, 1:2], T.pc[:, 0:1], 15, None, A.bitwise_and, r=["pc"], w=["pc1"])
+    cp(col(RC), T.pc[:, 1:2], ["pc1"], ["RC"])
+    ts(T.pc[:, 0:1], T.pc[:, 1:2], 7, None, A.bitwise_and, r=["pc1"], w=["pc"])
+    ts(T.RM[:], T.J[:], col(RC), None, A.is_equal, r=["J", "RC"], w=["RM"])
+    ts(col(LT8), col(RC), 8.0, None, A.is_lt, r=["RC"], w=["LT8"])
+    ts(col(INIT), col(RC), 8.0, -1.0, A.is_lt, A.mult, r=["RC"], w=["INIT"])
+    ts(col(Z1C), col(RC), -8.0, 192.0, A.add, A.mult, r=["RC"], w=["Z1C"])
+    ts(col(LT4), col(RC), 4.0, None, A.is_lt, r=["RC"], w=["LT4"])
+    ts(col(OC), T.pc[:, 0:1], B0, None, A.add, r=["pc"], w=["OC"])
+    ts(col(Z1C), col(Z1C), col(LT8), None, A.max, r=["LT8"], w=["Z1C"])
+    ts(T.lim[:], T.ones[:, 0:S], col(LT8), 254.0, A.mult, A.mult, r=["LT8", "ones"], w=["lim"], k=0.5)
+    ts(T.lim[:], T.lim[:], 1.0, None, A.add, w=["lim"], k=0.5)
+    cp(T.cb[:, 1, 15:128:16], b15, ["BD", "cbz"], ["Z2"])
+    tt(T.BDt[:], T.IW[:, 8:136], T.IW[:, 4:132], A.add, ["IW"], ["BDt"])
+    tt(T.BDt[:], T.BDt[:], T.IW[:, 0:128], A.add, ["IW"], ["BDt"])
+    ts(cb("xrep"), T.BDt[:], col(LT4), None, A.mult, r=["BDt", "LT4"], w=["xrep"], k=0.5)
+    ts(T.cb[:, 0, 15:128:16], b15, col(Z1C), None, A.mult, r=["BD", "Z1C", "cbz"], w=["Z1"])
+    cp(T.col[:, S1:S1 + 3], ps(5, 160, 163), pk(5, 160, 176), ["S1"])
+    cp(T.PAT[:], ps(5, 0, 160), pk(5, 0, 160), ["PAT"])
+    tt(col(S2), col(S2), col(S2 + 1), A.add, w=["S1"])
+    ms(T.MB[:, :, 128:144], 0.0, w=["MB8"])
+    ms(T.ch[:, 0, :], 0.0, w=["chz"])
+    ms(T.TB[:], 0.0, w=["TB"])
+    act(T.GM[:], T.BD[:, 0:128:16], r=["BD"], w=["GM"])
+    for k in range(8):
+        if k < MBS:
+            act(T.MB[:, :, 16 * k:16 * k + 16], T.PAT[:], r=["PAT", "GM"], w=["MB%d" % k], scale=T.GM[:, k:k + 1])
+        else:
+            ts(T.MB[:, :, 16 * k:16 * k + 16], T.PAT[:], T.GM[:, k:k + 1], None, A.mult, r=["PAT", "GM"], w=["MB%d" % k], k=0.5)
+    MBk = ["MB%d" % k for k in range(9)]
+    scan(T.pw[:], T.two[:], T.RM[:], 0.0, A.mult, A.add, ["two", "RM"], ["pw"])
+    ts(col(ZAC), RM(12), 8192.0, RM(8), A.mult, A.add, r=["RM"], w=["ZAC"])
+    ts(col(ZAC), RM(9), 2048.0, col(ZAC), A.mult, A.add, r=["RM"], w=["ZAC"])
+    ts(col(SUB), RM(8), RM(9), 2048.0, A.add, A.mult, r=["RM"], w=["SUB"])
+    ts(col(R1), col(RC), 1.0, None, A.add, r=["RC"], w=["R1"])
+    ts(T.trash[:], T.trash[:], col(RC), None, A.add, r=["RC"], w=["trash"])
+    ts(col(THR), T.pw[:, 15:16], 2.5, None, A.mult, r=["pw"], w=["THR"])
+    act(T.tgc[:], T.tgr[:], AF.Identity, ["tgr"], ["tgc"], bias=-128.0)
+    ts(T.ch[:, 0, 15:128:16], b15, col(ZAC), None, A.mult, r=["ZAC", "chz", "BD"], w=["ZA"])
+    for k in range(9):
+        ts(ch("b%d" % k), T.BD[:], RM(k), 1.0 / 256 if k < 4 else 1.0, A.mult, A.mult, r=["BD", "RM"], w=["b%d" % k], k=0.5)
+    cp(ch("Ih"), I, ["IW"], ["Ih"], k=0.5)
+    ts(T.cb[:, 2, 15:128:16], b15, RM(0), None, A.mult, r=["BD", "RM", "cbz"], w=["Z3"])
+    ts(T.cb[:, 3, 15:128:16], b15, RM(0), 128.0, A.mult, A.mult, r=["BD", "RM", "cbz"], w=["Zm"])
+    ts(cb("pen"), T.BD[:], RM(12), -131072.0, A.mult, A.mult, r=["BD", "RM"], w=["pen"], k=0.5)
+    for name, sc, key in (("orep", RM(3), "RM"), ("cnt", col(LT8), "LT8"), ("pow", T.pw[:, 15:16], "pw"), ("big", 65536.0, "BD"), ("ycw", col(R1), "R1")):
+        act(cb(name), T.BD[:], r=["BD", key], w=[name], scale=sc)
+    for name, sc in (("I64", 64.0), ("In", -1.0)):
+        act(cb(name), I, r=["IW"], w=[name], scale=sc)
+    SFk = ["SF%d" % o for o in range(N)]
+
+    def zero_sf():
+        for o in range(N):
+            act(T.SF[:, S * o:S * o + CAP], T.Z[:, 0:CAP], r=["Z"], w=[SFk[o]])
+    zero_sf()
+    RYz = ["RYz%d" % k for k in range(3)]
+    for k in range(3):
+        act(T.RY[:, 512 * k:512 * k + 512], T.Z[:, 0:512], r=["Z"], w=[RYz[k]])
+    Mz = ["Mz%d" % k for k in range(8)]
+    for k in range(8):
+        act(T.ST[:, S * k:S * k + CAP], T.Z[:, 0:CAP], r=["Z"], w=["STz%d" % k])
+        part = T.M[:, 256 + 512 * k:768 + 512 * k]
+        if k < MZG:
+            op("g", lambda part=part: g.iota(part, [[0, 512]], 0, 0, allow_small_or_imprecise_dtypes=True), [], [Mz[k]], 1.2)
+        else:
+            act(part, T.Z[:, 0:512], r=["Z"], w=[Mz[k]])
+    tag("fp")
+    Fk = ["Fp%d" % k for k in range(16)]
+    for m in range(16):
+        act(T.Fp[:, 128 * m:128 * m + 128], T.Fr[:, m:2048:16], AF.Identity, ["Fr"], [Fk[m]], bias=-128.0)
+
+    tag("am")
+    for k in range(8):
+        b = (6, 7, 5)[k % 3]
+        mm([(ps(b, 128 * ((j % 2) * 2 + j // 2), 128 * ((j % 2) * 2 + j // 2) + 128), T.C[:, 128 * (4 * k + j):128 * (4 * k + j) + 128], I, True, True)
+            for j in range(4)], ["C%d" % (k // 2), "IW"], pk(b))
+        for hf in range(2):
+            a = 2048 * hf + 256 * k
+            scan(T.SC[:, a:a + 256], T.RST[:], ps(b, 256 * hf, 256 * hf + 256), 0.0, A.add, A.max,
+                 ["RST"] + pk(b, 256 * hf, 256 * hf + 256), ["SC%d_%d" % (k, hf)])
+    tag("am2")
+    ts(T.E[:], T.SC[:, 15:4096:16], 16.0, None, A.mult, r=["SC%d_%d" % (k, hf) for k in range(8) for hf in range(2)], w=["E"])
+    ts(T.E[:], T.E[:], 15, None, A.bitwise_and, w=["E"])
+    for k in range(8):
+        ts(T.R2[:, :, 16 * k:16 * k + 16], T.E[:, k:256:8], -1.0, 15.0, A.mult, A.add, r=["E"], w=["R2%d" % k])
+    mm([(ps(6, 128 * hf, 128 * hf + 128), T.R2[:, hf, :], I, True, True) for hf in range(2)], ["R2%d" % k for k in range(8)] + ["IW"], pk(6, 0, 256))
+    cp(T.T2[:], ps(6, 0, 256), pk(6, 0, 256), ["T2"])
+    for r in range(4):
+        dma("ys"[r % 2], T.M[r:128:16, 256 - OFF[r]:256 - OFF[r] + 4096], T.T2[:], "dm0", r=["T2"] + Mz, w=["Mrow%d" % r], lat=2.8)
+    for r in range(1, 4):
+        dma("ys"[r % 2], T.M[r:128:16, 4352 - OFF[r]:4608 - OFF[r]], T.T2[0:128:16, :], "dm0", r=["T2"] + Mz, w=["Mwrap%d" % r], lat=2.8)
+
+    Xk = ["X%d" % e for e in range(5)]
+
+    def home_update(r):
+        tag("hu")
+        ry = ["RY", "RYr", "RYg", "slot"]
+        ts(T.st[:], T.RY[:].indirect(T.slot[:]), 8.0, -8.0, A.min, A.max, r=ry, w=["st"], k="g")
+        act(T.yg[:, r, :], T.RY[:].indirect(T.slot[:]), r=ry, w=["yg%d" % r], k="g")
+        tt(T.X[:], T.X[:], T.st[:], A.add, ["st"], Xk)
+        ts(T.X[:], T.X[:], 255, None, A.bitwise_and, w=Xk)
+
+    def home_route(r):
+        tag("hr")
+        ts(T.ob[:], T.X[:], 1.0 / 32, B0 - 0.484375, A.mult, A.add, r=Xk, w=["ob"])
+        mm([(ps(2, 0, S), cb("orep"), T.ob[:], True, True)], ["ob", "orep"], pk(2, 0, S))
+        cp(T.xb[:], T.X[:], Xk, ["xb"])
+        mm([(ps(3, 0, S), cb("xrep"), T.xb[:], True, True)], ["xb", "xrep"], pk(3, 0, S))
+        ts(T.h[:], ps(2, 0, S), col(OC), None, A.is_equal, r=pk(2, 0, S) + ["OC"], w=["h"])
+        act(T.Fh[:], ps(3, 0, S), AF.Identity, pk(3, 0, S) + ["S1"], ["Fh"], bias=col(S2), scale=col(S1))
+        scan(T.cum[:], T.h[:], T.lim[:], col(INIT), A.add, A.min, ["h", "lim", "INIT"], ["cum"], k=0.5)
+        tt(T.val[:], T.h[:], T.cum[:], A.mult, ["h", "cum"], ["val"])
+        mm(group(ps(4, 0, 12), [(cb("Z1", 15 - k), T.val[:, k:S:16]) for k in range(16)]), ["val", "Z1"], pk(4, 0, 12))
+        cp(T.slot[:], ps(4, 0, 12), pk(4, 0, 12), ["slot"])
+        cp(T.SF[:].indirect(T.slot[:]), T.Fh[:], ["slot", "Fh"], SFk, k="s")
+        RF, RT = T["RF%d" % r], T["RT%d" % r]
+        send("f", r, lambda o: T.SF[:, S * o:S * o + CAP], RF[:, CAP * me:CAP * me + CAP], SFk + RYz, ["RYg"], "RFr%d" % r)
+        act(RF[:, CAP * me:CAP * me + CAP], T.SF[:, S * me:S * me + CAP], r=SFk, w=["RF%d" % r])
+        mm([(ps(4, 256, 256 + S), cb("cnt"), T.val[:], True, True)], ["val", "cnt"], pk(4, 256, 256 + S))
+        act(T.sg[:, r, :], ps(4, 256, 256 + S), AF.Sign, pk(4, 256, 256 + S), ["sg%d" % r], bias=31.5, scale=-1.0)
+        tag("ht")
+        cp(T.ST[:].indirect(T.slot[:]), T.tgc[:], ["slot", "tgc"] + ["STz%d" % k for k in range(8)], ["ST"], k="s")
+        send("t", r, lambda o: T.ST[:, S * o:S * o + CAP], RT[:, CAP * me:CAP * me + CAP], ["ST"] + ["Mrow%d" % k for k in range(4)], [], "RTr%d" % r)
+        act(RT[:, CAP * me:CAP * me + CAP], T.ST[:, S * me:S * me + CAP], r=["ST"], w=["RT%d" % r])
+        if r < RO - 1:
+            zero_sf()
+
+    Mk = ["M"] + ["Mrow%d" % k for k in range(4)] + ["Mwrap%d" % k for k in range(1, 4)]
+    Ck = ["C%d" % k for k in range(4)]
+    Nk = ["Fn%d" % k for k in range(16)]
+
+    def owner_values(r):
+        tag("hash")
+        RF = T["RF%d" % r]
+        rf = ["RF%d" % r, "RFr%d" % r] + MBk
+        for k0, b in ((0, 4), (3, 5)):
+            for j in (1, 0, 2):
+                mm(group(ps(b, 64 * j, 64 * j + 64), [(T.MB[:, k0 + j, 3 - q:131 - q], RF[:, q:256:4]) for q in range(4)]), rf, pk(b, 64 * j, 64 * j + 64))
+        mm([(ps(6, 256, 512), T.MB[:, 7, 0:128], RF[:], True, True)], rf, pk(6, 256, 512))
+        mm([(ps(6, 0, 256), T.MB[:, 6, 0:128], RF[:], True, True)], rf, pk(6, 0, 256))
+        mm([(ps(7, 0, 256), T.MB[:, 8, 0:128], RF[:], True, True)], rf, pk(7, 0, 256))
+        cp(T.hv[:], ps(4, 64, 128), pk(4, 64, 128), ["hv"])
+        tt(T.hp[:], ps(4, 0, 64), T.hv[:], A.mult, ["hv"] + pk(4, 0, 64), ["hp"])
+        tt(T.hi[:], ps(4, 128, 192), T.hp[:], A.add, ["hp"] + pk(4, 128, 192), ["hi"])
+        ts(T.hi[:], T.hi[:], 2, 4095, A.arith_shift_right, A.bitwise_and, w=["hi"])
+        cp(T.ML[:], T.hi[:], ["hi"], ["ML"])
+        act(T.Mo[:, 16 * MGV:1024], T.M[:, 256:4352].indirect(T.ML[:, MGV:64]), r=Mk + ["ML"], w=["Mo"], k="g")
+        if MGV:
+            cp(T.Mo[:, 0:16 * MGV], T.M[:, 256:4352].indirect(T.ML[:, 0:MGV]), Mk + ["ML"], ["Mo2"], k="g")
+        tag("hashb")
+        act(T.bv[:], ps(5, 64, 128), r=pk(5, 64, 128), w=["bv"])
+        tt(T.bp[:], ps(5, 0, 64), T.bv[:], A.mult, ["bv"] + pk(5, 0, 64), ["bp"])
+        tt(T.bi[:], ps(5, 128, 192), T.bp[:], A.add, ["bp"] + pk(5, 128, 192), ["bi"])
+        ts(T.bi[:], T.bi[:], 2, 127, A.arith_shift_right, A.bitwise_and, w=["bi"])
+        cp(T.BB[:, 0:64], T.bi[:], ["bi"], ["BB0"])
+        for ab in range(1, 4):
+            ts(T.BB[:, 64 * ab:64 * ab + 64], T.bi[:], 128.0 - BOFF[ab], -128.0, A.is_ge, A.mult, r=["bi"], w=["BB%d" % ab])
+        tag("hashw")
+        act(T.fv[:], ps(6, 256, 512), r=pk(6, 256, 512), w=["fv"])
+        tt(T.fv[:], ps(6, 0, 256), T.fv[:], A.mult, pk(6, 0, 256), ["fv"])
+        tt(T.fi[:], ps(7, 0, 256), T.fv[:], A.add, pk(7, 0, 256) + ["fv"], ["fi"])
+        ts(T.fi[:], T.fi[:], 2, 4095, A.arith_shift_right, A.bitwise_and, w=["fi"])
+        ts(T.Q[:], T.fi[:], col(SUB), None, A.subtract, r=["fi", "SUB"], w=["Q"])
+        for ab in range(4):
+            tag("fc")
+            b, lo = 4 + ab % 2, 256 + 64 * (ab // 2)
+            pairs = [(I, T.BB[:, 0:64])] + ([(I, T.BB[:, 64 * ab:64 * ab + 64])] if ab else [])
+            pairs += [(T.MB[:, 9, 3 - q:131 - q], T.Mo[:, 4 * ab + q:1024:16]) for q in range(4)]
+            mm(group(ps(b, lo, lo + 64), pairs), ["BB0", "BB%d" % ab, "Mo", "Mo2", "IW"] + MBk, pk(b, lo, lo + 64))
+            ts(T.FL[:, 64 * ab:64 * ab + 64], ps(b, lo, lo + 64), float(BOFF[ab]), None, A.add, r=pk(b, lo, lo + 64), w=["FL%d" % ab])
+            tag("fg")
+            for lo_, n in ([(0, 64)] if ab < 3 else [(0, 32), (32, 32)]):
+                a = 64 * ab + lo_
+                act(T.VG[:, 16 * a:16 * (a + n)], T.Fp[:, 0:2048].indirect(T.FL[:, a:a + n]), r=Fk + ["FL%d" % ab], w=["VG%d" % a], k="g")
+        tag("W")
+        for hf in range(2):
+            mm([(P01[:, 32 * hf:32 * hf + 32, cd, :], ch("b%d" % (4 + cd)), T.Q[:, 128 * hf:128 * hf + 128], True, True) for cd in range(4)],
+               ["Q", "b4", "b5", "b6", "b7"], pk(hf))
+        for k in range(2):
+            mm([(ps(2 + k, 256 * j, 256 * j + 256), ch("b%d" % (2 * k + j)), T.Q[:], True, True) for j in range(2)],
+               ["Q", "b0", "b1", "b2", "b3"], pk(2 + k))
+            if EVAC[k] == "v":
+                cp(T.Wab[:, 512 * k:512 * k + 512], ps(2 + k), pk(2 + k), ["Wab%d" % k])
+            else:
+                act(T.Wab[:, 512 * k:512 * k + 512], ps(2 + k), r=pk(2 + k), w=["Wab%d" % k])
+        tag("diag")
+        mm(group(ps(7, 256, 272), [(ch("ZA", 15 - k), T.Q[:, k:256:16]) for k in range(16)]), ["Q", "ZA"], pk(7, 256, 272))
+        mm([(ps(6, 0, 256), ch("b8"), T.Q[:], True, True)], ["Q", "b8"], pk(6, 0, 256))
+        tag("keys")
+        ts(T.AI[:, 0:16], ps(7, 256, 272), 4196352.0, None, A.add, r=pk(7, 256, 272), w=["AI"])
+        ts(T.BI[:], T.AI[:, 0:16], 16, None, A.arith_shift_right, r=["AI"], w=["BI"])
+        ts(T.AI[:, 16:32], T.AI[:, 0:16], 16383, None, A.bitwise_and, r=["AI"], w=["AL"])
+        ts(T.KY[:, 0:16], T.AI[:, 16:32], -8192.0, 0.0, A.add, A.max, r=["AL"], w=["KYc"])
+        ts(T.KL[:, 0:16], T.AI[:, 16:32], -8192.0, 0.0, A.add, A.max, r=["AL"], w=["KLc"])
+        if EQV:
+            ts(T.KS[:, 0:16], T.AI[:, 16:32], -10240.0, None, A.add, r=["AL"], w=["KSc"])
+            cp(T.KR[:, 0:256], ps(6, 0, 256), pk(6, 0, 256), ["KR0"])
+        if EQV < 8:
+            ts(T.KN[:], T.AI[:, 16:32], -1.0, 10240.0, A.mult, A.add, r=["AL"], w=["KSn"])
+        ts(T.dd[:], T.AI[:, 16:32], 8192.0, -8192.0, A.is_lt, A.mult, r=["AL"], w=["dd"])
+        cp(T.BL[:], T.BI[:], ["BI"], ["BL"])
+        act(T.Ms[:], T.M[:, 256:4352].indirect(T.KL[:, 0:16]), r=Mk + ["KLc"], w=["Ms"], k="g")
+        for ab in range(4):
+            tag("mul")
+            VW = T["VW%d" % ab]
+            b, c0 = 2 + ab % 2, 256 * (ab // 2)
+            reg, ks = ps(b, c0, c0 + 256), pk(b, c0, c0 + 256)
+            for lo, n in ([(0, 64)] if ab < 3 else [(0, 32), (32, 32)]):
+                wk = ["VW%d_%d" % (ab, k) for k in range(lo // 32, (lo + n) // 32)]
+                tt(VW[:, lo:lo + n], T.VG[:, 1024 * ab + 16 * lo:1024 * ab + 16 * (lo + n)], P01[:, lo:lo + n], A.mult,
+                   ["VG%d" % (64 * ab + lo)] + [k_ for k in range(lo // 32, (lo + n) // 32) for k_ in pk(k)], wk)
+                mm(group(ps(b, c0 + 4 * lo, c0 + 4 * (lo + n)), [(ch("Ih"), VW[:, lo:lo + n, cd, :]) for cd in range(4)]),
+                   wk + ["Ih"], pk(b, c0 + 4 * lo, c0 + 4 * (lo + n)))
+            tag("sum")
+            w_, sk = T.Wab[:, 256 * ab:256 * ab + 256], ["Wab%d" % (ab // 2)]
+            if ab == 0:
+                tt(T.acc[:], reg, w_, A.mult, ks + sk, ["acc"])
+            else:
+                tt(reg, reg, w_, A.mult, sk, ks)
+                tt(T.acc[:], reg, T.acc[:], A.add, ks, ["acc"])
+        yb = T["yb%d" % r]
+        ts(T.y16[:], T.acc[:], 1152.0 - 255.0 / 512, None, A.add, r=["acc"], w=["y16"])
+        ts(yb[:], T.y16[:], -1152.0, None, A.add, r=["y16"], w=["yb%d" % r], k=0.5)
+        send("y", r, lambda o: yb[:, CAP * o:CAP * o + CAP], T.RY[:, S * me:S * me + CAP], ["yb%d" % r], [], "RYr")
+        act(T.RY[:, S * me:S * me + CAP], yb[:, CAP * me:CAP * me + CAP], r=["yb%d" % r] + RYz, w=["RY"])
+
+    def losers(r, k):
+        tag("eq%d" % k)
+        EQ = T["EQ%d" % k]
+        end = lambda c: 128 * (c // 8 + 1)
+        for c in range(16):
+            if k == 0 and c % 8 >= EQV:
+                eq = EQ[:, c, 0:end(c) - 16 * c]
+                act(eq, ps(6, 16 * c, end(c)), AF.Abs, pk(6, 16 * c, end(c)) + ["KSn"], ["EQ0_%d" % c], bias=T.KN[:, c:c + 1])
+                act(eq, eq, AF.Relu, [], ["EQ0_%d" % c], bias=1.0, scale=-1.0)
+                continue
+            ts(EQ[:, c, 0:end(c) - 16 * c], T.KR[:, 256 * k + 16 * c:256 * k + end(c)], T.KS[:, 16 * k + c:16 * k + c + 1], None, A.is_equal,
+               r=["KR%d" % k, "KS" + "cf"[k]], w=["EQ%d_%d" % (k, c)], k=0.5)
+        tag("cnt%d" % k)
+        b, o = (6, 256) if k == 0 else (5, 0)
+        items = [(ps(b, o, o + 256), cb("pen"), T["RF%d" % r][:], True, False)]
+        items += [(ps(b, o + 16 * (c + 1), o + end(c)), cb("big"), EQ[:, c, 16:end(c) - 16 * c], False, False) for c in range(16) if c % 8 < 7]
+        items += [(ps(b, o, o + 256), cb("pow"), EQ[:, :, 0:16], False, True)]
+        mm(items, ["EQ%d_%d" % (k, c) for c in range(16)] + ["pen", "big", "pow", "RF%d" % r, "RFr%d" % r], pk(b, o, o + 256))
+        act(T.LS[:, 256 * k:256 * k + 256], ps(b, o, o + 256), AF.Identity, pk(b, o, o + 256), ["LS%d" % k], bias=131072.0)
+
+    def put(win, k, src, r, w):
+        for hf in (1, 0):
+            cp(win.indirect(T.OL[:, 16 * k + 8 * hf:16 * k + 8 * hf + 8]), src[:, 128 * hf:128 * hf + 128], r + ["OL"], w, k="s")
+
+    def train(r):
+        last = r == RO - 1
+        tag("g")
+        yb, RT = T["yb%d" % r], T["RT%d" % r]
+        mm(group(ps(7, 288, 304), [(cb("Z3" if last else "Zm", 15 - k), T.Ms[:, k:256:16]) for k in range(16)]), ["Ms", "Zm", "Z3"], pk(7, 288, 304))
+        mm(group(ps(2, 256, 512), [(I, RT[:]), (cb("In"), yb[:])]), ["yb%d" % r, "RT%d" % r, "RTr%d" % r, "In", "IW"], pk(2, 256, 512))
+        for k in range(2):
+            act(ps(0, 256 * k, 256 * k + 256), ps(2, 256, 512), AF.Sign, pk(2, 256, 512), pk(0, 256 * k, 256 * k + 256))
+        tag("ug")
+        for j in range(16):
+            act(T.UG[:, 256 * j:256 * j + 256], T.Fp[:, 128 * j:128 * j + 128].indirect(T.BL[:]), AF.Identity, Fk + ["BL"], ["UG%d" % j], k="g", bias=128.0)
+        tag("fk")
+        if last:
+            ts(T.BI[:], T.BI[:], 16.0, None, A.mult, w=["BI"])
+        tt(T.KY[:, 16:32], ps(7, 288, 304), T.BI[:], A.add, pk(7, 288, 304) + ["BI"], ["KYf"])
+        cp(T.KL[:, 16:32], T.KY[:, 16:32], ["KYf"], ["KLf"])
+        tt(T.KS[:, 16:32], T.KY[:, 16:32], T.dd[:], A.add, ["KYf", "dd"], ["KSf"])
+        cp(T.KR[:, 256:512], T.IOTA[:].indirect(T.KL[:, 16:32]), ["KLf"] + ["IOTA%d" % k for k in range(4)], ["KR1"], k="g")
+        act(T.Co[:], T.C[:, 0:4096].indirect(T.KL[:, 0:16]), r=Ck + ["KLc"], w=["Co"], k="g")
+        act(T.Fo[:], (T.Fr if last else T.Fp)[:, 0:2048].indirect(T.KL[:, 16:32]), r=(Nk if last else Fk) + ["KLf"], w=["Fo"], k="g")
+        losers(r, 0)
+        losers(r, 1)
+        tag("win")
+        mm(group(ps(7, 304, 336), [(cb("Z3", 15 - k), T.LS[:, k:512:16]) for k in range(16)]), ["LS0", "LS1", "Z3"], pk(7, 304, 336))
+        ts(T.bad[:], ps(7, 304, 336), col(THR), 65536.0, A.is_gt, A.mult, r=pk(7, 304, 336) + ["THR"], w=["bad"])
+        tt(T.bad[:], T.bad[:], T.trash[:], A.min, ["trash"], ["bad"])
+        tt(T.bad[:], T.bad[:], T.KY[:], A.max, ["KYc", "KYf"], ["bad"])
+        cp(T.OL[:], T.bad[:], ["bad"], ["OL"])
+        tag("prod")
+        for j in range(8):
+            tt(T.PR[:, 512 * j:512 * j + 512], T.UG[:, 512 * j:512 * j + 512], ps(0), A.mult,
+               ["UG%d" % (2 * j), "UG%d" % (2 * j + 1)] + pk(0), ["PR%d" % j])
+            mm([(ps(1, 0, 256), cb("Z2", 15 - jj), T.PR[:, 256 * jj:256 * jj + 256], jj == 0, jj == 15) for jj in (2 * j, 2 * j + 1)],
+               ["PR%d" % j, "Z2"], pk(1) if j == 0 else (["usum"] if j == 7 else []), ["#1grp"])
+        tag("wf")
+        tt(T.Fn[:], ps(0, 0, 256), T.Fo[:], A.add, pk(0, 0, 256) + ["Fo"], ["Fn"])
+        ts(T.Fn[:], T.Fn[:], 255.0 if last else 127.0, 0.0 if last else -128.0, A.min, A.max, w=["Fn"], k=0.5)
+        put(T.Fr[:] if last else T.Fp[:], 1, T.Fn, ["Fn"], Nk if last else Fk)
+        tag("nc")
+        act(ps(1, 256, 512), ps(1, 0, 256), AF.Sign, pk(1, 0, 256) + ["usum"], pk(1, 256, 512))
+        tt(T.Cn[:], ps(1, 256, 512), T.Co[:], A.add, pk(1, 256, 512) + ["Co"], ["Cn"])
+        if last:
+            return
+        tag("wm")
+        op("v", lambda: V.transpose(T.TR[:], T.Cn[:]), ["Cn"], ["TR"], cost(256, 0.5))
+        scan(T.sn[:], T.RST[:], T.TR[:], 0.0, A.add, A.max, ["TR", "RST"], ["sn"])
+        ts(T.e16[:], T.sn[:, 15:256:16], 16.0, None, A.mult, r=["sn"], w=["e16"])
+        ts(T.e16[:], T.e16[:], 15, None, A.bitwise_and, w=["e16"])
+        ts(T.TB[:, 0:256:16], T.e16[:], -1.0, 15.0, A.mult, A.add, r=["e16"], w=["TB"])
+        op("v", lambda: V.transpose(T.Mn[:], T.TB[:]), ["TB"], ["Mn"], cost(256, 0.5))
+        put(T.M[:, 256:4864], 0, T.Mn, ["Mn"], Mk)
+        act(T.M[:, 4352:4608], T.M[:, 256:512], w=["M"])
+        for k in range(1, 4):
+            dma("y", T.M[k:128:16, 256:4352], T.M[0:128:16, 256 + OFF[k]:4352 + OFF[k]], "dm%d" % (r + 1), r=["M"], w=["Mrow%d" % k], lat=2.6)
+        tag("wc")
+        put(T.C[:], 0, T.Cn, ["Cn"], Ck)
+
+    YCk = ["YC%d" % k for k in range(8)]
+    home_route(0)
+    for r in range(RO):
+        now[0] = r
+        owner_values(r)
+        train(r)
+        home_update(r)
+        if r < RO - 1:
+            home_route(r + 1)
+        if r == RO - 2:
+            tag("fn")
+            for m in range(16):
+                act(T.Fr[:, m:2048:16], T.Fp[:, 128 * m:128 * m + 128], AF.Identity, Fk, [Nk[m]], bias=128.0)
+            tag("yc")
+            for k in range(8):
+                b = 2 + k % 2
+                mm([(ps(b), cb("ycw"), T.C[:, 512 * k:512 * k + 512], True, True)], Ck + ["ycw"], pk(b))
+                act(T.YC[:, 512 * k:512 * k + 512], ps(b), r=pk(b), w=[YCk[k]])
+    tag("end")
+    mm([(ps(6, 0, 256), cb("ycw"), T.Cn[:], True, True)], ["Cn", "ycw"], pk(6, 0, 256))
+    act(T.ycn[:], ps(6, 0, 256), r=pk(6, 0, 256), w=["ycn"])
+    put(T.YC[:], 0, T.ycn, ["ycn"], YCk)
+    dma("y", T.yc[:], T.YC[0:128:16, 0:4096], "out", r=YCk, lat=2.6)
+    dma("y", T.yf[:], T.Fr[:, 0:2048], "out", r=Nk, lat=4.0)
+    cp(T.xO[:], T.X[:], Xk, ["xO"])
+    mm(group(ps(3, 0, S), [(cb("I64"), T.sg[:, k, :]) for k in range(RO)] + [(I, T.yg[:, k, :]) for k in range(RO)]),
+       ["sg%d" % k for k in range(RO)] + ["yg%d" % k for k in range(RO)] + ["I64", "IW"], pk(3, 0, S))
+    act(T.ysO[:], ps(3, 0, S), AF.Identity, pk(3, 0, S), ["ysO"], bias=192.0)
+    for e in range(4):
+        dma("ys"[e % 2], T.yx[e:32:4, :], T.xO[e:128:16, :], "out", r=["xO"])
+    dma("s", T.ys[:], T.ysO[:], "out", r=["ysO"])
+    if not ORDER:
+        rng = np.random.default_rng(1)
+        names = sorted({e["tag"] + e["q"] for e in ops})
+        best, bias = schedule({}), {}
+        for _ in range(TRIES):
+            other = dict(bias)
+            for k in rng.integers(0, len(names), int(rng.integers(1, 4))):
+                other[names[k]] = other.get(names[k], 0.0) + 3.0 * float(rng.standard_normal())
+            got = schedule(other)
+            if got[0] <= best[0]:
+                best, bias = got, other
+        ORDER.extend(best)
+    for i in ORDER[1]:
+        emit(ops[i])
+    for sem, val in total.items():
+        need("y", (sem, val))

@@ -7,93 +7,115 @@ N, S, CAP, RO = 8, 192, 32, 3
 B0 = 160.0
 OFF = (0, 61, 173, 234)
 BOFF = (0, 89, 91, 52)
-NP = 11
+NP = 12
 TAG = [""]
-CY, GA, SCA, WAKE, SENT, LAND, SLACK = 1.04e-3, 1.6, 3.8, 0.09, 3.1, 0.9, 0.15
-SPLIT = (4, 2)
-EVAC, MZG, MGV, EQV, MBS, VECQ = "sv", 6, 24, 8, 4, "gss"
-TRIES, ORDER = 1200, []
+CY, GA, SCA, FIX, WAKE, SENT, ROW, LAND, TF, FIRST = 0.9e-3, 1.56, 3.8, 0.02, 0.1, 1.0, 0.022, 0.6, 1.1, 2.0
+SPLIT = 4
+YP = [(0, 1, 2, 3), (4, 5), (6, 7)]
+EVAC, MZG, MGQ, EQV, MBS, VECQ, VECH = "ssss", 2, "vssss", 8, 4, "gss", "sv"
+LCH = [(0, 64), (64, 64), (128, 64), (192, 32), (224, 32)]
+BCH = [(0, 64), (64, 192)]
+FGV, UGV, CLF = (0, 0, 0, 0, 0), 0, 1
+UGS = [(0, 2), (2, 2), (4, 4), (8, 4), (12, 2), (14, 2)]
+PRO = list(range(16))
+TRIES, ORDER = 4000, []
+SW = 1824
 bf, f32, i32, u16, f16 = "bfloat16", "float32", "int32", "uint16", "float16"
-CB = ["Z1", "Z2", "Z3", "Zm", "orep", "xrep", "pow", "big", "pen", "cnt", "ycw", "I64", "In"]
-CH = ["ZA", "b0", "b1", "b2", "b3", "b4", "b5", "b6", "b7", "b8", "Ih"]
+CB = ["Z2", "Z3", "Zy", "dC", "dF", "dN", "xC", "xF", "xN", "pow", "big", "pen", "ycw", "I64", "In", "I2",
+      "r1", "r2", "rs", "w0", "w1", "w2", "w3"]
+CH = ["ZA", "Z1", "Zh", "b0", "b1", "b2", "b3", "cnt"]
 SB = {
-    "C": ([128, 4608], bf), "Fr": ([128, 2304], bf), "Fp": ([128, 2304], bf), "M": ([128, 4864], bf), "YC": ([128, 4608], f32),
-    "X": ([128, S], i32), "tgr": ([128, S], bf), "tgc": ([128, S], bf), "st": ([128, S], i32), "ob": ([128, S], bf), "xb": ([128, S], bf),
-    "h": ([128, S], bf), "cum": ([128, S], bf), "val": ([128, S], bf), "Fh": ([128, S], bf), "lim": ([128, S], bf),
+    "C": ([128, 4608], bf), "F": ([128, 2304], bf), "M": ([128, 4864], bf), "YC": ([128, 4608], f32), "YK": ([128, 256], f32),
+    "X": ([128, S], i32), "tgr": ([128, S], bf), "tgc": ([128, S], bf), "cl": ([128, S], bf), "ob": ([128, S], bf), "wr": ([128, S], bf),
+    "h": ([128, S], f16), "cum": ([128, S], f16), "val": ([128, S], f16), "Fh": ([128, S], bf), "lim": ([128, S], f16), "PI": ([128, S], f32),
     "yg": ([128, RO, S], bf), "sg": ([128, RO, S], bf), "ysO": ([128, S], f32), "xO": ([128, S], f32),
-    "SF": ([128, N * S], bf), "ST": ([128, N * S], bf), "RY": ([128, N * S], bf), "slot": ([128, 12], u16),
+    "SF0": ([128, SW], bf), "SF1": ([128, SW], bf), "SF2": ([128, SW], bf),
+    "ST": ([128, SW], bf), "RY": ([128, SW], bf), "slot": ([128, 12], u16), "GS": ([128, 256], bf), "n256": ([128, 128], bf),
     "RF0": ([128, 256], bf), "RF1": ([128, 256], bf), "RF2": ([128, 256], bf),
     "RT0": ([128, 256], bf), "RT1": ([128, 256], bf), "RT2": ([128, 256], bf),
     "yb0": ([128, 256], bf), "yb1": ([128, 256], bf), "yb2": ([128, 256], bf),
-    "ones": ([128, 256], bf), "Z": ([128, 512], bf), "IW": ([128, 136], bf), "BD": ([128, 128], bf), "BDt": ([128, 128], bf),
-    "cb": ([128, len(CB), 144], bf), "ch": ([128, len(CH), 144], f16), "MB": ([128, NP - 1, 144], bf),
-    "VEC": ([128, 4, NP * 16], bf), "comb": ([128, 144], bf), "PAT": ([128, NP - 1, 16], bf),
-    "pc": ([128, 2], i32), "col": ([128, 16], f32), "J": ([128, 16], f32), "RM": ([128, 16], f32), "two": ([128, 16], f32), "pw": ([128, 16], f32),
-    "RST": ([128, 256], bf), "trash": ([128, 32], f32), "IOTA": ([128, 2048], i32),
+    "ones": ([128, 256], bf), "Z": ([128, 512], bf), "IW": ([128, 144], bf), "BDu": ([128, 128], bf), "BD": ([128, 128], bf), "BDt": ([128, 128], bf),
+    "cb": ([128, len(CB), 144], bf), "ch": ([128, len(CH), 144], f16), "MB": ([128, NP, 144], bf),
+    "VEC": ([128, 4, NP * 16], bf), "comb": ([128, 144], bf), "PAT": ([128, NP, 16], bf),
+    "pc": ([128, 4], i32), "col": ([128, 32], f32), "R4": ([128, 4], f32), "J": ([128, 16], f32), "RM": ([128, 16], f32), "two": ([128, 16], f32), "pw": ([128, 16], f32),
+    "RST": ([128, 256], bf), "trash": ([128, 32], f32), "IOTA": ([128, 2048], f32),
     "SC": ([128, 4096], f32), "E": ([128, 256], i32), "R2": ([128, 2, 128], bf), "T2": ([128, 256], bf),
     "hv": ([128, 64], f32), "hp": ([128, 64], f32), "hi": ([128, 64], i32), "ML": ([128, 64], u16),
-    "bv": ([128, 64], f32), "bp": ([128, 64], f32), "bi": ([128, 64], i32), "BB": ([128, 256], bf),
-    "fv": ([128, 256], f32), "fi": ([128, 256], i32), "Q": ([128, 256], f16),
+    "bv": ([128, 256], f32), "bi": ([128, 256], i32), "BB": ([128, 256], bf), "Lv": ([128, S], bf), "Lh": ([128, S], bf),
+    "fv": ([128, 64], f32), "fi": ([128, 64], i32), "Q": ([128, 64], f16),
     "Mo": ([128, 1024], bf), "FL": ([128, 256], u16), "VG": ([128, 4096], bf),
-    "VW0": ([128, 64, 4, 4], f16), "VW1": ([128, 64, 4, 4], f16), "VW2": ([128, 64, 4, 4], f16), "VW3": ([128, 64, 4, 4], f16), "Wab": ([128, 1024], bf), "acc": ([128, 256], f32),
-    "KS": ([128, 32], f32), "KY": ([128, 32], f32), "KL": ([128, 32], u16), "BI": ([128, 16], i32), "AI": ([128, 32], i32), "y16": ([128, 256], f16), "BL": ([128, 16], u16), "dd": ([128, 16], f32), "KN": ([128, 16], f32), "GM": ([128, 8], f32),
+    "VL": ([128, 4096], f16), "D0": ([128, 1024], bf), "PD": ([128, 1280], f32), "R5": ([128, 1280], bf), "Y5": ([128, 1280], f16),
+    "KS": ([128, 32], f32), "KY": ([128, 32], f32), "KL": ([128, 32], u16), "BI": ([128, 16], i32), "AI": ([128, 32], i32), "y16": ([128, 256], f16), "UL": ([128, 256], u16), "dd": ([128, 16], f32), "KN": ([128, 16], f32), "GM": ([128, 8], f32),
     "KR": ([128, 512], f16), "EQ0": ([128, 16, 128], bf), "EQ1": ([128, 16, 128], bf), "LS": ([128, 512], bf),
     "bad": ([128, 32], f32), "OL": ([128, 32], u16),
     "Ms": ([128, 256], bf), "Co": ([128, 256], bf), "Fo": ([128, 256], bf), "Cn": ([128, 256], bf), "Fn": ([128, 256], bf),
-    "UG": ([128, 4096], bf), "PR": ([128, 4096], bf), "TR": ([128, 256], bf), "TB": ([128, 256], bf), "Mn": ([128, 256], bf),
+    "UG": ([128, 4096], f16), "PR": ([128, 4096], f16), "TR": ([128, 256], bf), "TB": ([128, 256], bf), "Mn": ([128, 256], bf),
     "sn": ([128, 256], f32), "e16": ([128, 16], i32), "ycn": ([128, 256], f32),
 }
 SCRATCH = {k: ("sbuf", v[0], v[1]) for k, v in SB.items()}
-SCRATCH["P01"] = ("psum", [128, 64, 4, 4], f32)
-for _k in range(2, 8):
+for _k in range(8):
     SCRATCH["P%d" % _k] = ("psum", [128, 512], f32)
-SEMAPHORES = (["cv", "ct", "cs", "cg", "dx", "dc0", "dc1", "dc2", "dc3", "df", "dtg", "dm0", "dm1", "dm2", "out"]
-              + [p + str(r) for p in ("af", "at", "ay", "lf", "lt", "ly") for r in range(RO)])
+SEMAPHORES = (["cv", "ct", "cs", "cg", "dx", "dc0", "dc1", "dc2", "dc3", "df", "dtg", "dm0", "dm1", "dm2", "dyc", "out"]
+              + [p + str(r) for p in ("af", "at", "ay", "lf", "lt") for r in range(RO)]
+              + ["ly%d_%d" % (r, k) for r in range(RO) for k in range(4)])
 
 
-def plan(topo, cores, src):
+def plan(topo, cores, src, parts=None):
     k = cores.index(src)
     turn = cores[k + 1:] + cores[:k]
     far = [d for d in turn if topo.chip(d) != topo.chip(src)]
     near = [d for d in turn if topo.chip(d) == topo.chip(src)]
     pool = list(topo.engines(src, far[0]))
+    if parts is None:
+        sets = [far[:SPLIT] + near, far[SPLIT:]]
+    else:
+        sets = [[d for d in turn if cores.index(d) in part] for part in parts]
     calls = []
-    for n in SPLIT:
-        part, far = far[:n], far[n:]
-        w = len(pool) // n
-        calls.append({d: pool[w * j:w * j + w] for j, d in enumerate(part)})
-    calls[0][near[0]] = [e for e in topo.engines(src, near[0]) if e not in pool]
+    for ds in sets:
+        out = [d for d in ds if d in far]
+        w = len(pool)
+        while w * len(out) > len(pool):
+            w //= 2
+        calls.append({d: pool[w * j:w * j + w] for j, d in enumerate(out)})
+        for d in ds:
+            if d in near:
+                calls[-1][d] = [e for e in topo.engines(src, d) if e not in pool]
     return calls
 
 
 def patterns():
     p = {}
 
-    def put(k, row, c, v):
-        p[(row, 16 * k + c)] = float(v)
+    def put(k, c, rows, one=0.0, by=1.0):
+        for row, v in rows.items():
+            p[(row, 16 * k + c)] = p.get((row, 16 * k + c), 0.0) + by * v
+        for row in range(12, 16) if one else ():
+            p[(row, 16 * k + c)] = p.get((row, 16 * k + c), 0.0) + one / 16
+    pa = ({0: 1}, {0: 1, 2: 1}, {1: 1, 2: -1}, {1: 1})
+    pb = ({4: 1}, {5: 1}, {4: 1, 6: 1, 5: -1}, {6: 1})
     for x in range(4):
-        c, lo, hi = 4 * x + 3, x & 1, x >> 1
-        for k, ru, rv in ((0, 0, 1), (3, 2, 3)):
-            put(k, ru, c, 1); put(k, 12, c, lo - B0)
-            put(k + 1, rv, c, 2); put(k + 1, 12, c, -2 * B0); put(k + 1, 13, c, 2 * hi + 1)
-        put(2, 2, c, 244); put(2, 3, c, 692); put(2, 12, c, 14080)
-        put(5, 0, c, 356); put(5, 1, c, 364)
-        put(9, x, c, 128)
-        for base, eu, ev in ((0, 0, 1), (4, 2, 3)):
-            su, sv = (1 if lo else -1), (1 if hi else -1)
-            put(6, 4 + eu, base + x, 4 * su); put(6, eu, base + x, -16 * su); put(6, 12, base + x, 16 * B0 * su + (0 if lo else 16))
-            put(7, 4 + ev, base + x, sv); put(7, ev, base + x, -4 * sv); put(7, 12, base + x, 4 * B0 * sv + (0 if hi else 4))
-    for role, ru, rv in ((8, 8, 9), (9, 10, 11)):
-        up = 1 if role == 8 else 32
-        put(6, ru, role, up); put(6, 12, role, -B0 * up)
-        put(7, rv, role, 2); put(7, 12, role, -2 * B0); put(7, 13, role, 1)
-    put(6, 12, 12, 4); put(7, 12, 12, 1)
-    put(8, 10, 8, 244); put(8, 11, 8, 692); put(8, 12, 8, 14080); put(8, 8, 9, 356 * 32); put(8, 9, 9, 364 * 32)
+        put(0, 12 + x, pa[x]); put(1, 12 + x, pb[x], 1, 2); put(2, 12 + x, {8: 244, 9: 692})
+        put(9, 12 + x, {x: 1})
+        for cd in range(4):
+            put(3, 4 * x + cd, {8: 1}, cd & 1); put(4, 4 * x + cd, {9: 2}, 2 * (cd >> 1) + 1)
+            put(5, 4 * x + cd, pa[x], 0, 356); put(5, 4 * x + cd, pb[x], 0, 364)
+    put(6, 12, {0: 1}); put(7, 12, {4: 2}, 1); put(8, 12, {10: 244, 11: 692})
+    put(6, 13, {10: 32}); put(7, 13, {11: 2}, 1); put(8, 13, {0: 356 * 32, 4: 364 * 32})
+    put(8, 14, {}, 4)
+    odd = lambda e: {4 * e + 3: 1, 4 * e + 2: -1, 4 * e + 1: 1, 4 * e: -1}
+    for c, rows in ((0, {1: 1}), (1, {0: 1, 3: 1, 1: -1}), (4, {5: 1}), (5, {6: 1}), (6, {4: 1, 7: 1, 5: -1}),
+                    (8, {8: 1}), (9, {12: 1}), (10, {9: 1}), (11, {13: 1})):
+        put(10, c, rows); put(10, c, {11: -B0}); put(11, c, {11: 1})
+    put(10, 2, {0: 1, 3: 1, 1: -2}); put(10, 3, odd(0)); put(10, 7, odd(0)); put(10, 7, odd(1))
+    put(11, 2, odd(1)); put(11, 3, odd(1)); put(11, 7, {11: 1})
+    for cd in range(4):
+        for k, row, bit in ((10, 8, cd & 1), (11, 12, cd >> 1)):
+            put(k, 12 + cd, {row + 2: 1, row: -4, 11: 4 * B0 - (0 if bit else 4)}, 0, 1 if bit else -1)
     runs = []
     by = {}
     for (row, c), v in sorted(p.items()):
-        by.setdefault((row, v), []).append(c)
-    for (row, v), cs in by.items():
+        by.setdefault((row, float(v), c >= 160), []).append(c)
+    for (row, v, home), cs in by.items():
         while cs:
             best = [cs[0]]
             for c2 in cs[1:]:
@@ -103,14 +125,15 @@ def patterns():
                 if len(run) > len(best):
                     best = run
             st = best[1] - best[0] if len(best) > 1 else 1
-            runs.append((row // 4, slice(row % 4, row % 4 + 1), slice(best[0], best[-1] + 1, st), len(best), v))
+            cols = (best[0], best[-1] + 1, st)
+            for e in runs:
+                if e[0] == row // 4 and e[2] == row % 4 and e[3] == cols and e[5] == v:
+                    e[2] += 1
+                    break
+            else:
+                runs.append([row // 4, row % 4, row % 4 + 1, cols, len(best), v, home])
             cs = [c for c in cs if c not in best]
-    c0 = 16 * (NP - 1)
-    for q, vals in enumerate(((0.25, B0, -0.375), (1.0, 0, 0), (0.25, B0, -0.125), (0, 1.0, 0))):
-        for j, v in enumerate(vals):
-            if v:
-                runs.append((q, slice(0, 4), slice(c0 + j, c0 + j + 1), 4, float(v)))
-    return runs
+    return [(q, slice(a, b), slice(*cols), n * (b - a), v, home) for q, a, b, cols, n, v, home in runs]
 
 
 def rank_program(g, core, T, topo):
@@ -135,7 +158,7 @@ def rank_program(g, core, T, topo):
             if clock[q].get(k, 0) < v:
                 clock[q][k] = v
 
-    def deps(q, r, w, x):
+    def deps(q, r, w, x, acc):
         evs = {}
 
         def add(ev):
@@ -144,7 +167,8 @@ def rank_program(g, core, T, topo):
         for k in r:
             add(wr.get(k))
         for k in w:
-            add(wr.get(k))
+            if not acc:
+                add(wr.get(k))
             for ev in rd.get(k, {}).items():
                 add(ev)
         for b in x:
@@ -177,7 +201,7 @@ def rank_program(g, core, T, topo):
             return 0.05 + n * GA * CY
         if k == "s":
             return 0.05 + n * SCA * CY
-        return 0.03 + max(64, n * k) * CY
+        return FIX + max(64, n * k) * CY
 
     def op(q, fn, r=(), w=(), c=0.1, o=(), lat=0.0, kind="c", extra=None):
         x = sorted({int(k[1]) for k in list(r) + list(w) + list(o) if k[0] == "#"})
@@ -186,12 +210,12 @@ def rank_program(g, core, T, topo):
     def dma(q, out, in_, sem, r=(), w=(), lat=2.2):
         op(q, lambda: Qs[q].dma_start(out, in_), r, w, 0.1, (), lat, "d", sem)
 
-    def mm(items, r, w, o=()):
+    def mm(items, r, w, o=(), acc=False):
         def fn():
             for it in items:
                 i = P.matmul(*it)
             return i
-        op("t", fn, r, w, sum(0.005 + max(64, size(it[2])) * CY for it in items), o, 0.1)
+        op("t", fn, r, w, sum(0.005 + max(64, size(it[2])) * CY * TF for it in items), o, 0.02, extra=acc)
 
     def group(out, pairs, start=True, stop=True):
         return [(out, l, rr, start and k == 0, stop and k == len(pairs) - 1) for k, (l, rr) in enumerate(pairs)]
@@ -218,35 +242,37 @@ def rank_program(g, core, T, topo):
     def act(out, a, fn=AF.Copy, r=(), w=(), k=1, **kw):
         op("s", lambda: Sc.activation(out, a, fn, **kw), r, w, cost(size(out), k))
 
-    plans = {c: plan(topo, cores, c) for c in cores}
-    arrive = sum(len(call.get(core, ())) for c in cores for call in plans[c])
-    leave = sum(len(e) for call in plans[core] for e in call.values())
-
-    def send(kind, rnd, src, dst, r, w, landed):
-        ls = "l%s%d" % (kind, rnd)
+    def send(kind, rnd, src, dst, r, w, landed, parts=None, part=None):
+        plans = {c: plan(topo, cores, c, parts) for c in cores}
+        calls = plans[core] if part is None else plans[core][part:part + 1]
+        ls = "l%s%d" % (kind, rnd) + ("" if part is None else "_%d" % part)
+        arrive = sum(len(call.get(core, ())) for c in cores for call in plans[c])
+        leave = sum(len(e) for call in calls for e in call.values())
 
         def fn():
-            for call in plans[core]:
+            for call in calls:
                 trs = []
                 for d, engines in call.items():
                     rid, pid, _ = topo.addr(d)
                     trs.append(RemoteDMATransfer(dst_ids=[DstId(rid=rid, pnc=pid)], dma_engine_mask=sum(1 << e for e in engines),
                                                  remote_sem=T.sem["a%s%d" % (kind, rnd)], src=src(cores.index(d)), dst=dst))
                 g.remote_dma_fused(trs, local_sem=T.sem[ls])
-        op("g", fn, r, w, 0.6 * len(SPLIT), ["eng"], SENT, "r", (ls, landed))
+        rows = 96 if part is None else 16 * len(parts[part])
+        op("g", fn, r, w, 0.4 * len(calls) + (FIRST if ls == "lf0" else 0.0), ["eng"], SENT + ROW * rows, "r",
+           (ls, landed, "a%s%d" % (kind, rnd), arrive, leave))
 
     def emit(e):
         q = e["q"]
         TAG[0] = e["tag"]
-        deps(q, e["r"], e["w"], e["x"])
+        deps(q, e["r"], e["w"], e["x"], q == "t" and e["extra"])
         if q == "g" and e["kind"] == "c" and "cg" in total:
             need(q, ("cg", total["cg"]))
         if e["kind"] == "r":
-            ls, landed = e["extra"]
+            ls, landed, sem, arrive, leave = e["extra"]
             e["fn"]()
             total[ls] = leave
-            total["a" + ls[1:]] = arrive
-            wr[landed] = ("a" + ls[1:], arrive)
+            total[sem] = arrive
+            wr[landed] = (sem, arrive)
             ev = (ls, leave)
         else:
             sem, n = (e["extra"], 16) if e["kind"] == "d" else ("c" + q, 1)
@@ -255,7 +281,7 @@ def rank_program(g, core, T, topo):
             ev = (sem, total[sem])
         done(q, ev, e["r"], e["w"], e["x"])
 
-    def schedule(bias):
+    def graph():
         n = len(ops)
         pre = [dict() for _ in range(n)]
         lw, lr, lo = {}, {}, {}
@@ -265,7 +291,7 @@ def rank_program(g, core, T, topo):
                     pre[i][j] = d
             for k in e["r"] + e["w"]:
                 if k in lw:
-                    edge(*lw[k])
+                    edge(lw[k][0], 0.0 if e["extra"] is True and k in e["w"] else lw[k][1])
             for k in e["w"]:
                 for j in lr.get(k, ()):
                     edge(j, ops[j]["lat"] + WAKE)
@@ -287,47 +313,66 @@ def rank_program(g, core, T, topo):
         level = [0.0] * n
         for i in range(n - 1, -1, -1):
             level[i] = ops[i]["c"] + max([ops[i]["lat"]] + [d + level[j] for j, d in post[i]])
-        left = [len(p) for p in pre]
-        ready = [0.0] * n
-        free = {q: 0.0 for q in Qs}
-        held = {}
-        avail = [i for i in range(n) if not left[i]]
-        order = []
-        while avail:
-            st = {}
-            for i in avail:
-                e = ops[i]
-                t = max(ready[i], free[e["q"]])
-                for b in e["x"]:
-                    for q2, t2 in held.get(b, {}).items():
-                        if q2 != e["q"] and t2 > t:
-                            t = t2
-                st[i] = t
-            first = min(avail, key=lambda i: st[i])
-            q = ops[first]["q"]
-            near = [i for i in avail if ops[i]["q"] == q and st[i] <= st[first] + SLACK * ops[first]["c"] + 0.02]
-            i = max(near, key=lambda i: (level[i] + bias.get(ops[i]["tag"] + q, 0.0), -i))
+        return [list(p.items()) for p in pre], post, level
+
+    def place(turn, before, back):
+        start = [0.0] * len(ops)
+        busy = {q: ([], []) for q in Qs}
+        held = [[] for _ in range(8)]
+        end = 0.0
+        for i in turn:
             e = ops[i]
-            end = st[i] + e["c"]
-            free[q] = end
-            for b in e["x"]:
-                held.setdefault(b, {})[q] = end + e["lat"] + WAKE
-            order.append(i)
-            avail.remove(i)
-            for j, d in post[i]:
-                ready[j] = max(ready[j], end + d)
-                left[j] -= 1
-                if not left[j]:
-                    avail.append(j)
-        return max(ready + list(free.values())), order
+            c, q, hold = e["c"], e["q"], e["lat"] + WAKE
+            t = e["lat"] if back else 0.0
+            for j, d in before[i]:
+                t = max(t, start[j] + ops[j]["c"] + d)
+            a, b = busy[q]
+            while True:
+                lo, hi = 0, len(b)
+                while lo < hi:
+                    mid = (lo + hi) // 2
+                    if b[mid] <= t:
+                        lo = mid + 1
+                    else:
+                        hi = mid
+                while lo < len(a) and a[lo] < t + c:
+                    t = b[lo]
+                    lo += 1
+                t0 = t
+                x0, x1 = (t - hold, t + c) if back else (t, t + c + hold)
+                for k in e["x"]:
+                    for y0, y1, q2 in held[k]:
+                        if q2 != q and y0 < x1 and x0 < y1:
+                            t = max(t, y1 + (hold if back else 0.0))
+                if t == t0:
+                    break
+            a.insert(lo, t)
+            b.insert(lo, t + c)
+            for k in e["x"]:
+                held[k].append((x0, x1, q))
+            start[i] = t
+            end = max(end, t + c + (0.0 if back else e["lat"]))
+        return end, start
+
+    def schedule(net, key):
+        pre, post = net[0], net[1]
+        n = len(ops)
+        key = list(key)
+        for i in range(n):
+            for j, d in pre[i]:
+                key[i] = max(key[i], key[j] + 1e-6)
+        end, start = place(sorted(range(n), key=lambda i: key[i]), pre, False)
+        late = place(sorted(range(n), key=lambda i: (-start[i] - ops[i]["c"], -i)), post, True)[1]
+        again = place(sorted(range(n), key=lambda i: (-late[i] - ops[i]["c"], i)), pre, False)
+        return again if again[0] <= end else (end, start)
 
     cb = lambda n, a=0: T.cb[:, CB.index(n), a:a + 128]
     ch = lambda n, a=0: T.ch[:, CH.index(n), a:a + 128]
     I = T.IW[:, 8:136]
     col = lambda j: T.col[:, j:j + 1]
     RM = lambda j: T.RM[:, j:j + 1]
-    RC, LT8, INIT, Z1C, OC, LT4, R1, ZAC, SUB, THR, S1, S2 = range(12)
-    P01 = T.P01
+    RC, LT8, INIT, Z1C, OC, R1, ZAC, SUB, THR, S1, S2, S3, LA, LB, GE8, XR, ON, XM, FR, KX, WB, PN, I4, O16, CR1, CR2, CRS = range(27)
+    WRAP = 256 * B0
     now = [0]
 
     def tag(s):
@@ -337,7 +382,7 @@ def rank_program(g, core, T, topo):
         return ["#%d_%d" % (b, j) for j in range(lo // 16, (hi + 15) // 16)]
 
     def ps(b, lo=0, hi=512):
-        return P01[:, 32 * b + lo // 16:32 * b + hi // 16] if b < 2 else T["P%d" % b][:, lo:hi]
+        return T["P%d" % b][:, lo:hi]
 
     tag("c0")
     ms(T.X[:], 0, w=["X0"])
@@ -345,38 +390,56 @@ def rank_program(g, core, T, topo):
     for k in range(4):
         dma("y", T.C[:, 1024 * k:1024 * k + 1024], T.cf[:, 1024 * k:1024 * k + 1024], "dc%d" % k, w=["C%d" % k], lat=2.9 + k)
     for e in range(4):
-        dma("ys"[e // 2], T.X[e:128:16, :], T.x0[e:32:4, :], "dx", r=["X0"], w=["X%d" % (e + 1)])
+        dma("ys"[e // 2], T.X[(0, 4, 10, 14)[e]:128:16, :], T.x0[e:32:4, :], "dx", r=["X0"], w=["X%d" % (e + 1)])
     dma("s", T.tgr[:], T.tg[:], "dtg", w=["tgr"])
-    dma("y", T.Fr[:, 0:2048], T.ft[:], "df", r=["C3"], w=["Fr"], lat=3.5)
-    op("g", lambda: g.affine_select(T.IW[:], T.ones[:, 0:136], [[-1, 136]], A.is_equal, 0.0, 8, 1), ["ones"], ["IW"], 0.45)
+    dma("y", T.F[:, 0:2048], T.ft[:], "df", r=["C3"], w=["F"], lat=3.5)
+    op("g", lambda: g.affine_select(T.IW[:], T.ones[:, 0:144], [[-1, 144]], A.is_equal, 0.0, 8, 1), ["ones"], ["IW"], 0.45)
+    op("g", lambda: g.iota(T.PI[:], [[256, 6], [1, 32]], 256, 0, allow_small_or_imprecise_dtypes=True), [], ["PI"], 0.5)
     op("g", lambda: g.iota(T.pc[:, 0:1], [[0, 1]], 0, 1), [], ["pc"], 0.14)
     op("g", lambda: g.iota(T.J[:], [[1, 16]], 0, 0, allow_small_or_imprecise_dtypes=True), [], ["J"], 0.17)
     op("g", lambda: g.affine_select(T.BDt[:], T.ones[:, 0:128], [[-16, 8], [0, 16]], A.is_ge, 0.0, 0, 1), ["ones"], ["BDt"], 0.44)
     op("g", lambda: g.affine_select(T.BD[:], T.BDt[:], [[16, 8], [0, 16]], A.is_ge, 0.0, 15, -1), ["BDt"], ["BD"], 0.44)
+    op("g", lambda: g.affine_select(cb("xC"), T.ones[:, 0:128], [[-16, 8], [-1, 4], [0, 4]], A.is_equal, 0.0, 0, 1), ["ones"], ["xC"], 0.44)
+    act(T.GM[:], T.BD[:, 0:128:16], r=["BD"], w=["GM"])
+    ms(T.MB[:, :, 128:144], 0.0, w=["MBz"])
     op("g", lambda: g.iota(T.trash[:], [[-2304, 2], [16, 16]], 4352, 0, allow_small_or_imprecise_dtypes=True), [], ["trash"], 0.2)
     for k in range(4):
-        op("g", lambda k=k: g.iota(T.IOTA[:, 512 * k:512 * k + 512], [[1, 512]], 512 * k, 0), [], ["IOTA%d" % k], 1.2)
+        op("g", lambda k=k: g.iota(T.IOTA[:, 512 * k:512 * k + 512], [[1, 512]], 512 * k, 0, allow_small_or_imprecise_dtypes=True), [], ["IOTA%d" % k], 1.1)
     ms(T.VEC[:], 0.0, w=["VEC"])
     ms(T.Z[:], 0.0, w=["Z"])
     ms(T.comb[:], 0.0, w=["comb"])
     ms(T.RST[:], 0.0625, w=["RST"])
-    ms(T.cb[:, 0:4, :], 0.0, w=["cbz"])
+    ms(T.cb[:, 0:3, :], 0.0, w=["cbz"])
+    ms(T.ch[:, 0:3, :], 0.0, w=["chz"])
     ms(T.two[:], 2.0, w=["two"])
     for q in range(4):
         ms(T.comb[32 * q:32 * q + 1, 4 * q + 3:128:16], 1.0, r=["comb"], w=["comb%d" % q])
     ms(T.RST[:, 0:256:16], -1024.0, w=["RST"])
-    vk = []
-    for k, (q, rows, cols, n, v) in enumerate(patterns()):
-        out = T.VEC[32 * q:32 * q + 1, rows, cols]
-        vk.append("vec%d" % k)
-        if VECQ[k % len(VECQ)] == "v":
-            ms(out, v, r=["VEC"], w=[vk[-1]])
-        elif VECQ[k % len(VECQ)] == "g" and v == int(v):
-            op("g", lambda out=out, n=n, v=v: g.iota(out, [[0, n]], int(v), 0, allow_small_or_imprecise_dtypes=True), ["VEC"], [vk[-1]], 0.15)
+    vk = [[], []]
+    for k, (q, rows, cols, n, v, home) in enumerate(patterns()):
+        tag("vh" if home else "vo")
+        out, key, who = T.VEC[32 * q:32 * q + 1, rows, cols], "vec%d" % k, (VECH if home else VECQ)
+        vk[home].append(key)
+        if who[k % len(who)] == "v":
+            ms(out, v, r=["VEC"], w=[key])
+        elif who[k % len(who)] == "g" and v == int(v):
+            op("g", lambda out=out, n=n, v=v: g.iota(out, [[0, n]], int(v), 0, allow_small_or_imprecise_dtypes=True), ["VEC"], [key], 0.2)
         else:
-            act(out, T.ones[32 * q:32 * q + 1, 0:n], r=["VEC", "ones"], w=[vk[-1]], scale=v)
-    mm(group(ps(5, 0, NP * 16), [(T.comb[:, 3 - k:131 - k], T.VEC[:, k, :]) for k in range(4)]),
-       vk + ["comb%d" % q for q in range(4)], pk(5, 0, NP * 16))
+            act(out, T.ones[32 * q:32 * q + 1, 0:n], r=["VEC", "ones"], w=[key], scale=v)
+    MBk = [["MBz"], ["MBz"]]
+    for home, lo, hi in ((1, 10, 12), (0, 0, 10)):
+        tag("vh" if home else "vo")
+        b = 5 - home
+        mm(group(ps(b, 16 * lo, 16 * hi), [(T.comb[:, 3 - k:131 - k], T.VEC[:, k, 16 * lo:16 * hi]) for k in range(4)]),
+           vk[home] + ["comb%d" % q for q in range(4)], pk(b, 16 * lo, 16 * hi))
+        cp(T.PAT[:, lo:hi], ps(b, 16 * lo, 16 * hi), pk(b, 16 * lo, 16 * hi), ["PAT%d" % home])
+        for k in range(8):
+            key = "MB%d_%d" % (home, k)
+            MBk[home].append(key)
+            if k < MBS:
+                act(T.MB[:, lo:hi, 16 * k:16 * k + 16], T.PAT[:, lo:hi], r=["PAT%d" % home, "GM"], w=[key], scale=T.GM[:, k:k + 1])
+            else:
+                ts(T.MB[:, lo:hi, 16 * k:16 * k + 16], T.PAT[:, lo:hi], T.GM[:, k:k + 1], None, A.mult, r=["PAT%d" % home, "GM"], w=[key], k=0.5)
     tag("c1")
     b15 = T.BD[:, 15:128:16]
     ts(T.pc[:, 1:2], T.pc[:, 0:1], 15, None, A.bitwise_and, r=["pc"], w=["pc1"])
@@ -384,71 +447,85 @@ def rank_program(g, core, T, topo):
     ts(T.pc[:, 0:1], T.pc[:, 1:2], 7, None, A.bitwise_and, r=["pc1"], w=["pc"])
     ts(T.RM[:], T.J[:], col(RC), None, A.is_equal, r=["J", "RC"], w=["RM"])
     ts(col(LT8), col(RC), 8.0, None, A.is_lt, r=["RC"], w=["LT8"])
-    ts(col(INIT), col(RC), 8.0, -1.0, A.is_lt, A.mult, r=["RC"], w=["INIT"])
-    ts(col(Z1C), col(RC), -8.0, 192.0, A.add, A.mult, r=["RC"], w=["Z1C"])
-    ts(col(LT4), col(RC), 4.0, None, A.is_lt, r=["RC"], w=["LT4"])
+    ts(col(LB), col(RC), 1.0, 32.0, A.add, A.mult, r=["RC"], w=["LB"])
+    ts(col(GE8), col(RC), 8.0, None, A.is_ge, r=["RC"], w=["GE8"])
+    ts(col(LB), col(LB), col(LT8), None, A.mult, r=["LT8"], w=["LB"])
+    ts(col(LA), col(RC), 8.0, 1.0 / 2048, A.is_ge, A.mult, r=["RC"], w=["LA"])
+    ts(col(INIT), col(LB), col(LT8), -32.0, A.subtract, A.add, r=["LB", "LT8"], w=["INIT"])
+    ts(col(Z1C), col(GE8), 2047.0, 1.0, A.mult, A.add, r=["GE8"], w=["Z1C"])
     ts(col(OC), T.pc[:, 0:1], B0, None, A.add, r=["pc"], w=["OC"])
-    ts(col(Z1C), col(Z1C), col(LT8), None, A.max, r=["LT8"], w=["Z1C"])
-    ts(T.lim[:], T.ones[:, 0:S], col(LT8), 254.0, A.mult, A.mult, r=["LT8", "ones"], w=["lim"], k=0.5)
-    ts(T.lim[:], T.lim[:], 1.0, None, A.add, w=["lim"], k=0.5)
-    cp(T.cb[:, 1, 15:128:16], b15, ["BD", "cbz"], ["Z2"])
-    tt(T.BDt[:], T.IW[:, 8:136], T.IW[:, 4:132], A.add, ["IW"], ["BDt"])
-    tt(T.BDt[:], T.BDt[:], T.IW[:, 0:128], A.add, ["IW"], ["BDt"])
-    ts(cb("xrep"), T.BDt[:], col(LT4), None, A.mult, r=["BDt", "LT4"], w=["xrep"], k=0.5)
-    ts(T.cb[:, 0, 15:128:16], b15, col(Z1C), None, A.mult, r=["BD", "Z1C", "cbz"], w=["Z1"])
-    cp(T.col[:, S1:S1 + 3], ps(5, 160, 163), pk(5, 160, 176), ["S1"])
-    cp(T.PAT[:], ps(5, 0, 160), pk(5, 0, 160), ["PAT"])
-    tt(col(S2), col(S2), col(S2 + 1), A.add, w=["S1"])
-    ms(T.MB[:, :, 128:144], 0.0, w=["MB8"])
-    ms(T.ch[:, 0, :], 0.0, w=["chz"])
+    ts(T.lim[:], T.PI[:], col(LA), col(LB), A.mult, A.add, r=["PI", "LA", "LB"], w=["lim"])
+    ts(T.ch[:, 1, 15:128:16], b15, col(Z1C), None, A.mult, r=["BD", "Z1C", "chz"], w=["Z1"])
+    ts(col(XR), RM(10), RM(14), None, A.add, r=["RM"], w=["XR"])
+    ts(col(ON), RM(11), RM(15), None, A.add, r=["RM"], w=["ON"])
+    ts(col(XM), col(XR), col(LT8), None, A.add, r=["XR", "LT8"], w=["XM"])
+    ts(T.pc[:, 2:3], T.pc[:, 1:2], 3, None, A.bitwise_and, r=["pc1"], w=["pc2"])
+    ts(col(S1), col(XR), 0.75, 0.25, A.mult, A.add, r=["XR"], w=["S1"])
+    ts(col(FR), col(XR), col(ON), 0.5, A.add, A.is_lt, r=["XR", "ON"], w=["FR"])
+    ts(col(S2), T.pc[:, 2:3], 0.25, B0 - 0.375, A.mult, A.add, r=["pc2"], w=["S2"])
+    ts(col(S1), col(ON), -0.25, col(S1), A.mult, A.add, r=["ON"], w=["S1"])
+    ts(col(S2), col(S2), col(FR), col(ON), A.mult, A.add, r=["FR", "ON"], w=["S2"])
+    mm([(ps(6, 0, 128), cb("xC"), cb("xC"), True, True)], ["xC"], pk(6, 0, 128))
+    ts(cb("xF"), ps(6, 0, 128), col(XM), None, A.mult, r=pk(6, 0, 128) + ["XM"], w=["xF"])
+    act(cb("xN"), ps(6, 0, 128), r=pk(6, 0, 128), w=["xN"], scale=-64.0)
+    act(cb("dF"), T.BD[:], r=["BD", "RM"], w=["dF"], scale=RM(14))
+    tag("c2")
+    cp(col(I4), T.pc[:, 2:3], ["pc2"], ["I4"])
+    ts(col(KX), col(LT8), -4 * B0, WRAP, A.mult, A.add, r=["LT8"], w=["KX"])
+    ts(col(WB), col(LT8), -4 * B0 / 256, B0 - 255.0 / 512, A.mult, A.add, r=["LT8"], w=["WB"])
+    ts(col(S3), col(S1), col(KX), col(S2), A.mult, A.add, r=["S1", "S2", "KX"], w=["S3"])
+    ts(col(PN), col(RC), 12.0, -8192.0, A.is_ge, A.mult, r=["RC"], w=["PN"])
+    ts(cb("dN"), T.BD[:], RM(12), -256.0, A.mult, A.mult, r=["BD", "RM"], w=["dN"], k=0.5)
+    ts(ch("cnt"), T.BD[:], col(GE8), None, A.mult, r=["BD", "GE8"], w=["cnt"], k=0.5)
+    cp(T.ch[:, 2, 15:128:16], b15, ["BD", "chz"], ["Zh"])
     ms(T.TB[:], 0.0, w=["TB"])
-    act(T.GM[:], T.BD[:, 0:128:16], r=["BD"], w=["GM"])
-    for k in range(8):
-        if k < MBS:
-            act(T.MB[:, :, 16 * k:16 * k + 16], T.PAT[:], r=["PAT", "GM"], w=["MB%d" % k], scale=T.GM[:, k:k + 1])
-        else:
-            ts(T.MB[:, :, 16 * k:16 * k + 16], T.PAT[:], T.GM[:, k:k + 1], None, A.mult, r=["PAT", "GM"], w=["MB%d" % k], k=0.5)
-    MBk = ["MB%d" % k for k in range(9)]
+    ms(T.D0[:, 0:1024:4], 0.0, w=["D0z"])
+    ms(T.R5[:], 1.0, w=["R5", "D04"])
+    ms(T.R5[:, 0:1280:5], 0.0, w=["R5"])
+    ts(col(O16), col(RC), 12.0, 1.0 / 16, A.is_ge, A.mult, r=["RC"], w=["O16"])
+    ts(col(CR1), RM(3), 2.0, col(O16), A.mult, A.add, r=["RM", "O16"], w=["CR1"])
+    ts(col(CR2), RM(3), -4.0, col(O16), A.mult, A.add, r=["RM", "O16"], w=["CR2"])
+    ts(col(CR2), RM(7), 2.0, col(CR2), A.mult, A.add, r=["RM"], w=["CR2"])
+    ts(col(CRS), col(O16), 4.0, RM(3), A.mult, A.add, r=["RM", "O16"], w=["CRS"])
+    ts(col(CRS), RM(7), -2.0, col(CRS), A.mult, A.add, r=["RM"], w=["CRS"])
+    ts(cb("rs"), T.BD[:], col(CRS), 1.0 / 256, A.mult, A.mult, r=["BD", "CRS"], w=["rs"], k=0.5)
+    for name, sc, key in [("r1", col(CR1), "CR1"), ("r2", col(CR2), "CR2")] + [("w%d" % k, RM(12 + k), "RM") for k in range(4)]:
+        act(cb(name), T.BD[:], r=["BD", key], w=[name], scale=sc)
+    ms(T.PD[:, 4:1280:5], 1152.0 - 255.0 / 512, w=["PDk"])
     scan(T.pw[:], T.two[:], T.RM[:], 0.0, A.mult, A.add, ["two", "RM"], ["pw"])
-    ts(col(ZAC), RM(12), 8192.0, RM(8), A.mult, A.add, r=["RM"], w=["ZAC"])
-    ts(col(ZAC), RM(9), 2048.0, col(ZAC), A.mult, A.add, r=["RM"], w=["ZAC"])
-    ts(col(SUB), RM(8), RM(9), 2048.0, A.add, A.mult, r=["RM"], w=["SUB"])
+    ts(T.R4[:], T.J[:, 0:4], col(I4), None, A.is_equal, r=["J", "I4"], w=["R4"])
+    ts(col(ZAC), T.R4[:, 2:3], 8192.0, T.R4[:, 0:1], A.mult, A.add, r=["R4"], w=["ZAC"])
+    ts(col(ZAC), T.R4[:, 1:2], 2048.0, col(ZAC), A.mult, A.add, r=["R4"], w=["ZAC"])
+    ts(col(SUB), col(I4), 2.0, 2048.0, A.is_lt, A.mult, r=["I4"], w=["SUB"])
     ts(col(R1), col(RC), 1.0, None, A.add, r=["RC"], w=["R1"])
     ts(T.trash[:], T.trash[:], col(RC), None, A.add, r=["RC"], w=["trash"])
     ts(col(THR), T.pw[:, 15:16], 2.5, None, A.mult, r=["pw"], w=["THR"])
     act(T.tgc[:], T.tgr[:], AF.Identity, ["tgr"], ["tgc"], bias=-128.0)
-    ts(T.ch[:, 0, 15:128:16], b15, col(ZAC), None, A.mult, r=["ZAC", "chz", "BD"], w=["ZA"])
-    for k in range(9):
-        ts(ch("b%d" % k), T.BD[:], RM(k), 1.0 / 256 if k < 4 else 1.0, A.mult, A.mult, r=["BD", "RM"], w=["b%d" % k], k=0.5)
-    cp(ch("Ih"), I, ["IW"], ["Ih"], k=0.5)
-    ts(T.cb[:, 2, 15:128:16], b15, RM(0), None, A.mult, r=["BD", "RM", "cbz"], w=["Z3"])
-    ts(T.cb[:, 3, 15:128:16], b15, RM(0), 128.0, A.mult, A.mult, r=["BD", "RM", "cbz"], w=["Zm"])
-    ts(cb("pen"), T.BD[:], RM(12), -131072.0, A.mult, A.mult, r=["BD", "RM"], w=["pen"], k=0.5)
-    for name, sc, key in (("orep", RM(3), "RM"), ("cnt", col(LT8), "LT8"), ("pow", T.pw[:, 15:16], "pw"), ("big", 65536.0, "BD"), ("ycw", col(R1), "R1")):
+    mm([(ps(6, 128, 256), cb("xC"), I, True, True)], ["xC", "IW"], pk(6, 128, 256))
+    ts(T.ch[:, 0, 12:140], ps(6, 128, 256), col(ZAC), None, A.mult, r=["ZAC", "chz"] + pk(6, 128, 256), w=["ZA"])
+    for k in range(4):
+        ts(ch("b%d" % k), T.BD[:], RM(4 * k), None, A.mult, r=["BD", "RM"], w=["b%d" % k], k=0.5)
+    ts(T.cb[:, 1, 15:128:16], b15, RM(0), None, A.mult, r=["BD", "RM", "cbz"], w=["Z3"])
+    ts(T.cb[:, 2, 15:128:16], b15, col(R1), None, A.mult, r=["BD", "R1", "cbz"], w=["Zy"])
+    for name, sc, key in (("pen", col(PN), "PN"), ("dC", RM(3), "RM"), ("pow", T.pw[:, 15:16], "pw"), ("big", 65536.0, "BD"), ("ycw", col(R1), "R1")):
         act(cb(name), T.BD[:], r=["BD", key], w=[name], scale=sc)
-    for name, sc in (("I64", 64.0), ("In", -1.0)):
+    act(T.n256[:], T.BD[:], r=["BD"], w=["n256"], scale=-256.0)
+    for name, sc in (("I64", 64.0), ("In", -1.0), ("I2", 2.0)):
         act(cb(name), I, r=["IW"], w=[name], scale=sc)
-    SFk = ["SF%d" % o for o in range(N)]
-
-    def zero_sf():
-        for o in range(N):
-            act(T.SF[:, S * o:S * o + CAP], T.Z[:, 0:CAP], r=["Z"], w=[SFk[o]])
-    zero_sf()
-    RYz = ["RYz%d" % k for k in range(3)]
-    for k in range(3):
-        act(T.RY[:, 512 * k:512 * k + 512], T.Z[:, 0:512], r=["Z"], w=[RYz[k]])
+    for r in range(RO):
+        act(T["SF%d" % r][:, 0:256], T.Z[:, 0:256], r=["Z"], w=["SF%d" % r])
+    act(T.ST[:, 0:256], T.Z[:, 0:256], r=["Z"], w=["ST"])
+    RYz = ["RYz%d" % k for k in range(4)]
+    for k in range(4):
+        act(T.RY[:, 256 + 392 * k:648 + 392 * k], T.Z[:, 0:392], r=["Z"], w=[RYz[k]])
     Mz = ["Mz%d" % k for k in range(8)]
     for k in range(8):
-        act(T.ST[:, S * k:S * k + CAP], T.Z[:, 0:CAP], r=["Z"], w=["STz%d" % k])
         part = T.M[:, 256 + 512 * k:768 + 512 * k]
         if k < MZG:
-            op("g", lambda part=part: g.iota(part, [[0, 512]], 0, 0, allow_small_or_imprecise_dtypes=True), [], [Mz[k]], 1.2)
+            op("g", lambda part=part: g.iota(part, [[0, 512]], 0, 0, allow_small_or_imprecise_dtypes=True), [], [Mz[k]], 1.1)
         else:
-            act(part, T.Z[:, 0:512], r=["Z"], w=[Mz[k]])
-    tag("fp")
-    Fk = ["Fp%d" % k for k in range(16)]
-    for m in range(16):
-        act(T.Fp[:, 128 * m:128 * m + 128], T.Fr[:, m:2048:16], AF.Identity, ["Fr"], [Fk[m]], bias=-128.0)
+            ms(part, 0.0, w=[Mz[k]])
+    Fk = ["F"]
 
     tag("am")
     for k in range(8):
@@ -475,135 +552,155 @@ def rank_program(g, core, T, topo):
 
     def home_update(r):
         tag("hu")
-        ry = ["RY", "RYr", "RYg", "slot"]
-        ts(T.st[:], T.RY[:].indirect(T.slot[:]), 8.0, -8.0, A.min, A.max, r=ry, w=["st"], k="g")
+        ry = ["RY", "RYg", "slot"] + RYz + ["RYr%d" % k for k in range(len(YP))]
+        mm([(ps(0, 0, S), cb("xF"), T.Fh[:], True, False)], ["Fh", "xF"], pk(0))
+        mm([(ps(3, 0, S), cb("xF"), T.Fh[:], True, False)], ["Fh", "xF"], pk(3))
+        if r < RO - 1:
+            mm([(ps(2, 0, S), cb("dF"), T.Fh[:], True, False)], ["Fh", "dF"], pk(2))
         act(T.yg[:, r, :], T.RY[:].indirect(T.slot[:]), r=ry, w=["yg%d" % r], k="g")
-        tt(T.X[:], T.X[:], T.st[:], A.add, ["st"], Xk)
-        ts(T.X[:], T.X[:], 255, None, A.bitwise_and, w=Xk)
+        if CLF:
+            ts(T.cl[:], T.RY[:].indirect(T.slot[:]), 8.0, -8.0, A.min, A.max, r=ry, w=["cl"], k="g")
+        else:
+            ts(T.cl[:], T.yg[:, r, :], 8.0, -8.0, A.min, A.max, r=["yg%d" % r], w=["cl"], k=0.5)
+        mm([(ps(0, 0, S), cb("xC"), T.cl[:], False, True)], ["cl", "xC"], pk(0), acc=True)
+        act(T.wr[:], ps(0, 0, S), AF.Identity, pk(0) + ["WB"], ["wr"], bias=col(WB), scale=1.0 / 256)
+        if r < RO - 1:
+            mm([(ps(2, 0, S), cb("dC"), T.cl[:], False, False)], ["cl", "dC"], pk(2), acc=True)
+            mm([(ps(2, 0, S), cb("dN"), T.wr[:], False, True)], ["wr", "dN"], pk(2), acc=True)
+        mm([(ps(3, 0, S), cb("xC"), T.cl[:], False, False)], ["cl", "xC"], pk(3), acc=True)
+        mm([(ps(3, 0, S), cb("xN"), T.wr[:], False, True)], ["wr", "xN"], pk(3), acc=True)
 
     def home_route(r):
         tag("hr")
-        ts(T.ob[:], T.X[:], 1.0 / 32, B0 - 0.484375, A.mult, A.add, r=Xk, w=["ob"])
-        mm([(ps(2, 0, S), cb("orep"), T.ob[:], True, True)], ["ob", "orep"], pk(2, 0, S))
-        cp(T.xb[:], T.X[:], Xk, ["xb"])
-        mm([(ps(3, 0, S), cb("xrep"), T.xb[:], True, True)], ["xb", "xrep"], pk(3, 0, S))
-        ts(T.h[:], ps(2, 0, S), col(OC), None, A.is_equal, r=pk(2, 0, S) + ["OC"], w=["h"])
-        act(T.Fh[:], ps(3, 0, S), AF.Identity, pk(3, 0, S) + ["S1"], ["Fh"], bias=col(S2), scale=col(S1))
+        if r == 0:
+            cp(T.Fh[:], T.X[:], Xk, ["Fh"])
+            mm([(ps(2, 0, S), cb("dF"), T.Fh[:], True, True)], ["Fh", "dF"], pk(2))
+            mm([(ps(3, 0, S), cb("xF"), T.Fh[:], True, True)], ["Fh", "xF"], pk(3))
+        act(T.ob[:], ps(2, 0, S), AF.Identity, pk(2), ["ob"], bias=B0 - 0.484375 + (WRAP / 32 if r else 0.0), scale=1.0 / 32)
+        ts(T.h[:], T.ob[:], col(OC), None, A.is_equal, r=["ob", "OC"], w=["h"], k=0.5)
+        act(T.Fh[:], ps(3, 0, S), AF.Identity, pk(3) + ["S1", "S3" if r else "S2"], ["Fh"], bias=col(S3 if r else S2), scale=col(S1))
+        mm([(ps(0, 0, S), T.MB[:, 11, 0:128], T.Fh[:], True, True)], ["Fh"] + MBk[1], pk(0))
+        mm([(ps(3, 0, S), T.MB[:, 10, 0:128], T.Fh[:], True, True)], ["Fh"] + MBk[1], pk(3))
+        act(T.Lv[:], ps(0, 0, S), r=pk(0), w=["Lv"])
+        tt(T.Lh[:], ps(3, 0, S), T.Lv[:], A.mult, pk(3) + ["Lv"], ["Lh"])
         scan(T.cum[:], T.h[:], T.lim[:], col(INIT), A.add, A.min, ["h", "lim", "INIT"], ["cum"], k=0.5)
-        tt(T.val[:], T.h[:], T.cum[:], A.mult, ["h", "cum"], ["val"])
-        mm(group(ps(4, 0, 12), [(cb("Z1", 15 - k), T.val[:, k:S:16]) for k in range(16)]), ["val", "Z1"], pk(4, 0, 12))
+        scan(T.val[:], T.cum[:], T.h[:], 0.0, A.max, A.mult, ["h", "cum"], ["val"], k=0.5)
+        mm(group(ps(4, 0, 12), [(ch("Z1", 15 - k), T.val[:, k:S:16]) for k in range(16)]), ["val", "Z1"], pk(4, 0, 12))
         cp(T.slot[:], ps(4, 0, 12), pk(4, 0, 12), ["slot"])
-        cp(T.SF[:].indirect(T.slot[:]), T.Fh[:], ["slot", "Fh"], SFk, k="s")
-        RF, RT = T["RF%d" % r], T["RT%d" % r]
-        send("f", r, lambda o: T.SF[:, S * o:S * o + CAP], RF[:, CAP * me:CAP * me + CAP], SFk + RYz, ["RYg"], "RFr%d" % r)
-        act(RF[:, CAP * me:CAP * me + CAP], T.SF[:, S * me:S * me + CAP], r=SFk, w=["RF%d" % r])
-        mm([(ps(4, 256, 256 + S), cb("cnt"), T.val[:], True, True)], ["val", "cnt"], pk(4, 256, 256 + S))
-        act(T.sg[:, r, :], ps(4, 256, 256 + S), AF.Sign, pk(4, 256, 256 + S), ["sg%d" % r], bias=31.5, scale=-1.0)
+        SF, RF, RT = T["SF%d" % r], T["RF%d" % r], T["RT%d" % r]
+        cp(SF[:].indirect(T.slot[:]), T.Lh[:], ["slot", "Lh"], ["SF%d" % r], k="s")
+        send("f", r, lambda o: SF[:, CAP * o:CAP * o + CAP], RF[:, CAP * me:CAP * me + CAP], ["SF%d" % r], ["RYg"], "RFr%d" % r)
+        act(RF[:, CAP * me:CAP * me + CAP], SF[:, CAP * me:CAP * me + CAP], r=["SF%d" % r], w=["RF%d" % r])
+        mm([(ps(4, 256, 256 + S), ch("cnt"), T.val[:], True, True)], ["val", "cnt"], pk(4, 256, 256 + S))
+        act(T.sg[:, r, :], ps(4, 256, 256 + S), AF.Sign, pk(4, 256, 256 + S), ["sg%d" % r], bias=0.03125, scale=-1.0)
         tag("ht")
-        cp(T.ST[:].indirect(T.slot[:]), T.tgc[:], ["slot", "tgc"] + ["STz%d" % k for k in range(8)], ["ST"], k="s")
-        send("t", r, lambda o: T.ST[:, S * o:S * o + CAP], RT[:, CAP * me:CAP * me + CAP], ["ST"] + ["Mrow%d" % k for k in range(4)], [], "RTr%d" % r)
-        act(RT[:, CAP * me:CAP * me + CAP], T.ST[:, S * me:S * me + CAP], r=["ST"], w=["RT%d" % r])
-        if r < RO - 1:
-            zero_sf()
+        cp(T.ST[:].indirect(T.slot[:]), T.tgc[:], ["slot", "tgc"], ["ST"], k="s")
+        send("t", r, lambda o: T.ST[:, CAP * o:CAP * o + CAP], RT[:, CAP * me:CAP * me + CAP], ["ST"] + ["Mrow%d" % k for k in range(4)], [], "RTr%d" % r)
+        act(RT[:, CAP * me:CAP * me + CAP], T.ST[:, CAP * me:CAP * me + CAP], r=["ST"], w=["RT%d" % r])
 
     Mk = ["M"] + ["Mrow%d" % k for k in range(4)] + ["Mwrap%d" % k for k in range(1, 4)]
     Ck = ["C%d" % k for k in range(4)]
-    Nk = ["Fn%d" % k for k in range(16)]
 
     def owner_values(r):
         tag("hash")
         RF = T["RF%d" % r]
-        rf = ["RF%d" % r, "RFr%d" % r] + MBk
-        for k0, b in ((0, 4), (3, 5)):
-            for j in (1, 0, 2):
-                mm(group(ps(b, 64 * j, 64 * j + 64), [(T.MB[:, k0 + j, 3 - q:131 - q], RF[:, q:256:4]) for q in range(4)]), rf, pk(b, 64 * j, 64 * j + 64))
-        mm([(ps(6, 256, 512), T.MB[:, 7, 0:128], RF[:], True, True)], rf, pk(6, 256, 512))
-        mm([(ps(6, 0, 256), T.MB[:, 6, 0:128], RF[:], True, True)], rf, pk(6, 0, 256))
-        mm([(ps(7, 0, 256), T.MB[:, 8, 0:128], RF[:], True, True)], rf, pk(7, 0, 256))
+        rf = ["RF%d" % r, "RFr%d" % r] + MBk[0]
+        for j in (1, 0, 2):
+            mm(group(ps(4, 64 * j, 64 * j + 64), [(T.MB[:, j, 12 - 4 * q:140 - 4 * q], RF[:, q:256:4]) for q in range(4)]), rf, pk(4, 64 * j, 64 * j + 64))
+        for k, b, lo in ((4, 5, 256), (3, 5, 0), (5, 3, 0)):
+            mm([(ps(b, lo, lo + 256), T.MB[:, k, 0:128], RF[:], True, True)], rf, pk(b, lo, lo + 256))
         cp(T.hv[:], ps(4, 64, 128), pk(4, 64, 128), ["hv"])
         tt(T.hp[:], ps(4, 0, 64), T.hv[:], A.mult, ["hv"] + pk(4, 0, 64), ["hp"])
         tt(T.hi[:], ps(4, 128, 192), T.hp[:], A.add, ["hp"] + pk(4, 128, 192), ["hi"])
         ts(T.hi[:], T.hi[:], 2, 4095, A.arith_shift_right, A.bitwise_and, w=["hi"])
         cp(T.ML[:], T.hi[:], ["hi"], ["ML"])
-        act(T.Mo[:, 16 * MGV:1024], T.M[:, 256:4352].indirect(T.ML[:, MGV:64]), r=Mk + ["ML"], w=["Mo"], k="g")
-        if MGV:
-            cp(T.Mo[:, 0:16 * MGV], T.M[:, 256:4352].indirect(T.ML[:, 0:MGV]), Mk + ["ML"], ["Mo2"], k="g")
+        for k, (lo, n) in enumerate(LCH):
+            tag("mo%d" % k)
+            src, lst = T.Mo[:, 4 * lo:4 * (lo + n)], T.M[:, 256:4352].indirect(T.ML[:, lo // 4:(lo + n) // 4])
+            if MGQ[k] == "v":
+                cp(src, lst, Mk + ["ML"], ["Mo%d" % k], k="g")
+            else:
+                act(src, lst, r=Mk + ["ML"], w=["Mo%d" % k], k="g")
         tag("hashb")
-        act(T.bv[:], ps(5, 64, 128), r=pk(5, 64, 128), w=["bv"])
-        tt(T.bp[:], ps(5, 0, 64), T.bv[:], A.mult, ["bv"] + pk(5, 0, 64), ["bp"])
-        tt(T.bi[:], ps(5, 128, 192), T.bp[:], A.add, ["bp"] + pk(5, 128, 192), ["bi"])
-        ts(T.bi[:], T.bi[:], 2, 127, A.arith_shift_right, A.bitwise_and, w=["bi"])
-        cp(T.BB[:, 0:64], T.bi[:], ["bi"], ["BB0"])
-        for ab in range(1, 4):
-            ts(T.BB[:, 64 * ab:64 * ab + 64], T.bi[:], 128.0 - BOFF[ab], -128.0, A.is_ge, A.mult, r=["bi"], w=["BB%d" % ab])
+        act(T.bv[:], ps(5, 256, 512), r=pk(5, 256, 512), w=["bv"])
+        for k, (lo, n) in enumerate(BCH):
+            sl = slice(lo, lo + n)
+            tt(T.bv[:, sl], ps(5, lo, lo + n), T.bv[:, sl], A.mult, ["bv"] + pk(5, lo, lo + n), ["bp%d" % k])
+            tt(T.bi[:, sl], ps(3, lo, lo + n), T.bv[:, sl], A.add, ["bp%d" % k] + pk(3, lo, lo + n), ["bi%d" % k])
+            ts(T.bi[:, sl], T.bi[:, sl], 2, 127, A.arith_shift_right, A.bitwise_and, w=["bi%d" % k])
+            ts(T.BB[:, sl], T.bi[:, sl], 16.0, None, A.mult, r=["bi%d" % k], w=["BB%d" % j for j in range(lo // 32, (lo + n) // 32)])
         tag("hashw")
-        act(T.fv[:], ps(6, 256, 512), r=pk(6, 256, 512), w=["fv"])
-        tt(T.fv[:], ps(6, 0, 256), T.fv[:], A.mult, pk(6, 0, 256), ["fv"])
-        tt(T.fi[:], ps(7, 0, 256), T.fv[:], A.add, pk(7, 0, 256) + ["fv"], ["fi"])
+        for j in (1, 0, 2):
+            mm(group(ps(6, 256 + 64 * j, 320 + 64 * j), [(T.MB[:, 6 + j, 12 - 4 * q:140 - 4 * q], RF[:, q:256:4]) for q in range(4)]), rf,
+               pk(6, 256 + 64 * j, 320 + 64 * j))
+        act(T.fv[:], ps(6, 320, 384), r=pk(6, 320, 384), w=["fv"])
+        tt(T.fv[:], ps(6, 256, 320), T.fv[:], A.mult, pk(6, 256, 320), ["fv"])
+        tt(T.fi[:], ps(6, 384, 448), T.fv[:], A.add, pk(6, 384, 448) + ["fv"], ["fi"])
         ts(T.fi[:], T.fi[:], 2, 4095, A.arith_shift_right, A.bitwise_and, w=["fi"])
         ts(T.Q[:], T.fi[:], col(SUB), None, A.subtract, r=["fi", "SUB"], w=["Q"])
-        for ab in range(4):
-            tag("fc")
-            b, lo = 4 + ab % 2, 256 + 64 * (ab // 2)
-            pairs = [(I, T.BB[:, 0:64])] + ([(I, T.BB[:, 64 * ab:64 * ab + 64])] if ab else [])
-            pairs += [(T.MB[:, 9, 3 - q:131 - q], T.Mo[:, 4 * ab + q:1024:16]) for q in range(4)]
-            mm(group(ps(b, lo, lo + 64), pairs), ["BB0", "BB%d" % ab, "Mo", "Mo2", "IW"] + MBk, pk(b, lo, lo + 64))
-            ts(T.FL[:, 64 * ab:64 * ab + 64], ps(b, lo, lo + 64), float(BOFF[ab]), None, A.add, r=pk(b, lo, lo + 64), w=["FL%d" % ab])
-            tag("fg")
-            for lo_, n in ([(0, 64)] if ab < 3 else [(0, 32), (32, 32)]):
-                a = 64 * ab + lo_
-                act(T.VG[:, 16 * a:16 * (a + n)], T.Fp[:, 0:2048].indirect(T.FL[:, a:a + n]), r=Fk + ["FL%d" % ab], w=["VG%d" % a], k="g")
+        for k, (lo, n) in enumerate(LCH):
+            tag("fc%d" % k)
+            b, c0, nv = 2 + k % 2, 256 + sum(m for _, m in LCH[k % 2:k:2]), FGV[k]
+            pairs = [(I, T.BB[:, lo:lo + n])] + [(T.MB[:, 9, 12 - 4 * x:140 - 4 * x], T.Mo[:, 4 * lo + x:4 * (lo + n):4]) for x in range(4)]
+            mm(group(ps(b, c0, c0 + n), pairs), ["BB%d" % j for j in range(lo // 32, (lo + n) // 32)] + ["Mo%d" % k, "IW"] + MBk[0], pk(b, c0, c0 + n))
+            cp(T.FL[:, lo:lo + n], ps(b, c0, c0 + n), pk(b, c0, c0 + n), ["FL%d" % k])
+            tag("fg%d" % k)
+            if nv < n:
+                act(T.VG[:, 16 * (lo + nv):16 * (lo + n)], T.F[:, 0:2048].indirect(T.FL[:, lo + nv:lo + n]), AF.Identity, Fk + ["FL%d" % k], ["VG%d" % k], k="g", bias=-128.0)
+            if nv:
+                ts(T.VG[:, 16 * lo:16 * (lo + nv)], T.F[:, 0:2048].indirect(T.FL[:, lo:lo + nv]), -128.0, None, A.add, r=Fk + ["FL%d" % k], w=["VV%d" % k], k="g")
         tag("W")
-        for hf in range(2):
-            mm([(P01[:, 32 * hf:32 * hf + 32, cd, :], ch("b%d" % (4 + cd)), T.Q[:, 128 * hf:128 * hf + 128], True, True) for cd in range(4)],
-               ["Q", "b4", "b5", "b6", "b7"], pk(hf))
-        for k in range(2):
-            mm([(ps(2 + k, 256 * j, 256 * j + 256), ch("b%d" % (2 * k + j)), T.Q[:], True, True) for j in range(2)],
-               ["Q", "b0", "b1", "b2", "b3"], pk(2 + k))
-            if EVAC[k] == "v":
-                cp(T.Wab[:, 512 * k:512 * k + 512], ps(2 + k), pk(2 + k), ["Wab%d" % k])
+        for name, b in (("r1", 2), ("r2", 7), ("rs", 6)):
+            mm([(ps(b, 0, 256), cb(name), RF[:], True, True)], rf[0:2] + [name], pk(b, 0, 256))
+        for j, (out, b) in enumerate(((T.D0[:, 1:1024:4], 2), (T.D0[:, 2:1024:4], 7), (T.D0[:, 3:1024:4], 2), (T.R5[:, 4:1280:5], 6))):
+            if EVAC[j] == "v":
+                cp(out, ps(b, 0, 256), pk(b, 0, 256), ["D0%d" % (j + 1)])
             else:
-                act(T.Wab[:, 512 * k:512 * k + 512], ps(2 + k), r=pk(2 + k), w=["Wab%d" % k])
+                act(out, ps(b, 0, 256), r=pk(b, 0, 256), w=["D0%d" % (j + 1)])
+        wp = lambda cd, lo, hi: (cd // 2, 256 * (cd % 2) + lo, 256 * (cd % 2) + hi)
+        for cd in range(4):
+            mm([(ps(*wp(cd, 0, 256)), cb("w%d" % cd), RF[:], True, True)], rf[0:2] + ["w%d" % cd], pk(*wp(cd, 0, 256)))
         tag("diag")
-        mm(group(ps(7, 256, 272), [(ch("ZA", 15 - k), T.Q[:, k:256:16]) for k in range(16)]), ["Q", "ZA"], pk(7, 256, 272))
-        mm([(ps(6, 0, 256), ch("b8"), T.Q[:], True, True)], ["Q", "b8"], pk(6, 0, 256))
+        mm(group(ps(7, 256, 272), [(ch("ZA", 12 - 4 * a), T.Q[:, a:64:4]) for a in range(4)]), ["Q", "ZA"], pk(7, 256, 272))
+        mm([(T.P6[:, q:256:4], ch("b%d" % q), T.Q[:], True, True) for q in range(4)], ["Q", "b0", "b1", "b2", "b3"], pk(6, 0, 256))
         tag("keys")
         ts(T.AI[:, 0:16], ps(7, 256, 272), 4196352.0, None, A.add, r=pk(7, 256, 272), w=["AI"])
-        ts(T.BI[:], T.AI[:, 0:16], 16, None, A.arith_shift_right, r=["AI"], w=["BI"])
+        ts(T.BI[:], T.AI[:, 0:16], 12, 2032, A.arith_shift_right, A.bitwise_and, r=["AI"], w=["BI"])
         ts(T.AI[:, 16:32], T.AI[:, 0:16], 16383, None, A.bitwise_and, r=["AI"], w=["AL"])
         ts(T.KY[:, 0:16], T.AI[:, 16:32], -8192.0, 0.0, A.add, A.max, r=["AL"], w=["KYc"])
         ts(T.KL[:, 0:16], T.AI[:, 16:32], -8192.0, 0.0, A.add, A.max, r=["AL"], w=["KLc"])
         if EQV:
             ts(T.KS[:, 0:16], T.AI[:, 16:32], -10240.0, None, A.add, r=["AL"], w=["KSc"])
-            cp(T.KR[:, 0:256], ps(6, 0, 256), pk(6, 0, 256), ["KR0"])
+            act(T.KR[:, 0:256], ps(6, 0, 256), r=pk(6, 0, 256), w=["KR0"])
         if EQV < 8:
             ts(T.KN[:], T.AI[:, 16:32], -1.0, 10240.0, A.mult, A.add, r=["AL"], w=["KSn"])
         ts(T.dd[:], T.AI[:, 16:32], 8192.0, -8192.0, A.is_lt, A.mult, r=["AL"], w=["dd"])
-        cp(T.BL[:], T.BI[:], ["BI"], ["BL"])
+        cp(T.UL[:, 0:16], T.BI[:], ["BI"], ["UL0"])
+        for k in range(4):
+            n = 16 << k
+            ts(T.UL[:, n:2 * n], T.UL[:, 0:n], float(1 << k), None, A.add, r=["UL%d" % j for j in range(k + 1)], w=["UL%d" % (k + 1)], k=0.5)
         act(T.Ms[:], T.M[:, 256:4352].indirect(T.KL[:, 0:16]), r=Mk + ["KLc"], w=["Ms"], k="g")
-        for ab in range(4):
-            tag("mul")
-            VW = T["VW%d" % ab]
-            b, c0 = 2 + ab % 2, 256 * (ab // 2)
-            reg, ks = ps(b, c0, c0 + 256), pk(b, c0, c0 + 256)
-            for lo, n in ([(0, 64)] if ab < 3 else [(0, 32), (32, 32)]):
-                wk = ["VW%d_%d" % (ab, k) for k in range(lo // 32, (lo + n) // 32)]
-                tt(VW[:, lo:lo + n], T.VG[:, 1024 * ab + 16 * lo:1024 * ab + 16 * (lo + n)], P01[:, lo:lo + n], A.mult,
-                   ["VG%d" % (64 * ab + lo)] + [k_ for k in range(lo // 32, (lo + n) // 32) for k_ in pk(k)], wk)
-                mm(group(ps(b, c0 + 4 * lo, c0 + 4 * (lo + n)), [(ch("Ih"), VW[:, lo:lo + n, cd, :]) for cd in range(4)]),
-                   wk + ["Ih"], pk(b, c0 + 4 * lo, c0 + 4 * (lo + n)))
-            tag("sum")
-            w_, sk = T.Wab[:, 256 * ab:256 * ab + 256], ["Wab%d" % (ab // 2)]
-            if ab == 0:
-                tt(T.acc[:], reg, w_, A.mult, ks + sk, ["acc"])
-            else:
-                tt(reg, reg, w_, A.mult, sk, ks)
-                tt(T.acc[:], reg, T.acc[:], A.add, ks, ["acc"])
         yb = T["yb%d" % r]
-        ts(T.y16[:], T.acc[:], 1152.0 - 255.0 / 512, None, A.add, r=["acc"], w=["y16"])
-        ts(yb[:], T.y16[:], -1152.0, None, A.add, r=["y16"], w=["yb%d" % r], k=0.5)
-        send("y", r, lambda o: yb[:, CAP * o:CAP * o + CAP], T.RY[:, S * me:S * me + CAP], ["yb%d" % r], [], "RYr")
-        act(T.RY[:, S * me:S * me + CAP], yb[:, CAP * me:CAP * me + CAP], r=["yb%d" % r] + RYz, w=["RY"])
+        yk = ["yb%d_%d" % (r, o) for o in range(N)]
+        for k, (lo, n) in enumerate(LCH):
+            tag("mul%d" % k)
+            for cd in range(4):
+                scan(T.VL[:, 1024 * cd + 4 * lo:1024 * cd + 4 * (lo + n)], T.D0[:, 4 * lo:4 * (lo + n)], T.VG[:, 16 * lo + cd:16 * (lo + n):4], 0.0,
+                     A.mult, A.add, ["VG%d" % k, "VV%d" % k, "D0z", "D01", "D02", "D03"],
+                     ["VL%d_%d" % (o, cd) for o in range(lo // 32, (lo + n) // 32)], k=0.5)
+        for k, part in enumerate(YP):
+            tag("sum%d" % k)
+            lo, hi = 32 * part[0], 32 * part[-1] + 32
+            for cd in range(4):
+                tt(T.PD[:, 5 * lo + cd:5 * hi:5], T.VL[:, 1024 * cd + 4 * lo + 3:1024 * cd + 4 * hi:4], ps(*wp(cd, lo, hi)), A.mult,
+                   ["VL%d_%d" % (o, cd) for o in part] + pk(*wp(cd, lo, hi)), ["PD%d_%d" % (k, cd)])
+            scan(T.Y5[:, 5 * lo:5 * hi], T.R5[:, 5 * lo:5 * hi], T.PD[:, 5 * lo:5 * hi], 0.0, A.mult, A.add,
+                 ["PD%d_%d" % (k, cd) for cd in range(4)] + ["PDk", "R5", "D04"], ["Y5%d" % k])
+            ts(yb[:, lo:hi], T.Y5[:, 5 * lo + 4:5 * hi:5], -1152.0, None, A.add, r=["Y5%d" % k], w=[yk[o] for o in part], k=0.5)
+        tag("ys")
+        for k, part in enumerate(YP):
+            send("y", r, lambda o: yb[:, CAP * o:CAP * o + CAP], T.RY[:, CAP * me:CAP * me + CAP], [yk[o] for o in part], [], "RYr%d" % k, YP, k)
+        act(T.RY[:, CAP * me:CAP * me + CAP], yb[:, CAP * me:CAP * me + CAP], r=yk, w=["RY"])
 
     def losers(r, k):
         tag("eq%d" % k)
@@ -622,7 +719,11 @@ def rank_program(g, core, T, topo):
         items = [(ps(b, o, o + 256), cb("pen"), T["RF%d" % r][:], True, False)]
         items += [(ps(b, o + 16 * (c + 1), o + end(c)), cb("big"), EQ[:, c, 16:end(c) - 16 * c], False, False) for c in range(16) if c % 8 < 7]
         items += [(ps(b, o, o + 256), cb("pow"), EQ[:, :, 0:16], False, True)]
-        mm(items, ["EQ%d_%d" % (k, c) for c in range(16)] + ["pen", "big", "pow", "RF%d" % r, "RFr%d" % r], pk(b, o, o + 256))
+        eq = ["EQ%d_%d" % (k, c) for c in range(16)]
+        mm(items[0:5], eq[0:4] + ["pen", "big", "RF%d" % r, "RFr%d" % r], pk(b))
+        mm(items[5:8], eq[4:8], pk(b), acc=True)
+        mm(items[8:12], eq[8:12], pk(b), acc=True)
+        mm(items[12:], eq + ["pow"], pk(b), acc=True)
         act(T.LS[:, 256 * k:256 * k + 256], ps(b, o, o + 256), AF.Identity, pk(b, o, o + 256), ["LS%d" % k], bias=131072.0)
 
     def put(win, k, src, r, w):
@@ -633,22 +734,21 @@ def rank_program(g, core, T, topo):
         last = r == RO - 1
         tag("g")
         yb, RT = T["yb%d" % r], T["RT%d" % r]
-        mm(group(ps(7, 288, 304), [(cb("Z3" if last else "Zm", 15 - k), T.Ms[:, k:256:16]) for k in range(16)]), ["Ms", "Zm", "Z3"], pk(7, 288, 304))
-        mm(group(ps(2, 256, 512), [(I, RT[:]), (cb("In"), yb[:])]), ["yb%d" % r, "RT%d" % r, "RTr%d" % r, "In", "IW"], pk(2, 256, 512))
-        for k in range(2):
-            act(ps(0, 256 * k, 256 * k + 256), ps(2, 256, 512), AF.Sign, pk(2, 256, 512), pk(0, 256 * k, 256 * k + 256))
+        mm(group(ps(7, 288, 304), [(cb("Z3", 15 - k), T.Ms[:, k:256:16]) for k in range(16)]), ["Ms", "Z3"], pk(7, 288, 304))
+        mm(group(ps(2, 256, 512), [(I, RT[:]), (cb("In"), yb[:])]), ["yb%d_%d" % (r, o) for o in range(N)] + ["RT%d" % r, "RTr%d" % r, "In", "IW"], pk(2, 256, 512))
+        ts(T.GS[:], ps(2, 256, 512), 0.5, -0.5, A.min, A.max, r=pk(2, 256, 512), w=["GS"])
         tag("ug")
-        for j in range(16):
-            act(T.UG[:, 256 * j:256 * j + 256], T.Fp[:, 128 * j:128 * j + 128].indirect(T.BL[:]), AF.Identity, Fk + ["BL"], ["UG%d" % j], k="g", bias=128.0)
+        for a, n in UGS:
+            ul = ["UL%d" % k for k in range(5) if 8 << k < 16 * (a + n)]
+            act(T.UG[:, 256 * a:256 * (a + n)], T.F[:, 0:2048].indirect(T.UL[:, 16 * a:16 * (a + n)]), AF.Identity, Fk + ul,
+                ["UG%d" % j for j in range(a, a + n)], k="g", bias=256.0)
         tag("fk")
-        if last:
-            ts(T.BI[:], T.BI[:], 16.0, None, A.mult, w=["BI"])
         tt(T.KY[:, 16:32], ps(7, 288, 304), T.BI[:], A.add, pk(7, 288, 304) + ["BI"], ["KYf"])
         cp(T.KL[:, 16:32], T.KY[:, 16:32], ["KYf"], ["KLf"])
         tt(T.KS[:, 16:32], T.KY[:, 16:32], T.dd[:], A.add, ["KYf", "dd"], ["KSf"])
-        cp(T.KR[:, 256:512], T.IOTA[:].indirect(T.KL[:, 16:32]), ["KLf"] + ["IOTA%d" % k for k in range(4)], ["KR1"], k="g")
+        act(T.KR[:, 256:512], T.IOTA[:].indirect(T.KL[:, 16:32]), r=["KLf"] + ["IOTA%d" % k for k in range(4)], w=["KR1"], k="g")
         act(T.Co[:], T.C[:, 0:4096].indirect(T.KL[:, 0:16]), r=Ck + ["KLc"], w=["Co"], k="g")
-        act(T.Fo[:], (T.Fr if last else T.Fp)[:, 0:2048].indirect(T.KL[:, 16:32]), r=(Nk if last else Fk) + ["KLf"], w=["Fo"], k="g")
+        act(T.Fo[:], T.F[:, 0:2048].indirect(T.KL[:, 16:32]), r=Fk + ["KLf"], w=["Fo"], k="g")
         losers(r, 0)
         losers(r, 1)
         tag("win")
@@ -658,15 +758,20 @@ def rank_program(g, core, T, topo):
         tt(T.bad[:], T.bad[:], T.KY[:], A.max, ["KYc", "KYf"], ["bad"])
         cp(T.OL[:], T.bad[:], ["bad"], ["OL"])
         tag("prod")
-        for j in range(8):
-            tt(T.PR[:, 512 * j:512 * j + 512], T.UG[:, 512 * j:512 * j + 512], ps(0), A.mult,
-               ["UG%d" % (2 * j), "UG%d" % (2 * j + 1)] + pk(0), ["PR%d" % j])
-            mm([(ps(1, 0, 256), cb("Z2", 15 - jj), T.PR[:, 256 * jj:256 * jj + 256], jj == 0, jj == 15) for jj in (2 * j, 2 * j + 1)],
-               ["PR%d" % j, "Z2"], pk(1) if j == 0 else (["usum"] if j == 7 else []), ["#1grp"])
+        mm([(ps(1, 0, 256), T.n256[:], T.GS[:], True, False)], ["GS", "n256"], pk(1), ["#1grp"])
+        for j in range(16):
+            if j >= 16 - UGV:
+                op("v", lambda j=j: V.tensor_tensor(T.PR[:, 256 * j:256 * j + 256], T.F[:, 0:2048].indirect(T.UL[:, 16 * j:16 * j + 16]), T.GS[:], A.mult),
+                   Fk + ["UL%d" % k for k in range(5)] + ["GS"], ["PR%d" % j], cost(256, "g"))
+                continue
+            scan(T.PR[:, 256 * j:256 * j + 256], T.UG[:, 256 * j:256 * j + 256], T.GS[:], 0.0, A.max, A.mult, ["UG%d" % j, "GS"], ["PR%d" % j], k=0.5)
+        for j in PRO:
+            mm([(ps(1, 0, 256), ch("Zh", 15 - j), T.PR[:, 256 * j:256 * j + 256], False, j == PRO[-1])],
+               ["PR%d" % j, "Zh"], ["usum"] if j == PRO[-1] else [], ["#1grp"])
         tag("wf")
-        tt(T.Fn[:], ps(0, 0, 256), T.Fo[:], A.add, pk(0, 0, 256) + ["Fo"], ["Fn"])
-        ts(T.Fn[:], T.Fn[:], 255.0 if last else 127.0, 0.0 if last else -128.0, A.min, A.max, w=["Fn"], k=0.5)
-        put(T.Fr[:] if last else T.Fp[:], 1, T.Fn, ["Fn"], Nk if last else Fk)
+        mm(group(ps(5, 256, 512), [(I, T.Fo[:]), (cb("I2"), T.GS[:])]), ["Fo", "GS", "I2", "IW"], pk(5, 256, 512))
+        ts(T.Fn[:], ps(5, 256, 512), 255.0, 0.0, A.min, A.max, r=pk(5, 256, 512), w=["Fn"])
+        put(T.F[:], 1, T.Fn, ["Fn"], Fk)
         tag("nc")
         act(ps(1, 256, 512), ps(1, 0, 256), AF.Sign, pk(1, 0, 256) + ["usum"], pk(1, 256, 512))
         tt(T.Cn[:], ps(1, 256, 512), T.Co[:], A.add, pk(1, 256, 512) + ["Co"], ["Cn"])
@@ -686,7 +791,7 @@ def rank_program(g, core, T, topo):
         tag("wc")
         put(T.C[:], 0, T.Cn, ["Cn"], Ck)
 
-    YCk = ["YC%d" % k for k in range(8)]
+    YCk = ["YC"]
     home_route(0)
     for r in range(RO):
         now[0] = r
@@ -696,39 +801,36 @@ def rank_program(g, core, T, topo):
         if r < RO - 1:
             home_route(r + 1)
         if r == RO - 2:
-            tag("fn")
-            for m in range(16):
-                act(T.Fr[:, m:2048:16], T.Fp[:, 128 * m:128 * m + 128], AF.Identity, Fk, [Nk[m]], bias=128.0)
             tag("yc")
-            for k in range(8):
-                b = 2 + k % 2
-                mm([(ps(b), cb("ycw"), T.C[:, 512 * k:512 * k + 512], True, True)], Ck + ["ycw"], pk(b))
-                act(T.YC[:, 512 * k:512 * k + 512], ps(b), r=pk(b), w=[YCk[k]])
+            for k in range(4):
+                mm([(ps(1, 0, 256), cb("Zy", 15 - j), T.C[:, 256 * j:256 * j + 256], j == 0, j == 15) for j in range(4 * k, 4 * k + 4)],
+                   Ck + ["Zy"], pk(1), acc=k > 0)
+            act(T.YK[:], ps(1, 0, 256), r=pk(1), w=["YK"])
+            dma("y", T.YC[0:128:16, 0:4096], T.YK[:], "dyc", r=["YK"], w=YCk)
     tag("end")
     mm([(ps(6, 0, 256), cb("ycw"), T.Cn[:], True, True)], ["Cn", "ycw"], pk(6, 0, 256))
     act(T.ycn[:], ps(6, 0, 256), r=pk(6, 0, 256), w=["ycn"])
     put(T.YC[:], 0, T.ycn, ["ycn"], YCk)
     dma("y", T.yc[:], T.YC[0:128:16, 0:4096], "out", r=YCk, lat=2.6)
-    dma("y", T.yf[:], T.Fr[:, 0:2048], "out", r=Nk, lat=4.0)
-    cp(T.xO[:], T.X[:], Xk, ["xO"])
-    mm(group(ps(3, 0, S), [(cb("I64"), T.sg[:, k, :]) for k in range(RO)] + [(I, T.yg[:, k, :]) for k in range(RO)]),
-       ["sg%d" % k for k in range(RO)] + ["yg%d" % k for k in range(RO)] + ["I64", "IW"], pk(3, 0, S))
-    act(T.ysO[:], ps(3, 0, S), AF.Identity, pk(3, 0, S), ["ysO"], bias=192.0)
+    dma("y", T.yf[:], T.F[:, 0:2048], "out", r=Fk, lat=3.2)
+    act(T.xO[:], ps(3, 0, S), AF.Identity, pk(3) + ["KX"], ["xO"], bias=col(KX))
+    mm(group(ps(4, 0, S), [(cb("I64"), T.sg[:, k, :]) for k in range(RO)] + [(I, T.yg[:, k, :]) for k in range(RO)]),
+       ["sg%d" % k for k in range(RO)] + ["yg%d" % k for k in range(RO)] + ["I64", "IW"], pk(4, 0, S))
+    act(T.ysO[:], ps(4, 0, S), AF.Identity, pk(4, 0, S), ["ysO"], bias=192.0)
     for e in range(4):
-        dma("ys"[e % 2], T.yx[e:32:4, :], T.xO[e:128:16, :], "out", r=["xO"])
+        dma("ys"[e % 2], T.yx[e:32:4, :], T.xO[4 * e:128:16, :], "out", r=["xO"])
     dma("s", T.ys[:], T.ysO[:], "out", r=["ysO"])
     if not ORDER:
         rng = np.random.default_rng(1)
         names = sorted({e["tag"] + e["q"] for e in ops})
-        best, bias = schedule({}), {}
+        net = graph()
+        best = schedule(net, [-v for v in net[2]])
         for _ in range(TRIES):
-            other = dict(bias)
-            for k in rng.integers(0, len(names), int(rng.integers(1, 4))):
-                other[names[k]] = other.get(names[k], 0.0) + 3.0 * float(rng.standard_normal())
-            got = schedule(other)
+            move = {names[k]: 2.0 * float(rng.standard_normal()) for k in rng.integers(0, len(names), int(rng.integers(1, 6)))}
+            got = schedule(net, [t + move.get(e["tag"] + e["q"], 0.0) for t, e in zip(best[1], ops)])
             if got[0] <= best[0]:
-                best, bias = got, other
-        ORDER.extend(best)
+                best = got
+        ORDER.extend([best[0], sorted(range(len(ops)), key=lambda i: (best[1][i], i))])
     for i in ORDER[1]:
         emit(ops[i])
     for sem, val in total.items():

@@ -9,16 +9,17 @@ OFF = (0, 61, 173, 234)
 BOFF = (0, 89, 91, 52)
 NP = 12
 TAG = [""]
-CY, GA, SCA, FIX, WAKE, SENT, ROW, LAND, TF, FIRST = 0.9e-3, 1.56, 3.8, 0.02, 0.1, 1.0, 0.022, 0.6, 1.1, 2.0
+CY, GA, SCA, FIX, WAKE, SENT, ROW, LAND, TF, FIRST = 0.87e-3, 1.56, 3.8, 0.005, 0.13, 1.1, 0.018, 0.6, 1.0, 2.0
 SPLIT = 4
 YP = [(0, 1, 2, 3), (4, 5), (6, 7)]
-EVAC, MZG, MGQ, EQV, MBS, VECQ, VECH = "ssss", 2, "vssss", 8, 4, "gss", "sv"
+EVAC, MZG, MGQ, EQV, MBS, VECQ, VECH = "ssss", 2, "vssss", 8, 4, "s", "vs"
 LCH = [(0, 64), (64, 64), (128, 64), (192, 32), (224, 32)]
 BCH = [(0, 64), (64, 192)]
 FGV, UGV, CLF = (0, 0, 0, 0, 0), 0, 1
 UGS = [(0, 2), (2, 2), (4, 4), (8, 4), (12, 2), (14, 2)]
 PRO = list(range(16))
-TRIES, ORDER = 4000, []
+GQ, PEN, WRS, FQ, MZQ = "vvss", 0, 0, "ssssss", "gggs"
+TRIES, EARLY, BOTH, MOVES, ONES, HEAT, ORDER = 7000, 0.2, 2, 5, 10, 0.05, []
 SW = 1824
 bf, f32, i32, u16, f16 = "bfloat16", "float32", "int32", "uint16", "float16"
 CB = ["Z2", "Z3", "Zy", "dC", "dF", "dN", "xC", "xF", "xN", "pow", "big", "pen", "ycw", "I64", "In", "I2",
@@ -47,7 +48,7 @@ SB = {
     "VL": ([128, 4096], f16), "D0": ([128, 1024], bf), "PD": ([128, 1280], f32), "R5": ([128, 1280], bf), "Y5": ([128, 1280], f16),
     "KS": ([128, 32], f32), "KY": ([128, 32], f32), "KL": ([128, 32], u16), "BI": ([128, 16], i32), "AI": ([128, 32], i32), "y16": ([128, 256], f16), "UL": ([128, 256], u16), "dd": ([128, 16], f32), "KN": ([128, 16], f32), "GM": ([128, 8], f32),
     "KR": ([128, 512], f16), "EQ0": ([128, 16, 128], bf), "EQ1": ([128, 16, 128], bf), "LS": ([128, 512], bf),
-    "bad": ([128, 32], f32), "OL": ([128, 32], u16),
+    "bad": ([128, 32], f32), "KD": ([128, 32], f32), "tneg": ([128, 32], f32), "OL": ([128, 32], u16),
     "Ms": ([128, 256], bf), "Co": ([128, 256], bf), "Fo": ([128, 256], bf), "Cn": ([128, 256], bf), "Fn": ([128, 256], bf),
     "UG": ([128, 4096], f16), "PR": ([128, 4096], f16), "TR": ([128, 256], bf), "TB": ([128, 256], bf), "Mn": ([128, 256], bf),
     "sn": ([128, 256], f32), "e16": ([128, 16], i32), "ycn": ([128, 256], f32),
@@ -188,7 +189,7 @@ def rank_program(g, core, T, topo):
         for b in x:
             bank.setdefault(b, {})[q] = ev
 
-    ops = []
+    ops, brief, marks = [], [], []
 
     def size(ap):
         n = 1
@@ -207,15 +208,24 @@ def rank_program(g, core, T, topo):
         x = sorted({int(k[1]) for k in list(r) + list(w) + list(o) if k[0] == "#"})
         ops.append(dict(q=q, fn=fn, r=list(r), w=list(w), x=x, o=list(o), c=c, lat=lat, kind=kind, extra=extra, tag=TAG[0]))
 
-    def dma(q, out, in_, sem, r=(), w=(), lat=2.2):
-        op(q, lambda: Qs[q].dma_start(out, in_), r, w, 0.1, (), lat, "d", sem)
+    def dma(q, out, in_, sem, r=(), w=(), lat=2.2, o=()):
+        op(q, lambda: Qs[q].dma_start(out, in_), r, w, 0.06, o, lat, "d", sem)
+
+    def fill(q, out, v, w):
+        n = size(out)
+        if q == "v":
+            ms(out, v, w=w)
+        elif q == "s":
+            act(out, T.ones[:, 0:n], r=["ones"], w=w, scale=v)
+        else:
+            op("g", lambda: g.iota(out, [[0, n]], int(v), 0, allow_small_or_imprecise_dtypes=True), [], w, 0.2 + 2 * n * CY)
 
     def mm(items, r, w, o=(), acc=False):
         def fn():
             for it in items:
                 i = P.matmul(*it)
             return i
-        op("t", fn, r, w, sum(0.005 + max(64, size(it[2])) * CY * TF for it in items), o, 0.02, extra=acc)
+        op("t", fn, r, w, sum(0.012 + max(64, size(it[2])) * CY * TF for it in items), o, 0.0, extra=acc)
 
     def group(out, pairs, start=True, stop=True):
         return [(out, l, rr, start and k == 0, stop and k == len(pairs) - 1) for k, (l, rr) in enumerate(pairs)]
@@ -241,6 +251,12 @@ def rank_program(g, core, T, topo):
 
     def act(out, a, fn=AF.Copy, r=(), w=(), k=1, **kw):
         op("s", lambda: Sc.activation(out, a, fn, **kw), r, w, cost(size(out), k))
+
+    def pick(q, out, a, r, w):
+        if q == "v":
+            cp(out, a, r, w, k="g")
+        else:
+            act(out, a, r=r, w=w, k="g")
 
     def send(kind, rnd, src, dst, r, w, landed, parts=None, part=None):
         plans = {c: plan(topo, cores, c, parts) for c in cores}
@@ -318,14 +334,16 @@ def rank_program(g, core, T, topo):
     def place(turn, before, back):
         start = [0.0] * len(ops)
         busy = {q: ([], []) for q in Qs}
-        held = [[] for _ in range(8)]
+        held = [{} for _ in range(8)]
+        stop = [0.0] * len(ops)
         end = 0.0
         for i in turn:
-            e = ops[i]
-            c, q, hold = e["c"], e["q"], e["lat"] + WAKE
-            t = e["lat"] if back else 0.0
+            c, q, lat, x = brief[i]
+            hold = lat + WAKE
+            t = lat if back else 0.0
             for j, d in before[i]:
-                t = max(t, start[j] + ops[j]["c"] + d)
+                if stop[j] + d > t:
+                    t = stop[j] + d
             a, b = busy[q]
             while True:
                 lo, hi = 0, len(b)
@@ -338,33 +356,42 @@ def rank_program(g, core, T, topo):
                 while lo < len(a) and a[lo] < t + c:
                     t = b[lo]
                     lo += 1
+                if not x:
+                    break
                 t0 = t
                 x0, x1 = (t - hold, t + c) if back else (t, t + c + hold)
-                for k in e["x"]:
-                    for y0, y1, q2 in held[k]:
-                        if q2 != q and y0 < x1 and x0 < y1:
-                            t = max(t, y1 + (hold if back else 0.0))
+                for k in x:
+                    for u in range(int(x0), int(x1) + 1):
+                        for y0, y1, q2 in held[k].get(u, ()):
+                            if q2 != q and y0 < x1 and x0 < y1:
+                                t = max(t, y1 + (hold if back else 0.0))
                 if t == t0:
                     break
             a.insert(lo, t)
             b.insert(lo, t + c)
-            for k in e["x"]:
-                held[k].append((x0, x1, q))
-            start[i] = t
-            end = max(end, t + c + (0.0 if back else e["lat"]))
+            for k in x:
+                for u in range(int(x0), int(x1) + 1):
+                    held[k].setdefault(u, []).append((x0, x1, q))
+            start[i], stop[i] = t, t + c
+            end = max(end, t + c + (0.0 if back else lat))
         return end, start
 
-    def schedule(net, key):
+    def schedule(net, key, both):
         pre, post = net[0], net[1]
         n = len(ops)
-        key = list(key)
         for i in range(n):
+            k = key[i]
             for j, d in pre[i]:
-                key[i] = max(key[i], key[j] + 1e-6)
-        end, start = place(sorted(range(n), key=lambda i: key[i]), pre, False)
-        late = place(sorted(range(n), key=lambda i: (-start[i] - ops[i]["c"], -i)), post, True)[1]
-        again = place(sorted(range(n), key=lambda i: (-late[i] - ops[i]["c"], i)), pre, False)
-        return again if again[0] <= end else (end, start)
+                if key[j] >= k:
+                    k = key[j] + 1e-6
+            key[i] = k
+        rate = lambda got: (got[0] + EARLY * sum(got[1][i] for i in marks) / len(marks), got[1], got[0])
+        got = rate(place(sorted(range(n), key=lambda i: key[i]), pre, False))
+        if both:
+            late = place(sorted(range(n), key=lambda i: (-got[1][i] - ops[i]["c"], -i)), post, True)[1]
+            again = rate(place(sorted(range(n), key=lambda i: (-late[i] - ops[i]["c"], i)), pre, False))
+            got = min(got, again, key=lambda v: v[0])
+        return got
 
     cb = lambda n, a=0: T.cb[:, CB.index(n), a:a + 128]
     ch = lambda n, a=0: T.ch[:, CH.index(n), a:a + 128]
@@ -387,12 +414,12 @@ def rank_program(g, core, T, topo):
     tag("c0")
     ms(T.X[:], 0, w=["X0"])
     ms(T.ones[:], 1.0, w=["ones"])
-    for k in range(4):
-        dma("y", T.C[:, 1024 * k:1024 * k + 1024], T.cf[:, 1024 * k:1024 * k + 1024], "dc%d" % k, w=["C%d" % k], lat=2.9 + k)
     for e in range(4):
-        dma("ys"[e // 2], T.X[(0, 4, 10, 14)[e]:128:16, :], T.x0[e:32:4, :], "dx", r=["X0"], w=["X%d" % (e + 1)])
-    dma("s", T.tgr[:], T.tg[:], "dtg", w=["tgr"])
-    dma("y", T.F[:, 0:2048], T.ft[:], "df", r=["C3"], w=["F"], lat=3.5)
+        dma("ys"[e // 2], T.X[(0, 4, 10, 14)[e]:128:16, :], T.x0[e:32:4, :], "dx", r=["X0"], w=["X%d" % (e + 1)], o=["load"], lat=1.8)
+    for k in range(4):
+        dma("y", T.C[:, 1024 * k:1024 * k + 1024], T.cf[:, 1024 * k:1024 * k + 1024], "dc%d" % k, w=["C%d" % k], lat=2.6 + k, o=["load"])
+    dma("y", T.tgr[:], T.tg[:], "dtg", w=["tgr"], o=["load"], lat=6.0)
+    dma("y", T.F[:, 0:2048], T.ft[:], "df", r=["SF0"], w=["F"], lat=3.5)
     op("g", lambda: g.affine_select(T.IW[:], T.ones[:, 0:144], [[-1, 144]], A.is_equal, 0.0, 8, 1), ["ones"], ["IW"], 0.45)
     op("g", lambda: g.iota(T.PI[:], [[256, 6], [1, 32]], 256, 0, allow_small_or_imprecise_dtypes=True), [], ["PI"], 0.5)
     op("g", lambda: g.iota(T.pc[:, 0:1], [[0, 1]], 0, 1), [], ["pc"], 0.14)
@@ -406,7 +433,6 @@ def rank_program(g, core, T, topo):
     for k in range(4):
         op("g", lambda k=k: g.iota(T.IOTA[:, 512 * k:512 * k + 512], [[1, 512]], 512 * k, 0, allow_small_or_imprecise_dtypes=True), [], ["IOTA%d" % k], 1.1)
     ms(T.VEC[:], 0.0, w=["VEC"])
-    ms(T.Z[:], 0.0, w=["Z"])
     ms(T.comb[:], 0.0, w=["comb"])
     ms(T.RST[:], 0.0625, w=["RST"])
     ms(T.cb[:, 0:3, :], 0.0, w=["cbz"])
@@ -478,10 +504,10 @@ def rank_program(g, core, T, topo):
     ts(cb("dN"), T.BD[:], RM(12), -256.0, A.mult, A.mult, r=["BD", "RM"], w=["dN"], k=0.5)
     ts(ch("cnt"), T.BD[:], col(GE8), None, A.mult, r=["BD", "GE8"], w=["cnt"], k=0.5)
     cp(T.ch[:, 2, 15:128:16], b15, ["BD", "chz"], ["Zh"])
-    ms(T.TB[:], 0.0, w=["TB"])
-    ms(T.D0[:, 0:1024:4], 0.0, w=["D0z"])
-    ms(T.R5[:], 1.0, w=["R5", "D04"])
-    ms(T.R5[:, 0:1280:5], 0.0, w=["R5"])
+    fill(FQ[0], T.TB[:], 0.0, ["TB"])
+    fill(FQ[1], T.D0[:, 0:1024:4], 0.0, ["D0z"])
+    for k in range(4):
+        fill(FQ[2], T.R5[:, k:1280:5], min(k, 1.0), ["R5%d" % k])
     ts(col(O16), col(RC), 12.0, 1.0 / 16, A.is_ge, A.mult, r=["RC"], w=["O16"])
     ts(col(CR1), RM(3), 2.0, col(O16), A.mult, A.add, r=["RM", "O16"], w=["CR1"])
     ts(col(CR2), RM(3), -4.0, col(O16), A.mult, A.add, r=["RM", "O16"], w=["CR2"])
@@ -491,7 +517,7 @@ def rank_program(g, core, T, topo):
     ts(cb("rs"), T.BD[:], col(CRS), 1.0 / 256, A.mult, A.mult, r=["BD", "CRS"], w=["rs"], k=0.5)
     for name, sc, key in [("r1", col(CR1), "CR1"), ("r2", col(CR2), "CR2")] + [("w%d" % k, RM(12 + k), "RM") for k in range(4)]:
         act(cb(name), T.BD[:], r=["BD", key], w=[name], scale=sc)
-    ms(T.PD[:, 4:1280:5], 1152.0 - 255.0 / 512, w=["PDk"])
+    fill(FQ[3], T.PD[:, 4:1280:5], 1152.0 - 255.0 / 512, ["PDk"])
     scan(T.pw[:], T.two[:], T.RM[:], 0.0, A.mult, A.add, ["two", "RM"], ["pw"])
     ts(T.R4[:], T.J[:, 0:4], col(I4), None, A.is_equal, r=["J", "I4"], w=["R4"])
     ts(col(ZAC), T.R4[:, 2:3], 8192.0, T.R4[:, 0:1], A.mult, A.add, r=["R4"], w=["ZAC"])
@@ -499,6 +525,7 @@ def rank_program(g, core, T, topo):
     ts(col(SUB), col(I4), 2.0, 2048.0, A.is_lt, A.mult, r=["I4"], w=["SUB"])
     ts(col(R1), col(RC), 1.0, None, A.add, r=["RC"], w=["R1"])
     ts(T.trash[:], T.trash[:], col(RC), None, A.add, r=["RC"], w=["trash"])
+    ts(T.tneg[:], T.trash[:], -1.0 / 8192, None, A.mult, r=["trash"], w=["tneg"])
     ts(col(THR), T.pw[:, 15:16], 2.5, None, A.mult, r=["pw"], w=["THR"])
     act(T.tgc[:], T.tgr[:], AF.Identity, ["tgr"], ["tgc"], bias=-128.0)
     mm([(ps(6, 128, 256), cb("xC"), I, True, True)], ["xC", "IW"], pk(6, 128, 256))
@@ -510,21 +537,21 @@ def rank_program(g, core, T, topo):
     for name, sc, key in (("pen", col(PN), "PN"), ("dC", RM(3), "RM"), ("pow", T.pw[:, 15:16], "pw"), ("big", 65536.0, "BD"), ("ycw", col(R1), "R1")):
         act(cb(name), T.BD[:], r=["BD", key], w=[name], scale=sc)
     act(T.n256[:], T.BD[:], r=["BD"], w=["n256"], scale=-256.0)
+    for j in range(16 - UGV, 16):
+        ms(T.n256[:, j:128:16], 0.0, w=["n256"])
     for name, sc in (("I64", 64.0), ("In", -1.0), ("I2", 2.0)):
         act(cb(name), I, r=["IW"], w=[name], scale=sc)
+    tag("z")
     for r in range(RO):
-        act(T["SF%d" % r][:, 0:256], T.Z[:, 0:256], r=["Z"], w=["SF%d" % r])
-    act(T.ST[:, 0:256], T.Z[:, 0:256], r=["Z"], w=["ST"])
-    RYz = ["RYz%d" % k for k in range(4)]
-    for k in range(4):
-        act(T.RY[:, 256 + 392 * k:648 + 392 * k], T.Z[:, 0:392], r=["Z"], w=[RYz[k]])
-    Mz = ["Mz%d" % k for k in range(8)]
-    for k in range(8):
-        part = T.M[:, 256 + 512 * k:768 + 512 * k]
-        if k < MZG:
-            op("g", lambda part=part: g.iota(part, [[0, 512]], 0, 0, allow_small_or_imprecise_dtypes=True), [], [Mz[k]], 1.1)
-        else:
-            ms(part, 0.0, w=[Mz[k]])
+        fill(FQ[4], T["SF%d" % r][:, 0:256], 0.0, ["SF%d" % r])
+    fill(FQ[4], T.ST[:, 0:256], 0.0, ["ST"])
+    RYz = ["RYz%d" % k for k in range(7)]
+    for k in range(7):
+        fill(FQ[5], T.RY[:, 256 + 224 * k:480 + 224 * k], 0.0, [RYz[k]])
+    tag("mz")
+    Mz = ["Mz%d" % k for k in range(16)]
+    for k in range(16):
+        fill(MZQ[k % len(MZQ)], T.M[:, 256 + 256 * k:512 + 256 * k], 0.0, [Mz[k]])
     Fk = ["F"]
 
     tag("am")
@@ -616,11 +643,7 @@ def rank_program(g, core, T, topo):
         cp(T.ML[:], T.hi[:], ["hi"], ["ML"])
         for k, (lo, n) in enumerate(LCH):
             tag("mo%d" % k)
-            src, lst = T.Mo[:, 4 * lo:4 * (lo + n)], T.M[:, 256:4352].indirect(T.ML[:, lo // 4:(lo + n) // 4])
-            if MGQ[k] == "v":
-                cp(src, lst, Mk + ["ML"], ["Mo%d" % k], k="g")
-            else:
-                act(src, lst, r=Mk + ["ML"], w=["Mo%d" % k], k="g")
+            pick(MGQ[k], T.Mo[:, 4 * lo:4 * (lo + n)], T.M[:, 256:4352].indirect(T.ML[:, lo // 4:(lo + n) // 4]), Mk + ["ML"], ["Mo%d" % k])
         tag("hashb")
         act(T.bv[:], ps(5, 256, 512), r=pk(5, 256, 512), w=["bv"])
         for k, (lo, n) in enumerate(BCH):
@@ -679,7 +702,8 @@ def rank_program(g, core, T, topo):
         for k in range(4):
             n = 16 << k
             ts(T.UL[:, n:2 * n], T.UL[:, 0:n], float(1 << k), None, A.add, r=["UL%d" % j for j in range(k + 1)], w=["UL%d" % (k + 1)], k=0.5)
-        act(T.Ms[:], T.M[:, 256:4352].indirect(T.KL[:, 0:16]), r=Mk + ["KLc"], w=["Ms"], k="g")
+        tag("ms")
+        pick(GQ[0], T.Ms[:], T.M[:, 256:4352].indirect(T.KL[:, 0:16]), Mk + ["KLc"], ["Ms"])
         yb = T["yb%d" % r]
         yk = ["yb%d_%d" % (r, o) for o in range(N)]
         for k, (lo, n) in enumerate(LCH):
@@ -695,7 +719,7 @@ def rank_program(g, core, T, topo):
                 tt(T.PD[:, 5 * lo + cd:5 * hi:5], T.VL[:, 1024 * cd + 4 * lo + 3:1024 * cd + 4 * hi:4], ps(*wp(cd, lo, hi)), A.mult,
                    ["VL%d_%d" % (o, cd) for o in part] + pk(*wp(cd, lo, hi)), ["PD%d_%d" % (k, cd)])
             scan(T.Y5[:, 5 * lo:5 * hi], T.R5[:, 5 * lo:5 * hi], T.PD[:, 5 * lo:5 * hi], 0.0, A.mult, A.add,
-                 ["PD%d_%d" % (k, cd) for cd in range(4)] + ["PDk", "R5", "D04"], ["Y5%d" % k])
+                 ["PD%d_%d" % (k, cd) for cd in range(4)] + ["PDk", "R50", "R51", "R52", "R53", "D04"], ["Y5%d" % k])
             ts(yb[:, lo:hi], T.Y5[:, 5 * lo + 4:5 * hi:5], -1152.0, None, A.add, r=["Y5%d" % k], w=[yk[o] for o in part], k=0.5)
         tag("ys")
         for k, part in enumerate(YP):
@@ -716,15 +740,23 @@ def rank_program(g, core, T, topo):
                r=["KR%d" % k, "KS" + "cf"[k]], w=["EQ%d_%d" % (k, c)], k=0.5)
         tag("cnt%d" % k)
         b, o = (6, 256) if k == 0 else (5, 0)
-        items = [(ps(b, o, o + 256), cb("pen"), T["RF%d" % r][:], True, False)]
-        items += [(ps(b, o + 16 * (c + 1), o + end(c)), cb("big"), EQ[:, c, 16:end(c) - 16 * c], False, False) for c in range(16) if c % 8 < 7]
-        items += [(ps(b, o, o + 256), cb("pow"), EQ[:, :, 0:16], False, True)]
         eq = ["EQ%d_%d" % (k, c) for c in range(16)]
-        mm(items[0:5], eq[0:4] + ["pen", "big", "RF%d" % r, "RFr%d" % r], pk(b))
-        mm(items[5:8], eq[4:8], pk(b), acc=True)
-        mm(items[8:12], eq[8:12], pk(b), acc=True)
-        mm(items[12:], eq + ["pow"], pk(b), acc=True)
-        act(T.LS[:, 256 * k:256 * k + 256], ps(b, o, o + 256), AF.Identity, pk(b, o, o + 256), ["LS%d" % k], bias=131072.0)
+        if PEN:
+            items = [(ps(b, o, o + 256), cb("pen"), T["RF%d" % r][:], True, False)]
+            items += [(ps(b, o + 16 * (c + 1), o + end(c)), cb("big"), EQ[:, c, 16:end(c) - 16 * c], False, False) for c in range(16) if c % 8 < 7]
+            items += [(ps(b, o, o + 256), cb("pow"), EQ[:, :, 0:16], False, True)]
+            mm(items[0:5], eq[0:4] + ["pen", "big", "RF%d" % r, "RFr%d" % r], pk(b))
+            mm(items[5:8], eq[4:8], pk(b), acc=True)
+            mm(items[8:12], eq[8:12], pk(b), acc=True)
+            mm(items[12:], eq + ["pow"], pk(b), acc=True)
+        else:
+            items = [(ps(b, o, o + 256), cb("pow"), EQ[:, :, 0:16], True, False)]
+            items += [(ps(b, o + 16 * (c + 1), o + end(c)), cb("big"), EQ[:, c, 16:end(c) - 16 * c], False, c == 14) for c in range(16) if c % 8 < 7]
+            mm(items[0:4], eq + ["pow", "big"], pk(b))
+            mm(items[4:8], [], pk(b), acc=True)
+            mm(items[8:11], [], pk(b), acc=True)
+            mm(items[11:], [], pk(b), acc=True)
+        act(T.LS[:, 256 * k:256 * k + 256], ps(b, o, o + 256), AF.Identity, pk(b, o, o + 256), ["LS%d" % k], bias=131072.0 * PEN)
 
     def put(win, k, src, r, w):
         for hf in (1, 0):
@@ -739,6 +771,9 @@ def rank_program(g, core, T, topo):
         ts(T.GS[:], ps(2, 256, 512), 0.5, -0.5, A.min, A.max, r=pk(2, 256, 512), w=["GS"])
         tag("ug")
         for a, n in UGS:
+            n = min(n, 16 - UGV - a)
+            if n <= 0:
+                continue
             ul = ["UL%d" % k for k in range(5) if 8 << k < 16 * (a + n)]
             act(T.UG[:, 256 * a:256 * (a + n)], T.F[:, 0:2048].indirect(T.UL[:, 16 * a:16 * (a + n)]), AF.Identity, Fk + ul,
                 ["UG%d" % j for j in range(a, a + n)], k="g", bias=256.0)
@@ -746,16 +781,23 @@ def rank_program(g, core, T, topo):
         tt(T.KY[:, 16:32], ps(7, 288, 304), T.BI[:], A.add, pk(7, 288, 304) + ["BI"], ["KYf"])
         cp(T.KL[:, 16:32], T.KY[:, 16:32], ["KYf"], ["KLf"])
         tt(T.KS[:, 16:32], T.KY[:, 16:32], T.dd[:], A.add, ["KYf", "dd"], ["KSf"])
-        act(T.KR[:, 256:512], T.IOTA[:].indirect(T.KL[:, 16:32]), r=["KLf"] + ["IOTA%d" % k for k in range(4)], w=["KR1"], k="g")
-        act(T.Co[:], T.C[:, 0:4096].indirect(T.KL[:, 0:16]), r=Ck + ["KLc"], w=["Co"], k="g")
-        act(T.Fo[:], T.F[:, 0:2048].indirect(T.KL[:, 16:32]), r=Fk + ["KLf"], w=["Fo"], k="g")
+        tag("kr")
+        pick(GQ[1], T.KR[:, 256:512], T.IOTA[:].indirect(T.KL[:, 16:32]), ["KLf"] + ["IOTA%d" % k for k in range(4)], ["KR1"])
+        tag("co")
+        pick(GQ[2], T.Co[:], T.C[:, 0:4096].indirect(T.KL[:, 0:16]), Ck + ["KLc"], ["Co"])
+        tag("fo")
+        pick(GQ[3], T.Fo[:], T.F[:, 0:2048].indirect(T.KL[:, 16:32]), Fk + ["KLf"], ["Fo"])
         losers(r, 0)
         losers(r, 1)
         tag("win")
         mm(group(ps(7, 304, 336), [(cb("Z3", 15 - k), T.LS[:, k:512:16]) for k in range(16)]), ["LS0", "LS1", "Z3"], pk(7, 304, 336))
         ts(T.bad[:], ps(7, 304, 336), col(THR), 65536.0, A.is_gt, A.mult, r=pk(7, 304, 336) + ["THR"], w=["bad"])
         tt(T.bad[:], T.bad[:], T.trash[:], A.min, ["trash"], ["bad"])
-        tt(T.bad[:], T.bad[:], T.KY[:], A.max, ["KYc", "KYf"], ["bad"])
+        if not PEN:
+            for k in range(2):
+                tt(T.KD[:, 16 * k:16 * k + 16], T.dd[:], T.tneg[:, 16 * k:16 * k + 16], A.mult, ["dd", "tneg"], ["KD%d" % k])
+            tt(T.KD[:], T.KD[:], T.KY[:], A.max, ["KYc", "KYf"], ["KD0", "KD1"])
+        tt(T.bad[:], T.bad[:], (T.KY if PEN else T.KD)[:], A.max, ["KYc", "KYf", "KD0", "KD1"], ["bad"])
         cp(T.OL[:], T.bad[:], ["bad"], ["OL"])
         tag("prod")
         mm([(ps(1, 0, 256), T.n256[:], T.GS[:], True, False)], ["GS", "n256"], pk(1), ["#1grp"])
@@ -785,9 +827,15 @@ def rank_program(g, core, T, topo):
         ts(T.TB[:, 0:256:16], T.e16[:], -1.0, 15.0, A.mult, A.add, r=["e16"], w=["TB"])
         op("v", lambda: V.transpose(T.Mn[:], T.TB[:]), ["TB"], ["Mn"], cost(256, 0.5))
         put(T.M[:, 256:4864], 0, T.Mn, ["Mn"], Mk)
-        act(T.M[:, 4352:4608], T.M[:, 256:512], w=["M"])
-        for k in range(1, 4):
-            dma("y", T.M[k:128:16, 256:4352], T.M[0:128:16, 256 + OFF[k]:4352 + OFF[k]], "dm%d" % (r + 1), r=["M"], w=["Mrow%d" % k], lat=2.6)
+        if WRS:
+            act(T.M[:, 4352:4608], T.M[:, 256:512], w=["M"])
+            for k in range(1, 4):
+                dma("y", T.M[k:128:16, 256:4352], T.M[0:128:16, 256 + OFF[k]:4352 + OFF[k]], "dm%d" % (r + 1), r=["M"], w=["Mrow%d" % k])
+        else:
+            for k in range(1, 4):
+                dma("y", T.M[k:128:16, 256:4352 - OFF[k]], T.M[0:128:16, 256 + OFF[k]:4352], "dm%d" % (r + 1), r=["M"], w=["Mrow%d" % k])
+            for k in range(1, 4):
+                dma("y", T.M[k:128:16, 4352 - OFF[k]:4352], T.M[0:128:16, 256:256 + OFF[k]], "dm%d" % (r + 1), r=["M"], w=["Mwrap%d" % k])
         tag("wc")
         put(T.C[:], 0, T.Cn, ["Cn"], Ck)
 
@@ -796,17 +844,17 @@ def rank_program(g, core, T, topo):
     for r in range(RO):
         now[0] = r
         owner_values(r)
+        if r == RO - 1:
+            tag("yc")
+            for k in range(8):
+                mm([(ps(4, 0, 256), cb("Zy", 15 - j), T.C[:, 256 * j:256 * j + 256], j == 0, j == 15) for j in range(2 * k, 2 * k + 2)],
+                   Ck + ["Zy"], pk(4), acc=k > 0)
+            act(T.YK[:], ps(4, 0, 256), r=pk(4), w=["YK"])
+            dma("y", T.YC[0:128:16, 0:4096], T.YK[:], "dyc", r=["YK"], w=YCk)
         train(r)
         home_update(r)
         if r < RO - 1:
             home_route(r + 1)
-        if r == RO - 2:
-            tag("yc")
-            for k in range(4):
-                mm([(ps(1, 0, 256), cb("Zy", 15 - j), T.C[:, 256 * j:256 * j + 256], j == 0, j == 15) for j in range(4 * k, 4 * k + 4)],
-                   Ck + ["Zy"], pk(1), acc=k > 0)
-            act(T.YK[:], ps(1, 0, 256), r=pk(1), w=["YK"])
-            dma("y", T.YC[0:128:16, 0:4096], T.YK[:], "dyc", r=["YK"], w=YCk)
     tag("end")
     mm([(ps(6, 0, 256), cb("ycw"), T.Cn[:], True, True)], ["Cn", "ycw"], pk(6, 0, 256))
     act(T.ycn[:], ps(6, 0, 256), r=pk(6, 0, 256), w=["ycn"])
@@ -822,15 +870,24 @@ def rank_program(g, core, T, topo):
     dma("s", T.ys[:], T.ysO[:], "out", r=["ysO"])
     if not ORDER:
         rng = np.random.default_rng(1)
-        names = sorted({e["tag"] + e["q"] for e in ops})
+        label = [(e["tag"] + e["q"], e["tag"]) for e in ops]
+        names = sorted({a for a, _ in label}) + sorted({b for _, b in label})
         net = graph()
-        best = schedule(net, [-v for v in net[2]])
-        for _ in range(TRIES):
-            move = {names[k]: 2.0 * float(rng.standard_normal()) for k in rng.integers(0, len(names), int(rng.integers(1, 6)))}
-            got = schedule(net, [t + move.get(e["tag"] + e["q"], 0.0) for t, e in zip(best[1], ops)])
+        brief.extend((e["c"], e["q"], e["lat"], e["x"]) for e in ops)
+        marks.extend(i for i, e in enumerate(ops) if e["kind"] != "c")
+        best = now_ = schedule(net, [-v for v in net[2]], True)
+        for it in range(TRIES):
+            wide = 1.5 * float(rng.random()) + 0.3
+            move = {names[k]: wide * float(rng.standard_normal()) for k in rng.integers(0, len(names), int(rng.integers(1, MOVES)))}
+            key = [t + move.get(a, 0.0) + move.get(b, 0.0) for t, (a, b) in zip(now_[1], label)]
+            for i in rng.integers(0, len(ops), ONES):
+                key[i] += wide * float(rng.standard_normal())
+            got = schedule(net, key, it % BOTH == 0)
+            if got[0] <= now_[0] + HEAT * (1.0 - it / TRIES) * float(rng.random()):
+                now_ = got
             if got[0] <= best[0]:
                 best = got
-        ORDER.extend([best[0], sorted(range(len(ops)), key=lambda i: (best[1][i], i))])
+        ORDER.extend([best[2], sorted(range(len(ops)), key=lambda i: (best[1][i], i)), net, ops])
     for i in ORDER[1]:
         emit(ops[i])
     for sem, val in total.items():

import numpy as np
from concourse.bass import DstId, RemoteDMATransfer
from concourse.mybir import dt, AluOpType, AxisListType, ActivationFunctionType
A = AluOpType
AF = ActivationFunctionType
N, S, CAP, RO = 8, 192, 32, 3
B0 = 160.0
OFF = (0, 61, 173, 234)
BOFF = (0, 89, 91, 52)
NP = 12
TAG = [""]
CY, GA, SCA, FIX, WAKE, SENT, ROW, LAND, TF, FIRST = 0.87e-3, 1.56, 3.8, 0.005, 0.13, 1.1, 0.018, 0.6, 1.0, 2.0
SPLIT = 4
YP = [(0, 1, 2, 3), (4, 5), (6, 7)]
EVAC, MZG, MGQ, EQV, MBS, VECQ, VECH = "ssss", 2, "vssss", 8, 4, "s", "vs"
LCH = [(0, 64), (64, 64), (128, 64), (192, 32), (224, 32)]
BCH = [(0, 64), (64, 192)]
FGV, UGV, CLF = (0, 0, 0, 0, 0), 0, 1
UGS = [(0, 2), (2, 2), (4, 4), (8, 4), (12, 2), (14, 2)]
PRO = list(range(16))
GQ, PEN, WRS, FQ, MZQ = "vvss", 0, 0, "ssssss", "gggs"
TRIES, EARLY, BOTH, MOVES, ONES, HEAT, ORDER = 7000, 0.2, 2, 5, 10, 0.05, []
SW = 1824
bf, f32, i32, u16, f16 = "bfloat16", "float32", "int32", "uint16", "float16"
CB = ["Z2", "Z3", "Zy", "dC", "dF", "dN", "xC", "xF", "xN", "pow", "big", "pen", "ycw", "I64", "In", "I2",
      "r1", "r2", "rs", "w0", "w1", "w2", "w3"]
CH = ["ZA", "Z1", "Zh", "b0", "b1", "b2", "b3", "cnt"]
SB = {
    "C": ([128, 4608], bf), "F": ([128, 2304], bf), "M": ([128, 4864], bf), "YC": ([128, 4608], f32), "YK": ([128, 256], f32),
    "X": ([128, S], i32), "tgr": ([128, S], bf), "tgc": ([128, S], bf), "cl": ([128, S], bf), "ob": ([128, S], bf), "wr": ([128, S], bf),
    "h": ([128, S], f16), "cum": ([128, S], f16), "val": ([128, S], f16), "Fh": ([128, S], bf), "lim": ([128, S], f16), "PI": ([128, S], f32),
    "yg": ([128, RO, S], bf), "sg": ([128, RO, S], bf), "ysO": ([128, S], f32), "xO": ([128, S], f32),
    "SF0": ([128, SW], bf), "SF1": ([128, SW], bf), "SF2": ([128, SW], bf),
    "ST": ([128, SW], bf), "RY": ([128, SW], bf), "slot": ([128, 12], u16), "GS": ([128, 256], bf), "n256": ([128, 128], bf),
    "RF0": ([128, 256], bf), "RF1": ([128, 256], bf), "RF2": ([128, 256], bf),
    "RT0": ([128, 256], bf), "RT1": ([128, 256], bf), "RT2": ([128, 256], bf),
    "yb0": ([128, 256], bf), "yb1": ([128, 256], bf), "yb2": ([128, 256], bf),
    "ones": ([128, 256], bf), "Z": ([128, 512], bf), "IW": ([128, 144], bf), "BDu": ([128, 128], bf), "BD": ([128, 128], bf), "BDt": ([128, 128], bf),
    "cb": ([128, len(CB), 144], bf), "ch": ([128, len(CH), 144], f16), "MB": ([128, NP, 144], bf),
    "VEC": ([128, 4, NP * 16], bf), "comb": ([128, 144], bf), "PAT": ([128, NP, 16], bf),
    "pc": ([128, 4], i32), "col": ([128, 32], f32), "R4": ([128, 4], f32), "J": ([128, 16], f32), "RM": ([128, 16], f32), "two": ([128, 16], f32), "pw": ([128, 16], f32),
    "RST": ([128, 256], bf), "trash": ([128, 32], f32), "IOTA": ([128, 2048], f32),
    "SC": ([128, 4096], f32), "E": ([128, 256], i32), "R2": ([128, 2, 128], bf), "T2": ([128, 256], bf),
    "hv": ([128, 64], f32), "hp": ([128, 64], f32), "hi": ([128, 64], i32), "ML": ([128, 64], u16),
    "bv": ([128, 256], f32), "bi": ([128, 256], i32), "BB": ([128, 256], bf), "Lv": ([128, S], bf), "Lh": ([128, S], bf),
    "fv": ([128, 64], f32), "fi": ([128, 64], i32), "Q": ([128, 64], f16),
    "Mo": ([128, 1024], bf), "FL": ([128, 256], u16), "VG": ([128, 4096], bf),
    "VL": ([128, 4096], f16), "D0": ([128, 1024], bf), "PD": ([128, 1280], f32), "R5": ([128, 1280], bf), "Y5": ([128, 1280], f16),
    "KS": ([128, 32], f32), "KY": ([128, 32], f32), "KL": ([128, 32], u16), "BI": ([128, 16], i32), "AI": ([128, 32], i32), "y16": ([128, 256], f16), "UL": ([128, 256], u16), "dd": ([128, 16], f32), "KN": ([128, 16], f32), "GM": ([128, 8], f32),
    "KR": ([128, 512], f16), "EQ0": ([128, 16, 128], bf), "EQ1": ([128, 16, 128], bf), "LS": ([128, 512], bf),
    "bad": ([128, 32], f32), "KD": ([128, 32], f32), "tneg": ([128, 32], f32), "OL": ([128, 32], u16),
    "Ms": ([128, 256], bf), "Co": ([128, 256], bf), "Fo": ([128, 256], bf), "Cn": ([128, 256], bf), "Fn": ([128, 256], bf),
    "UG": ([128, 4096], f16), "PR": ([128, 4096], f16), "TR": ([128, 256], bf), "TB": ([128, 256], bf), "Mn": ([128, 256], bf),
    "sn": ([128, 256], f32), "e16": ([128, 16], i32), "ycn": ([128, 256], f32),
}
SCRATCH = {k: ("sbuf", v[0], v[1]) for k, v in SB.items()}
for _k in range(8):
    SCRATCH["P%d" % _k] = ("psum", [128, 512], f32)
SEMAPHORES = (["cv", "ct", "cs", "cg", "dx", "dc0", "dc1", "dc2", "dc3", "df", "dtg", "dm0", "dm1", "dm2", "dyc", "out"]
              + [p + str(r) for p in ("af", "at", "ay", "lf", "lt") for r in range(RO)]
              + ["ly%d_%d" % (r, k) for r in range(RO) for k in range(4)])


def plan(topo, cores, src, parts=None):
    k = cores.index(src)
    turn = cores[k + 1:] + cores[:k]
    far = [d for d in turn if topo.chip(d) != topo.chip(src)]
    near = [d for d in turn if topo.chip(d) == topo.chip(src)]
    pool = list(topo.engines(src, far[0]))
    if parts is None:
        sets = [far[:SPLIT] + near, far[SPLIT:]]
    else:
        sets = [[d for d in turn if cores.index(d) in part] for part in parts]
    calls = []
    for ds in sets:
        out = [d for d in ds if d in far]
        w = len(pool)
        while w * len(out) > len(pool):
            w //= 2
        calls.append({d: pool[w * j:w * j + w] for j, d in enumerate(out)})
        for d in ds:
            if d in near:
                calls[-1][d] = [e for e in topo.engines(src, d) if e not in pool]
    return calls


def patterns():
    p = {}

    def put(k, c, rows, one=0.0, by=1.0):
        for row, v in rows.items():
            p[(row, 16 * k + c)] = p.get((row, 16 * k + c), 0.0) + by * v
        for row in range(12, 16) if one else ():
            p[(row, 16 * k + c)] = p.get((row, 16 * k + c), 0.0) + one / 16
    pa = ({0: 1}, {0: 1, 2: 1}, {1: 1, 2: -1}, {1: 1})
    pb = ({4: 1}, {5: 1}, {4: 1, 6: 1, 5: -1}, {6: 1})
    for x in range(4):
        put(0, 12 + x, pa[x]); put(1, 12 + x, pb[x], 1, 2); put(2, 12 + x, {8: 244, 9: 692})
        put(9, 12 + x, {x: 1})
        for cd in range(4):
            put(3, 4 * x + cd, {8: 1}, cd & 1); put(4, 4 * x + cd, {9: 2}, 2 * (cd >> 1) + 1)
            put(5, 4 * x + cd, pa[x], 0, 356); put(5, 4 * x + cd, pb[x], 0, 364)
    put(6, 12, {0: 1}); put(7, 12, {4: 2}, 1); put(8, 12, {10: 244, 11: 692})
    put(6, 13, {10: 32}); put(7, 13, {11: 2}, 1); put(8, 13, {0: 356 * 32, 4: 364 * 32})
    put(8, 14, {}, 4)
    odd = lambda e: {4 * e + 3: 1, 4 * e + 2: -1, 4 * e + 1: 1, 4 * e: -1}
    for c, rows in ((0, {1: 1}), (1, {0: 1, 3: 1, 1: -1}), (4, {5: 1}), (5, {6: 1}), (6, {4: 1, 7: 1, 5: -1}),
                    (8, {8: 1}), (9, {12: 1}), (10, {9: 1}), (11, {13: 1})):
        put(10, c, rows); put(10, c, {11: -B0}); put(11, c, {11: 1})
    put(10, 2, {0: 1, 3: 1, 1: -2}); put(10, 3, odd(0)); put(10, 7, odd(0)); put(10, 7, odd(1))
    put(11, 2, odd(1)); put(11, 3, odd(1)); put(11, 7, {11: 1})
    for cd in range(4):
        for k, row, bit in ((10, 8, cd & 1), (11, 12, cd >> 1)):
            put(k, 12 + cd, {row + 2: 1, row: -4, 11: 4 * B0 - (0 if bit else 4)}, 0, 1 if bit else -1)
    runs = []
    by = {}
    for (row, c), v in sorted(p.items()):
        by.setdefault((row, float(v), c >= 160), []).append(c)
    for (row, v, home), cs in by.items():
        while cs:
            best = [cs[0]]
            for c2 in cs[1:]:
                st, run = c2 - cs[0], [cs[0]]
                while run[-1] + st in cs:
                    run.append(run[-1] + st)
                if len(run) > len(best):
                    best = run
            st = best[1] - best[0] if len(best) > 1 else 1
            cols = (best[0], best[-1] + 1, st)
            for e in runs:
                if e[0] == row // 4 and e[2] == row % 4 and e[3] == cols and e[5] == v:
                    e[2] += 1
                    break
            else:
                runs.append([row // 4, row % 4, row % 4 + 1, cols, len(best), v, home])
            cs = [c for c in cs if c not in best]
    return [(q, slice(a, b), slice(*cols), n * (b - a), v, home) for q, a, b, cols, n, v, home in runs]


def rank_program(g, core, T, topo):
    me = T.rank_of(core)
    if me is None:
        return
    cores = list(T.cores)
    V, P, Sc, Y = g.vector, g.tensor, g.scalar, g.sync
    Qs = {"v": V, "t": P, "s": Sc, "g": g, "y": Y}
    total, clock, snap = {}, {q: {} for q in Qs}, {}
    wr, rd, bank = {}, {}, {}

    def need(q, ev):
        sem, val = ev
        if sem[0] == "d":
            val = total[sem]
        if clock[q].get(sem, 0) >= val:
            return
        Qs[q].wait_ge(T.sem[sem], val)
        clock[q][sem] = val
        for k, v in snap.get((sem, val), {}).items():
            if clock[q].get(k, 0) < v:
                clock[q][k] = v

    def deps(q, r, w, x, acc):
        evs = {}

        def add(ev):
            if ev and evs.get(ev[0], 0) < ev[1]:
                evs[ev[0]] = ev[1]
        for k in r:
            add(wr.get(k))
        for k in w:
            if not acc:
                add(wr.get(k))
            for ev in rd.get(k, {}).items():
                add(ev)
        for b in x:
            for q2, ev in bank.get(b, {}).items():
                if q2 != q:
                    add(ev)
        for ev in evs.items():
            need(q, ev)

    def done(q, ev, r, w, x):
        snap[ev] = dict(clock[q])
        for k in r:
            rd.setdefault(k, {})[ev[0]] = ev[1]
        for k in w:
            wr[k] = ev
            rd[k] = {}
        for b in x:
            bank.setdefault(b, {})[q] = ev

    ops, brief, marks = [], [], []

    def size(ap):
        n = 1
        for d in ap.shape[1:]:
            n *= d
        return n

    def cost(n, k):
        if k == "g":
            return 0.05 + n * GA * CY
        if k == "s":
            return 0.05 + n * SCA * CY
        return FIX + max(64, n * k) * CY

    def op(q, fn, r=(), w=(), c=0.1, o=(), lat=0.0, kind="c", extra=None):
        x = sorted({int(k[1]) for k in list(r) + list(w) + list(o) if k[0] == "#"})
        ops.append(dict(q=q, fn=fn, r=list(r), w=list(w), x=x, o=list(o), c=c, lat=lat, kind=kind, extra=extra, tag=TAG[0]))

    def dma(q, out, in_, sem, r=(), w=(), lat=2.2, o=()):
        op(q, lambda: Qs[q].dma_start(out, in_), r, w, 0.06, o, lat, "d", sem)

    def fill(q, out, v, w):
        n = size(out)
        if q == "v":
            ms(out, v, w=w)
        elif q == "s":
            act(out, T.ones[:, 0:n], r=["ones"], w=w, scale=v)
        else:
            op("g", lambda: g.iota(out, [[0, n]], int(v), 0, allow_small_or_imprecise_dtypes=True), [], w, 0.2 + 2 * n * CY)

    def mm(items, r, w, o=(), acc=False):
        def fn():
            for it in items:
                i = P.matmul(*it)
            return i
        op("t", fn, r, w, sum(0.012 + max(64, size(it[2])) * CY * TF for it in items), o, 0.0, extra=acc)

    def group(out, pairs, start=True, stop=True):
        return [(out, l, rr, start and k == 0, stop and k == len(pairs) - 1) for k, (l, rr) in enumerate(pairs)]

    def ts(out, in0, s1, s2, op0, op1=None, r=(), w=(), k=1):
        if op1 is None:
            op("v", lambda: V.tensor_scalar(out, in0, s1, None, op0), r, w, cost(size(out), k))
        else:
            op("v", lambda: V.tensor_scalar(out, in0, s1, s2, op0, op1), r, w, cost(size(out), k))

    def tt(out, a, b, o, r=(), w=()):
        ps = any(k[0] == "#" for k in list(r) + list(w))
        op("v", lambda: V.tensor_tensor(out, a, b, o), r, w, cost(size(b), 1 if ps else 2))

    def cp(out, a, r=(), w=(), k=1):
        op("v", lambda: V.tensor_copy(out, a), r, w, cost(size(a if k == "s" else out), k))

    def ms(out, k, r=(), w=()):
        op("v", lambda: V.memset(out, k), r, w, cost(size(out), 0.5))

    def scan(out, d0, d1, init, o0, o1, r, w, k=1):
        op("v", lambda: V.tensor_tensor_scan(out, d0, d1, init, o0, o1), r, w, cost(size(out), k))

    def act(out, a, fn=AF.Copy, r=(), w=(), k=1, **kw):
        op("s", lambda: Sc.activation(out, a, fn, **kw), r, w, cost(size(out), k))

    def pick(q, out, a, r, w):
        if q == "v":
            cp(out, a, r, w, k="g")
        else:
            act(out, a, r=r, w=w, k="g")

    def send(kind, rnd, src, dst, r, w, landed, parts=None, part=None):
        plans = {c: plan(topo, cores, c, parts) for c in cores}
        calls = plans[core] if part is None else plans[core][part:part + 1]
        ls = "l%s%d" % (kind, rnd) + ("" if part is None else "_%d" % part)
        arrive = sum(len(call.get(core, ())) for c in cores for call in plans[c])
        leave = sum(len(e) for call in calls for e in call.values())

        def fn():
            for call in calls:
                trs = []
                for d, engines in call.items():
                    rid, pid, _ = topo.addr(d)
                    trs.append(RemoteDMATransfer(dst_ids=[DstId(rid=rid, pnc=pid)], dma_engine_mask=sum(1 << e for e in engines),
                                                 remote_sem=T.sem["a%s%d" % (kind, rnd)], src=src(cores.index(d)), dst=dst))
                g.remote_dma_fused(trs, local_sem=T.sem[ls])
        rows = 96 if part is None else 16 * len(parts[part])
        op("g", fn, r, w, 0.4 * len(calls) + (FIRST if ls == "lf0" else 0.0), ["eng"], SENT + ROW * rows, "r",
           (ls, landed, "a%s%d" % (kind, rnd), arrive, leave))

    def emit(e):
        q = e["q"]
        TAG[0] = e["tag"]
        deps(q, e["r"], e["w"], e["x"], q == "t" and e["extra"])
        if q == "g" and e["kind"] == "c" and "cg" in total:
            need(q, ("cg", total["cg"]))
        if e["kind"] == "r":
            ls, landed, sem, arrive, leave = e["extra"]
            e["fn"]()
            total[ls] = leave
            total[sem] = arrive
            wr[landed] = (sem, arrive)
            ev = (ls, leave)
        else:
            sem, n = (e["extra"], 16) if e["kind"] == "d" else ("c" + q, 1)
            total[sem] = total.get(sem, 0) + n
            e["fn"]().then_inc(T.sem[sem], n)
            ev = (sem, total[sem])
        done(q, ev, e["r"], e["w"], e["x"])

    def graph():
        n = len(ops)
        pre = [dict() for _ in range(n)]
        lw, lr, lo = {}, {}, {}
        for i, e in enumerate(ops):
            def edge(j, d):
                if j != i and pre[i].get(j, -1.0) < d:
                    pre[i][j] = d
            for k in e["r"] + e["w"]:
                if k in lw:
                    edge(lw[k][0], 0.0 if e["extra"] is True and k in e["w"] else lw[k][1])
            for k in e["w"]:
                for j in lr.get(k, ()):
                    edge(j, ops[j]["lat"] + WAKE)
            for k in e["o"]:
                if k in lo:
                    edge(lo[k], 0.0)
                lo[k] = i
            for k in e["r"]:
                lr.setdefault(k, []).append(i)
            for k in e["w"]:
                lw[k] = (i, e["lat"] + WAKE)
                lr[k] = []
            if e["kind"] == "r":
                lw[e["extra"][1]] = (i, e["lat"] + LAND)
        post = [[] for _ in range(n)]
        for i in range(n):
            for j, d in pre[i].items():
                post[j].append((i, d))
        level = [0.0] * n
        for i in range(n - 1, -1, -1):
            level[i] = ops[i]["c"] + max([ops[i]["lat"]] + [d + level[j] for j, d in post[i]])
        return [list(p.items()) for p in pre], post, level

    def place(turn, before, back):
        start = [0.0] * len(ops)
        busy = {q: ([], []) for q in Qs}
        held = [{} for _ in range(8)]
        stop = [0.0] * len(ops)
        end = 0.0
        for i in turn:
            c, q, lat, x = brief[i]
            hold = lat + WAKE
            t = lat if back else 0.0
            for j, d in before[i]:
                if stop[j] + d > t:
                    t = stop[j] + d
            a, b = busy[q]
            while True:
                lo, hi = 0, len(b)
                while lo < hi:
                    mid = (lo + hi) // 2
                    if b[mid] <= t:
                        lo = mid + 1
                    else:
                        hi = mid
                while lo < len(a) and a[lo] < t + c:
                    t = b[lo]
                    lo += 1
                if not x:
                    break
                t0 = t
                x0, x1 = (t - hold, t + c) if back else (t, t + c + hold)
                for k in x:
                    for u in range(int(x0), int(x1) + 1):
                        for y0, y1, q2 in held[k].get(u, ()):
                            if q2 != q and y0 < x1 and x0 < y1:
                                t = max(t, y1 + (hold if back else 0.0))
                if t == t0:
                    break
            a.insert(lo, t)
            b.insert(lo, t + c)
            for k in x:
                for u in range(int(x0), int(x1) + 1):
                    held[k].setdefault(u, []).append((x0, x1, q))
            start[i], stop[i] = t, t + c
            end = max(end, t + c + (0.0 if back else lat))
        return end, start

    def schedule(net, key, both):
        pre, post = net[0], net[1]
        n = len(ops)
        for i in range(n):
            k = key[i]
            for j, d in pre[i]:
                if key[j] >= k:
                    k = key[j] + 1e-6
            key[i] = k
        rate = lambda got: (got[0] + EARLY * sum(got[1][i] for i in marks) / len(marks), got[1], got[0])
        got = rate(place(sorted(range(n), key=lambda i: key[i]), pre, False))
        if both:
            late = place(sorted(range(n), key=lambda i: (-got[1][i] - ops[i]["c"], -i)), post, True)[1]
            again = rate(place(sorted(range(n), key=lambda i: (-late[i] - ops[i]["c"], i)), pre, False))
            got = min(got, again, key=lambda v: v[0])
        return got

    cb = lambda n, a=0: T.cb[:, CB.index(n), a:a + 128]
    ch = lambda n, a=0: T.ch[:, CH.index(n), a:a + 128]
    I = T.IW[:, 8:136]
    col = lambda j: T.col[:, j:j + 1]
    RM = lambda j: T.RM[:, j:j + 1]
    RC, LT8, INIT, Z1C, OC, R1, ZAC, SUB, THR, S1, S2, S3, LA, LB, GE8, XR, ON, XM, FR, KX, WB, PN, I4, O16, CR1, CR2, CRS = range(27)
    WRAP = 256 * B0
    now = [0]

    def tag(s):
        TAG[0] = s + str(now[0])

    def pk(b, lo=0, hi=512):
        return ["#%d_%d" % (b, j) for j in range(lo // 16, (hi + 15) // 16)]

    def ps(b, lo=0, hi=512):
        return T["P%d" % b][:, lo:hi]

    tag("c0")
    ms(T.X[:], 0, w=["X0"])
    ms(T.ones[:], 1.0, w=["ones"])
    for e in range(4):
        dma("ys"[e // 2], T.X[(0, 4, 10, 14)[e]:128:16, :], T.x0[e:32:4, :], "dx", r=["X0"], w=["X%d" % (e + 1)], o=["load"], lat=1.8)
    for k in range(4):
        dma("y", T.C[:, 1024 * k:1024 * k + 1024], T.cf[:, 1024 * k:1024 * k + 1024], "dc%d" % k, w=["C%d" % k], lat=2.6 + k, o=["load"])
    dma("y", T.tgr[:], T.tg[:], "dtg", w=["tgr"], o=["load"], lat=6.0)
    dma("y", T.F[:, 0:2048], T.ft[:], "df", r=["SF0"], w=["F"], lat=3.5)
    op("g", lambda: g.affine_select(T.IW[:], T.ones[:, 0:144], [[-1, 144]], A.is_equal, 0.0, 8, 1), ["ones"], ["IW"], 0.45)
    op("g", lambda: g.iota(T.PI[:], [[256, 6], [1, 32]], 256, 0, allow_small_or_imprecise_dtypes=True), [], ["PI"], 0.5)
    op("g", lambda: g.iota(T.pc[:, 0:1], [[0, 1]], 0, 1), [], ["pc"], 0.14)
    op("g", lambda: g.iota(T.J[:], [[1, 16]], 0, 0, allow_small_or_imprecise_dtypes=True), [], ["J"], 0.17)
    op("g", lambda: g.affine_select(T.BDt[:], T.ones[:, 0:128], [[-16, 8], [0, 16]], A.is_ge, 0.0, 0, 1), ["ones"], ["BDt"], 0.44)
    op("g", lambda: g.affine_select(T.BD[:], T.BDt[:], [[16, 8], [0, 16]], A.is_ge, 0.0, 15, -1), ["BDt"], ["BD"], 0.44)
    op("g", lambda: g.affine_select(cb("xC"), T.ones[:, 0:128], [[-16, 8], [-1, 4], [0, 4]], A.is_equal, 0.0, 0, 1), ["ones"], ["xC"], 0.44)
    act(T.GM[:], T.BD[:, 0:128:16], r=["BD"], w=["GM"])
    ms(T.MB[:, :, 128:144], 0.0, w=["MBz"])
    op("g", lambda: g.iota(T.trash[:], [[-2304, 2], [16, 16]], 4352, 0, allow_small_or_imprecise_dtypes=True), [], ["trash"], 0.2)
    for k in range(4):
        op("g", lambda k=k: g.iota(T.IOTA[:, 512 * k:512 * k + 512], [[1, 512]], 512 * k, 0, allow_small_or_imprecise_dtypes=True), [], ["IOTA%d" % k], 1.1)
    ms(T.VEC[:], 0.0, w=["VEC"])
    ms(T.comb[:], 0.0, w=["comb"])
    ms(T.RST[:], 0.0625, w=["RST"])
    ms(T.cb[:, 0:3, :], 0.0, w=["cbz"])
    ms(T.ch[:, 0:3, :], 0.0, w=["chz"])
    ms(T.two[:], 2.0, w=["two"])
    for q in range(4):
        ms(T.comb[32 * q:32 * q + 1, 4 * q + 3:128:16], 1.0, r=["comb"], w=["comb%d" % q])
    ms(T.RST[:, 0:256:16], -1024.0, w=["RST"])
    vk = [[], []]
    for k, (q, rows, cols, n, v, home) in enumerate(patterns()):
        tag("vh" if home else "vo")
        out, key, who = T.VEC[32 * q:32 * q + 1, rows, cols], "vec%d" % k, (VECH if home else VECQ)
        vk[home].append(key)
        if who[k % len(who)] == "v":
            ms(out, v, r=["VEC"], w=[key])
        elif who[k % len(who)] == "g" and v == int(v):
            op("g", lambda out=out, n=n, v=v: g.iota(out, [[0, n]], int(v), 0, allow_small_or_imprecise_dtypes=True), ["VEC"], [key], 0.2)
        else:
            act(out, T.ones[32 * q:32 * q + 1, 0:n], r=["VEC", "ones"], w=[key], scale=v)
    MBk = [["MBz"], ["MBz"]]
    for home, lo, hi in ((1, 10, 12), (0, 0, 10)):
        tag("vh" if home else "vo")
        b = 5 - home
        mm(group(ps(b, 16 * lo, 16 * hi), [(T.comb[:, 3 - k:131 - k], T.VEC[:, k, 16 * lo:16 * hi]) for k in range(4)]),
           vk[home] + ["comb%d" % q for q in range(4)], pk(b, 16 * lo, 16 * hi))
        cp(T.PAT[:, lo:hi], ps(b, 16 * lo, 16 * hi), pk(b, 16 * lo, 16 * hi), ["PAT%d" % home])
        for k in range(8):
            key = "MB%d_%d" % (home, k)
            MBk[home].append(key)
            if k < MBS:
                act(T.MB[:, lo:hi, 16 * k:16 * k + 16], T.PAT[:, lo:hi], r=["PAT%d" % home, "GM"], w=[key], scale=T.GM[:, k:k + 1])
            else:
                ts(T.MB[:, lo:hi, 16 * k:16 * k + 16], T.PAT[:, lo:hi], T.GM[:, k:k + 1], None, A.mult, r=["PAT%d" % home, "GM"], w=[key], k=0.5)
    tag("c1")
    b15 = T.BD[:, 15:128:16]
    ts(T.pc[:, 1:2], T.pc[:, 0:1], 15, None, A.bitwise_and, r=["pc"], w=["pc1"])
    cp(col(RC), T.pc[:, 1:2], ["pc1"], ["RC"])
    ts(T.pc[:, 0:1], T.pc[:, 1:2], 7, None, A.bitwise_and, r=["pc1"], w=["pc"])
    ts(T.RM[:], T.J[:], col(RC), None, A.is_equal, r=["J", "RC"], w=["RM"])
    ts(col(LT8), col(RC), 8.0, None, A.is_lt, r=["RC"], w=["LT8"])
    ts(col(LB), col(RC), 1.0, 32.0, A.add, A.mult, r=["RC"], w=["LB"])
    ts(col(GE8), col(RC), 8.0, None, A.is_ge, r=["RC"], w=["GE8"])
    ts(col(LB), col(LB), col(LT8), None, A.mult, r=["LT8"], w=["LB"])
    ts(col(LA), col(RC), 8.0, 1.0 / 2048, A.is_ge, A.mult, r=["RC"], w=["LA"])
    ts(col(INIT), col(LB), col(LT8), -32.0, A.subtract, A.add, r=["LB", "LT8"], w=["INIT"])
    ts(col(Z1C), col(GE8), 2047.0, 1.0, A.mult, A.add, r=["GE8"], w=["Z1C"])
    ts(col(OC), T.pc[:, 0:1], B0, None, A.add, r=["pc"], w=["OC"])
    ts(T.lim[:], T.PI[:], col(LA), col(LB), A.mult, A.add, r=["PI", "LA", "LB"], w=["lim"])
    ts(T.ch[:, 1, 15:128:16], b15, col(Z1C), None, A.mult, r=["BD", "Z1C", "chz"], w=["Z1"])
    ts(col(XR), RM(10), RM(14), None, A.add, r=["RM"], w=["XR"])
    ts(col(ON), RM(11), RM(15), None, A.add, r=["RM"], w=["ON"])
    ts(col(XM), col(XR), col(LT8), None, A.add, r=["XR", "LT8"], w=["XM"])
    ts(T.pc[:, 2:3], T.pc[:, 1:2], 3, None, A.bitwise_and, r=["pc1"], w=["pc2"])
    ts(col(S1), col(XR), 0.75, 0.25, A.mult, A.add, r=["XR"], w=["S1"])
    ts(col(FR), col(XR), col(ON), 0.5, A.add, A.is_lt, r=["XR", "ON"], w=["FR"])
    ts(col(S2), T.pc[:, 2:3], 0.25, B0 - 0.375, A.mult, A.add, r=["pc2"], w=["S2"])
    ts(col(S1), col(ON), -0.25, col(S1), A.mult, A.add, r=["ON"], w=["S1"])
    ts(col(S2), col(S2), col(FR), col(ON), A.mult, A.add, r=["FR", "ON"], w=["S2"])
    mm([(ps(6, 0, 128), cb("xC"), cb("xC"), True, True)], ["xC"], pk(6, 0, 128))
    ts(cb("xF"), ps(6, 0, 128), col(XM), None, A.mult, r=pk(6, 0, 128) + ["XM"], w=["xF"])
    act(cb("xN"), ps(6, 0, 128), r=pk(6, 0, 128), w=["xN"], scale=-64.0)
    act(cb("dF"), T.BD[:], r=["BD", "RM"], w=["dF"], scale=RM(14))
    tag("c2")
    cp(col(I4), T.pc[:, 2:3], ["pc2"], ["I4"])
    ts(col(KX), col(LT8), -4 * B0, WRAP, A.mult, A.add, r=["LT8"], w=["KX"])
    ts(col(WB), col(LT8), -4 * B0 / 256, B0 - 255.0 / 512, A.mult, A.add, r=["LT8"], w=["WB"])
    ts(col(S3), col(S1), col(KX), col(S2), A.mult, A.add, r=["S1", "S2", "KX"], w=["S3"])
    ts(col(PN), col(RC), 12.0, -8192.0, A.is_ge, A.mult, r=["RC"], w=["PN"])
    ts(cb("dN"), T.BD[:], RM(12), -256.0, A.mult, A.mult, r=["BD", "RM"], w=["dN"], k=0.5)
    ts(ch("cnt"), T.BD[:], col(GE8), None, A.mult, r=["BD", "GE8"], w=["cnt"], k=0.5)
    cp(T.ch[:, 2, 15:128:16], b15, ["BD", "chz"], ["Zh"])
    fill(FQ[0], T.TB[:], 0.0, ["TB"])
    fill(FQ[1], T.D0[:, 0:1024:4], 0.0, ["D0z"])
    for k in range(4):
        fill(FQ[2], T.R5[:, k:1280:5], min(k, 1.0), ["R5%d" % k])
    ts(col(O16), col(RC), 12.0, 1.0 / 16, A.is_ge, A.mult, r=["RC"], w=["O16"])
    ts(col(CR1), RM(3), 2.0, col(O16), A.mult, A.add, r=["RM", "O16"], w=["CR1"])
    ts(col(CR2), RM(3), -4.0, col(O16), A.mult, A.add, r=["RM", "O16"], w=["CR2"])
    ts(col(CR2), RM(7), 2.0, col(CR2), A.mult, A.add, r=["RM"], w=["CR2"])
    ts(col(CRS), col(O16), 4.0, RM(3), A.mult, A.add, r=["RM", "O16"], w=["CRS"])
    ts(col(CRS), RM(7), -2.0, col(CRS), A.mult, A.add, r=["RM"], w=["CRS"])
    ts(cb("rs"), T.BD[:], col(CRS), 1.0 / 256, A.mult, A.mult, r=["BD", "CRS"], w=["rs"], k=0.5)
    for name, sc, key in [("r1", col(CR1), "CR1"), ("r2", col(CR2), "CR2")] + [("w%d" % k, RM(12 + k), "RM") for k in range(4)]:
        act(cb(name), T.BD[:], r=["BD", key], w=[name], scale=sc)
    fill(FQ[3], T.PD[:, 4:1280:5], 1152.0 - 255.0 / 512, ["PDk"])
    scan(T.pw[:], T.two[:], T.RM[:], 0.0, A.mult, A.add, ["two", "RM"], ["pw"])
    ts(T.R4[:], T.J[:, 0:4], col(I4), None, A.is_equal, r=["J", "I4"], w=["R4"])
    ts(col(ZAC), T.R4[:, 2:3], 8192.0, T.R4[:, 0:1], A.mult, A.add, r=["R4"], w=["ZAC"])
    ts(col(ZAC), T.R4[:, 1:2], 2048.0, col(ZAC), A.mult, A.add, r=["R4"], w=["ZAC"])
    ts(col(SUB), col(I4), 2.0, 2048.0, A.is_lt, A.mult, r=["I4"], w=["SUB"])
    ts(col(R1), col(RC), 1.0, None, A.add, r=["RC"], w=["R1"])
    ts(T.trash[:], T.trash[:], col(RC), None, A.add, r=["RC"], w=["trash"])
    ts(T.tneg[:], T.trash[:], -1.0 / 8192, None, A.mult, r=["trash"], w=["tneg"])
    ts(col(THR), T.pw[:, 15:16], 2.5, None, A.mult, r=["pw"], w=["THR"])
    act(T.tgc[:], T.tgr[:], AF.Identity, ["tgr"], ["tgc"], bias=-128.0)
    mm([(ps(6, 128, 256), cb("xC"), I, True, True)], ["xC", "IW"], pk(6, 128, 256))
    ts(T.ch[:, 0, 12:140], ps(6, 128, 256), col(ZAC), None, A.mult, r=["ZAC", "chz"] + pk(6, 128, 256), w=["ZA"])
    for k in range(4):
        ts(ch("b%d" % k), T.BD[:], RM(4 * k), None, A.mult, r=["BD", "RM"], w=["b%d" % k], k=0.5)
    ts(T.cb[:, 1, 15:128:16], b15, RM(0), None, A.mult, r=["BD", "RM", "cbz"], w=["Z3"])
    ts(T.cb[:, 2, 15:128:16], b15, col(R1), None, A.mult, r=["BD", "R1", "cbz"], w=["Zy"])
    for name, sc, key in (("pen", col(PN), "PN"), ("dC", RM(3), "RM"), ("pow", T.pw[:, 15:16], "pw"), ("big", 65536.0, "BD"), ("ycw", col(R1), "R1")):
        act(cb(name), T.BD[:], r=["BD", key], w=[name], scale=sc)
    act(T.n256[:], T.BD[:], r=["BD"], w=["n256"], scale=-256.0)
    for j in range(16 - UGV, 16):
        ms(T.n256[:, j:128:16], 0.0, w=["n256"])
    for name, sc in (("I64", 64.0), ("In", -1.0), ("I2", 2.0)):
        act(cb(name), I, r=["IW"], w=[name], scale=sc)
    tag("z")
    for r in range(RO):
        fill(FQ[4], T["SF%d" % r][:, 0:256], 0.0, ["SF%d" % r])
    fill(FQ[4], T.ST[:, 0:256], 0.0, ["ST"])
    RYz = ["RYz%d" % k for k in range(7)]
    for k in range(7):
        fill(FQ[5], T.RY[:, 256 + 224 * k:480 + 224 * k], 0.0, [RYz[k]])
    tag("mz")
    Mz = ["Mz%d" % k for k in range(16)]
    for k in range(16):
        fill(MZQ[k % len(MZQ)], T.M[:, 256 + 256 * k:512 + 256 * k], 0.0, [Mz[k]])
    Fk = ["F"]

    tag("am")
    for k in range(8):
        b = (6, 7, 5)[k % 3]
        mm([(ps(b, 128 * ((j % 2) * 2 + j // 2), 128 * ((j % 2) * 2 + j // 2) + 128), T.C[:, 128 * (4 * k + j):128 * (4 * k + j) + 128], I, True, True)
            for j in range(4)], ["C%d" % (k // 2), "IW"], pk(b))
        for hf in range(2):
            a = 2048 * hf + 256 * k
            scan(T.SC[:, a:a + 256], T.RST[:], ps(b, 256 * hf, 256 * hf + 256), 0.0, A.add, A.max,
                 ["RST"] + pk(b, 256 * hf, 256 * hf + 256), ["SC%d_%d" % (k, hf)])
    tag("am2")
    ts(T.E[:], T.SC[:, 15:4096:16], 16.0, None, A.mult, r=["SC%d_%d" % (k, hf) for k in range(8) for hf in range(2)], w=["E"])
    ts(T.E[:], T.E[:], 15, None, A.bitwise_and, w=["E"])
    for k in range(8):
        ts(T.R2[:, :, 16 * k:16 * k + 16], T.E[:, k:256:8], -1.0, 15.0, A.mult, A.add, r=["E"], w=["R2%d" % k])
    mm([(ps(6, 128 * hf, 128 * hf + 128), T.R2[:, hf, :], I, True, True) for hf in range(2)], ["R2%d" % k for k in range(8)] + ["IW"], pk(6, 0, 256))
    cp(T.T2[:], ps(6, 0, 256), pk(6, 0, 256), ["T2"])
    for r in range(4):
        dma("ys"[r % 2], T.M[r:128:16, 256 - OFF[r]:256 - OFF[r] + 4096], T.T2[:], "dm0", r=["T2"] + Mz, w=["Mrow%d" % r], lat=2.8)
    for r in range(1, 4):
        dma("ys"[r % 2], T.M[r:128:16, 4352 - OFF[r]:4608 - OFF[r]], T.T2[0:128:16, :], "dm0", r=["T2"] + Mz, w=["Mwrap%d" % r], lat=2.8)

    Xk = ["X%d" % e for e in range(5)]

    def home_update(r):
        tag("hu")
        ry = ["RY", "RYg", "slot"] + RYz + ["RYr%d" % k for k in range(len(YP))]
        mm([(ps(0, 0, S), cb("xF"), T.Fh[:], True, False)], ["Fh", "xF"], pk(0))
        mm([(ps(3, 0, S), cb("xF"), T.Fh[:], True, False)], ["Fh", "xF"], pk(3))
        if r < RO - 1:
            mm([(ps(2, 0, S), cb("dF"), T.Fh[:], True, False)], ["Fh", "dF"], pk(2))
        act(T.yg[:, r, :], T.RY[:].indirect(T.slot[:]), r=ry, w=["yg%d" % r], k="g")
        if CLF:
            ts(T.cl[:], T.RY[:].indirect(T.slot[:]), 8.0, -8.0, A.min, A.max, r=ry, w=["cl"], k="g")
        else:
            ts(T.cl[:], T.yg[:, r, :], 8.0, -8.0, A.min, A.max, r=["yg%d" % r], w=["cl"], k=0.5)
        mm([(ps(0, 0, S), cb("xC"), T.cl[:], False, True)], ["cl", "xC"], pk(0), acc=True)
        act(T.wr[:], ps(0, 0, S), AF.Identity, pk(0) + ["WB"], ["wr"], bias=col(WB), scale=1.0 / 256)
        if r < RO - 1:
            mm([(ps(2, 0, S), cb("dC"), T.cl[:], False, False)], ["cl", "dC"], pk(2), acc=True)
            mm([(ps(2, 0, S), cb("dN"), T.wr[:], False, True)], ["wr", "dN"], pk(2), acc=True)
        mm([(ps(3, 0, S), cb("xC"), T.cl[:], False, False)], ["cl", "xC"], pk(3), acc=True)
        mm([(ps(3, 0, S), cb("xN"), T.wr[:], False, True)], ["wr", "xN"], pk(3), acc=True)

    def home_route(r):
        tag("hr")
        if r == 0:
            cp(T.Fh[:], T.X[:], Xk, ["Fh"])
            mm([(ps(2, 0, S), cb("dF"), T.Fh[:], True, True)], ["Fh", "dF"], pk(2))
            mm([(ps(3, 0, S), cb("xF"), T.Fh[:], True, True)], ["Fh", "xF"], pk(3))
        act(T.ob[:], ps(2, 0, S), AF.Identity, pk(2), ["ob"], bias=B0 - 0.484375 + (WRAP / 32 if r else 0.0), scale=1.0 / 32)
        ts(T.h[:], T.ob[:], col(OC), None, A.is_equal, r=["ob", "OC"], w=["h"], k=0.5)
        act(T.Fh[:], ps(3, 0, S), AF.Identity, pk(3) + ["S1", "S3" if r else "S2"], ["Fh"], bias=col(S3 if r else S2), scale=col(S1))
        mm([(ps(0, 0, S), T.MB[:, 11, 0:128], T.Fh[:], True, True)], ["Fh"] + MBk[1], pk(0))
        mm([(ps(3, 0, S), T.MB[:, 10, 0:128], T.Fh[:], True, True)], ["Fh"] + MBk[1], pk(3))
        act(T.Lv[:], ps(0, 0, S), r=pk(0), w=["Lv"])
        tt(T.Lh[:], ps(3, 0, S), T.Lv[:], A.mult, pk(3) + ["Lv"], ["Lh"])
        scan(T.cum[:], T.h[:], T.lim[:], col(INIT), A.add, A.min, ["h", "lim", "INIT"], ["cum"], k=0.5)
        scan(T.val[:], T.cum[:], T.h[:], 0.0, A.max, A.mult, ["h", "cum"], ["val"], k=0.5)
        mm(group(ps(4, 0, 12), [(ch("Z1", 15 - k), T.val[:, k:S:16]) for k in range(16)]), ["val", "Z1"], pk(4, 0, 12))
        cp(T.slot[:], ps(4, 0, 12), pk(4, 0, 12), ["slot"])
        SF, RF, RT = T["SF%d" % r], T["RF%d" % r], T["RT%d" % r]
        cp(SF[:].indirect(T.slot[:]), T.Lh[:], ["slot", "Lh"], ["SF%d" % r], k="s")
        send("f", r, lambda o: SF[:, CAP * o:CAP * o + CAP], RF[:, CAP * me:CAP * me + CAP], ["SF%d" % r], ["RYg"], "RFr%d" % r)
        act(RF[:, CAP * me:CAP * me + CAP], SF[:, CAP * me:CAP * me + CAP], r=["SF%d" % r], w=["RF%d" % r])
        mm([(ps(4, 256, 256 + S), ch("cnt"), T.val[:], True, True)], ["val", "cnt"], pk(4, 256, 256 + S))
        act(T.sg[:, r, :], ps(4, 256, 256 + S), AF.Sign, pk(4, 256, 256 + S), ["sg%d" % r], bias=0.03125, scale=-1.0)
        tag("ht")
        cp(T.ST[:].indirect(T.slot[:]), T.tgc[:], ["slot", "tgc"], ["ST"], k="s")
        send("t", r, lambda o: T.ST[:, CAP * o:CAP * o + CAP], RT[:, CAP * me:CAP * me + CAP], ["ST"] + ["Mrow%d" % k for k in range(4)], [], "RTr%d" % r)
        act(RT[:, CAP * me:CAP * me + CAP], T.ST[:, CAP * me:CAP * me + CAP], r=["ST"], w=["RT%d" % r])

    Mk = ["M"] + ["Mrow%d" % k for k in range(4)] + ["Mwrap%d" % k for k in range(1, 4)]
    Ck = ["C%d" % k for k in range(4)]

    def owner_values(r):
        tag("hash")
        RF = T["RF%d" % r]
        rf = ["RF%d" % r, "RFr%d" % r] + MBk[0]
        for j in (1, 0, 2):
            mm(group(ps(4, 64 * j, 64 * j + 64), [(T.MB[:, j, 12 - 4 * q:140 - 4 * q], RF[:, q:256:4]) for q in range(4)]), rf, pk(4, 64 * j, 64 * j + 64))
        for k, b, lo in ((4, 5, 256), (3, 5, 0), (5, 3, 0)):
            mm([(ps(b, lo, lo + 256), T.MB[:, k, 0:128], RF[:], True, True)], rf, pk(b, lo, lo + 256))
        cp(T.hv[:], ps(4, 64, 128), pk(4, 64, 128), ["hv"])
        tt(T.hp[:], ps(4, 0, 64), T.hv[:], A.mult, ["hv"] + pk(4, 0, 64), ["hp"])
        tt(T.hi[:], ps(4, 128, 192), T.hp[:], A.add, ["hp"] + pk(4, 128, 192), ["hi"])
        ts(T.hi[:], T.hi[:], 2, 4095, A.arith_shift_right, A.bitwise_and, w=["hi"])
        cp(T.ML[:], T.hi[:], ["hi"], ["ML"])
        for k, (lo, n) in enumerate(LCH):
            tag("mo%d" % k)
            pick(MGQ[k], T.Mo[:, 4 * lo:4 * (lo + n)], T.M[:, 256:4352].indirect(T.ML[:, lo // 4:(lo + n) // 4]), Mk + ["ML"], ["Mo%d" % k])
        tag("hashb")
        act(T.bv[:], ps(5, 256, 512), r=pk(5, 256, 512), w=["bv"])
        for k, (lo, n) in enumerate(BCH):
            sl = slice(lo, lo + n)
            tt(T.bv[:, sl], ps(5, lo, lo + n), T.bv[:, sl], A.mult, ["bv"] + pk(5, lo, lo + n), ["bp%d" % k])
            tt(T.bi[:, sl], ps(3, lo, lo + n), T.bv[:, sl], A.add, ["bp%d" % k] + pk(3, lo, lo + n), ["bi%d" % k])
            ts(T.bi[:, sl], T.bi[:, sl], 2, 127, A.arith_shift_right, A.bitwise_and, w=["bi%d" % k])
            ts(T.BB[:, sl], T.bi[:, sl], 16.0, None, A.mult, r=["bi%d" % k], w=["BB%d" % j for j in range(lo // 32, (lo + n) // 32)])
        tag("hashw")
        for j in (1, 0, 2):
            mm(group(ps(6, 256 + 64 * j, 320 + 64 * j), [(T.MB[:, 6 + j, 12 - 4 * q:140 - 4 * q], RF[:, q:256:4]) for q in range(4)]), rf,
               pk(6, 256 + 64 * j, 320 + 64 * j))
        act(T.fv[:], ps(6, 320, 384), r=pk(6, 320, 384), w=["fv"])
        tt(T.fv[:], ps(6, 256, 320), T.fv[:], A.mult, pk(6, 256, 320), ["fv"])
        tt(T.fi[:], ps(6, 384, 448), T.fv[:], A.add, pk(6, 384, 448) + ["fv"], ["fi"])
        ts(T.fi[:], T.fi[:], 2, 4095, A.arith_shift_right, A.bitwise_and, w=["fi"])
        ts(T.Q[:], T.fi[:], col(SUB), None, A.subtract, r=["fi", "SUB"], w=["Q"])
        for k, (lo, n) in enumerate(LCH):
            tag("fc%d" % k)
            b, c0, nv = 2 + k % 2, 256 + sum(m for _, m in LCH[k % 2:k:2]), FGV[k]
            pairs = [(I, T.BB[:, lo:lo + n])] + [(T.MB[:, 9, 12 - 4 * x:140 - 4 * x], T.Mo[:, 4 * lo + x:4 * (lo + n):4]) for x in range(4)]
            mm(group(ps(b, c0, c0 + n), pairs), ["BB%d" % j for j in range(lo // 32, (lo + n) // 32)] + ["Mo%d" % k, "IW"] + MBk[0], pk(b, c0, c0 + n))
            cp(T.FL[:, lo:lo + n], ps(b, c0, c0 + n), pk(b, c0, c0 + n), ["FL%d" % k])
            tag("fg%d" % k)
            if nv < n:
                act(T.VG[:, 16 * (lo + nv):16 * (lo + n)], T.F[:, 0:2048].indirect(T.FL[:, lo + nv:lo + n]), AF.Identity, Fk + ["FL%d" % k], ["VG%d" % k], k="g", bias=-128.0)
            if nv:
                ts(T.VG[:, 16 * lo:16 * (lo + nv)], T.F[:, 0:2048].indirect(T.FL[:, lo:lo + nv]), -128.0, None, A.add, r=Fk + ["FL%d" % k], w=["VV%d" % k], k="g")
        tag("W")
        for name, b in (("r1", 2), ("r2", 7), ("rs", 6)):
            mm([(ps(b, 0, 256), cb(name), RF[:], True, True)], rf[0:2] + [name], pk(b, 0, 256))
        for j, (out, b) in enumerate(((T.D0[:, 1:1024:4], 2), (T.D0[:, 2:1024:4], 7), (T.D0[:, 3:1024:4], 2), (T.R5[:, 4:1280:5], 6))):
            if EVAC[j] == "v":
                cp(out, ps(b, 0, 256), pk(b, 0, 256), ["D0%d" % (j + 1)])
            else:
                act(out, ps(b, 0, 256), r=pk(b, 0, 256), w=["D0%d" % (j + 1)])
        wp = lambda cd, lo, hi: (cd // 2, 256 * (cd % 2) + lo, 256 * (cd % 2) + hi)
        for cd in range(4):
            mm([(ps(*wp(cd, 0, 256)), cb("w%d" % cd), RF[:], True, True)], rf[0:2] + ["w%d" % cd], pk(*wp(cd, 0, 256)))
        tag("diag")
        mm(group(ps(7, 256, 272), [(ch("ZA", 12 - 4 * a), T.Q[:, a:64:4]) for a in range(4)]), ["Q", "ZA"], pk(7, 256, 272))
        mm([(T.P6[:, q:256:4], ch("b%d" % q), T.Q[:], True, True) for q in range(4)], ["Q", "b0", "b1", "b2", "b3"], pk(6, 0, 256))
        tag("keys")
        ts(T.AI[:, 0:16], ps(7, 256, 272), 4196352.0, None, A.add, r=pk(7, 256, 272), w=["AI"])
        ts(T.BI[:], T.AI[:, 0:16], 12, 2032, A.arith_shift_right, A.bitwise_and, r=["AI"], w=["BI"])
        ts(T.AI[:, 16:32], T.AI[:, 0:16], 16383, None, A.bitwise_and, r=["AI"], w=["AL"])
        ts(T.KY[:, 0:16], T.AI[:, 16:32], -8192.0, 0.0, A.add, A.max, r=["AL"], w=["KYc"])
        ts(T.KL[:, 0:16], T.AI[:, 16:32], -8192.0, 0.0, A.add, A.max, r=["AL"], w=["KLc"])
        if EQV:
            ts(T.KS[:, 0:16], T.AI[:, 16:32], -10240.0, None, A.add, r=["AL"], w=["KSc"])
            act(T.KR[:, 0:256], ps(6, 0, 256), r=pk(6, 0, 256), w=["KR0"])
        if EQV < 8:
            ts(T.KN[:], T.AI[:, 16:32], -1.0, 10240.0, A.mult, A.add, r=["AL"], w=["KSn"])
        ts(T.dd[:], T.AI[:, 16:32], 8192.0, -8192.0, A.is_lt, A.mult, r=["AL"], w=["dd"])
        cp(T.UL[:, 0:16], T.BI[:], ["BI"], ["UL0"])
        for k in range(4):
            n = 16 << k
            ts(T.UL[:, n:2 * n], T.UL[:, 0:n], float(1 << k), None, A.add, r=["UL%d" % j for j in range(k + 1)], w=["UL%d" % (k + 1)], k=0.5)
        tag("ms")
        pick(GQ[0], T.Ms[:], T.M[:, 256:4352].indirect(T.KL[:, 0:16]), Mk + ["KLc"], ["Ms"])
        yb = T["yb%d" % r]
        yk = ["yb%d_%d" % (r, o) for o in range(N)]
        for k, (lo, n) in enumerate(LCH):
            tag("mul%d" % k)
            for cd in range(4):
                scan(T.VL[:, 1024 * cd + 4 * lo:1024 * cd + 4 * (lo + n)], T.D0[:, 4 * lo:4 * (lo + n)], T.VG[:, 16 * lo + cd:16 * (lo + n):4], 0.0,
                     A.mult, A.add, ["VG%d" % k, "VV%d" % k, "D0z", "D01", "D02", "D03"],
                     ["VL%d_%d" % (o, cd) for o in range(lo // 32, (lo + n) // 32)], k=0.5)
        for k, part in enumerate(YP):
            tag("sum%d" % k)
            lo, hi = 32 * part[0], 32 * part[-1] + 32
            for cd in range(4):
                tt(T.PD[:, 5 * lo + cd:5 * hi:5], T.VL[:, 1024 * cd + 4 * lo + 3:1024 * cd + 4 * hi:4], ps(*wp(cd, lo, hi)), A.mult,
                   ["VL%d_%d" % (o, cd) for o in part] + pk(*wp(cd, lo, hi)), ["PD%d_%d" % (k, cd)])
            scan(T.Y5[:, 5 * lo:5 * hi], T.R5[:, 5 * lo:5 * hi], T.PD[:, 5 * lo:5 * hi], 0.0, A.mult, A.add,
                 ["PD%d_%d" % (k, cd) for cd in range(4)] + ["PDk", "R50", "R51", "R52", "R53", "D04"], ["Y5%d" % k])
            ts(yb[:, lo:hi], T.Y5[:, 5 * lo + 4:5 * hi:5], -1152.0, None, A.add, r=["Y5%d" % k], w=[yk[o] for o in part], k=0.5)
        tag("ys")
        for k, part in enumerate(YP):
            send("y", r, lambda o: yb[:, CAP * o:CAP * o + CAP], T.RY[:, CAP * me:CAP * me + CAP], [yk[o] for o in part], [], "RYr%d" % k, YP, k)
        act(T.RY[:, CAP * me:CAP * me + CAP], yb[:, CAP * me:CAP * me + CAP], r=yk, w=["RY"])

    def losers(r, k):
        tag("eq%d" % k)
        EQ = T["EQ%d" % k]
        end = lambda c: 128 * (c // 8 + 1)
        for c in range(16):
            if k == 0 and c % 8 >= EQV:
                eq = EQ[:, c, 0:end(c) - 16 * c]
                act(eq, ps(6, 16 * c, end(c)), AF.Abs, pk(6, 16 * c, end(c)) + ["KSn"], ["EQ0_%d" % c], bias=T.KN[:, c:c + 1])
                act(eq, eq, AF.Relu, [], ["EQ0_%d" % c], bias=1.0, scale=-1.0)
                continue
            ts(EQ[:, c, 0:end(c) - 16 * c], T.KR[:, 256 * k + 16 * c:256 * k + end(c)], T.KS[:, 16 * k + c:16 * k + c + 1], None, A.is_equal,
               r=["KR%d" % k, "KS" + "cf"[k]], w=["EQ%d_%d" % (k, c)], k=0.5)
        tag("cnt%d" % k)
        b, o = (6, 256) if k == 0 else (5, 0)
        eq = ["EQ%d_%d" % (k, c) for c in range(16)]
        if PEN:
            items = [(ps(b, o, o + 256), cb("pen"), T["RF%d" % r][:], True, False)]
            items += [(ps(b, o + 16 * (c + 1), o + end(c)), cb("big"), EQ[:, c, 16:end(c) - 16 * c], False, False) for c in range(16) if c % 8 < 7]
            items += [(ps(b, o, o + 256), cb("pow"), EQ[:, :, 0:16], False, True)]
            mm(items[0:5], eq[0:4] + ["pen", "big", "RF%d" % r, "RFr%d" % r], pk(b))
            mm(items[5:8], eq[4:8], pk(b), acc=True)
            mm(items[8:12], eq[8:12], pk(b), acc=True)
            mm(items[12:], eq + ["pow"], pk(b), acc=True)
        else:
            items = [(ps(b, o, o + 256), cb("pow"), EQ[:, :, 0:16], True, False)]
            items += [(ps(b, o + 16 * (c + 1), o + end(c)), cb("big"), EQ[:, c, 16:end(c) - 16 * c], False, c == 14) for c in range(16) if c % 8 < 7]
            mm(items[0:4], eq + ["pow", "big"], pk(b))
            mm(items[4:8], [], pk(b), acc=True)
            mm(items[8:11], [], pk(b), acc=True)
            mm(items[11:], [], pk(b), acc=True)
        act(T.LS[:, 256 * k:256 * k + 256], ps(b, o, o + 256), AF.Identity, pk(b, o, o + 256), ["LS%d" % k], bias=131072.0 * PEN)

    def put(win, k, src, r, w):
        for hf in (1, 0):
            cp(win.indirect(T.OL[:, 16 * k + 8 * hf:16 * k + 8 * hf + 8]), src[:, 128 * hf:128 * hf + 128], r + ["OL"], w, k="s")

    def train(r):
        last = r == RO - 1
        tag("g")
        yb, RT = T["yb%d" % r], T["RT%d" % r]
        mm(group(ps(7, 288, 304), [(cb("Z3", 15 - k), T.Ms[:, k:256:16]) for k in range(16)]), ["Ms", "Z3"], pk(7, 288, 304))
        mm(group(ps(2, 256, 512), [(I, RT[:]), (cb("In"), yb[:])]), ["yb%d_%d" % (r, o) for o in range(N)] + ["RT%d" % r, "RTr%d" % r, "In", "IW"], pk(2, 256, 512))
        ts(T.GS[:], ps(2, 256, 512), 0.5, -0.5, A.min, A.max, r=pk(2, 256, 512), w=["GS"])
        tag("ug")
        for a, n in UGS:
            n = min(n, 16 - UGV - a)
            if n <= 0:
                continue
            ul = ["UL%d" % k for k in range(5) if 8 << k < 16 * (a + n)]
            act(T.UG[:, 256 * a:256 * (a + n)], T.F[:, 0:2048].indirect(T.UL[:, 16 * a:16 * (a + n)]), AF.Identity, Fk + ul,
                ["UG%d" % j for j in range(a, a + n)], k="g", bias=256.0)
        tag("fk")
        tt(T.KY[:, 16:32], ps(7, 288, 304), T.BI[:], A.add, pk(7, 288, 304) + ["BI"], ["KYf"])
        cp(T.KL[:, 16:32], T.KY[:, 16:32], ["KYf"], ["KLf"])
        tt(T.KS[:, 16:32], T.KY[:, 16:32], T.dd[:], A.add, ["KYf", "dd"], ["KSf"])
        tag("kr")
        pick(GQ[1], T.KR[:, 256:512], T.IOTA[:].indirect(T.KL[:, 16:32]), ["KLf"] + ["IOTA%d" % k for k in range(4)], ["KR1"])
        tag("co")
        pick(GQ[2], T.Co[:], T.C[:, 0:4096].indirect(T.KL[:, 0:16]), Ck + ["KLc"], ["Co"])
        tag("fo")
        pick(GQ[3], T.Fo[:], T.F[:, 0:2048].indirect(T.KL[:, 16:32]), Fk + ["KLf"], ["Fo"])
        losers(r, 0)
        losers(r, 1)
        tag("win")
        mm(group(ps(7, 304, 336), [(cb("Z3", 15 - k), T.LS[:, k:512:16]) for k in range(16)]), ["LS0", "LS1", "Z3"], pk(7, 304, 336))
        ts(T.bad[:], ps(7, 304, 336), col(THR), 65536.0, A.is_gt, A.mult, r=pk(7, 304, 336) + ["THR"], w=["bad"])
        tt(T.bad[:], T.bad[:], T.trash[:], A.min, ["trash"], ["bad"])
        if not PEN:
            for k in range(2):
                tt(T.KD[:, 16 * k:16 * k + 16], T.dd[:], T.tneg[:, 16 * k:16 * k + 16], A.mult, ["dd", "tneg"], ["KD%d" % k])
            tt(T.KD[:], T.KD[:], T.KY[:], A.max, ["KYc", "KYf"], ["KD0", "KD1"])
        tt(T.bad[:], T.bad[:], (T.KY if PEN else T.KD)[:], A.max, ["KYc", "KYf", "KD0", "KD1"], ["bad"])
        cp(T.OL[:], T.bad[:], ["bad"], ["OL"])
        tag("prod")
        mm([(ps(1, 0, 256), T.n256[:], T.GS[:], True, False)], ["GS", "n256"], pk(1), ["#1grp"])
        for j in range(16):
            if j >= 16 - UGV:
                op("v", lambda j=j: V.tensor_tensor(T.PR[:, 256 * j:256 * j + 256], T.F[:, 0:2048].indirect(T.UL[:, 16 * j:16 * j + 16]), T.GS[:], A.mult),
                   Fk + ["UL%d" % k for k in range(5)] + ["GS"], ["PR%d" % j], cost(256, "g"))
                continue
            scan(T.PR[:, 256 * j:256 * j + 256], T.UG[:, 256 * j:256 * j + 256], T.GS[:], 0.0, A.max, A.mult, ["UG%d" % j, "GS"], ["PR%d" % j], k=0.5)
        for j in PRO:
            mm([(ps(1, 0, 256), ch("Zh", 15 - j), T.PR[:, 256 * j:256 * j + 256], False, j == PRO[-1])],
               ["PR%d" % j, "Zh"], ["usum"] if j == PRO[-1] else [], ["#1grp"])
        tag("wf")
        mm(group(ps(5, 256, 512), [(I, T.Fo[:]), (cb("I2"), T.GS[:])]), ["Fo", "GS", "I2", "IW"], pk(5, 256, 512))
        ts(T.Fn[:], ps(5, 256, 512), 255.0, 0.0, A.min, A.max, r=pk(5, 256, 512), w=["Fn"])
        put(T.F[:], 1, T.Fn, ["Fn"], Fk)
        tag("nc")
        act(ps(1, 256, 512), ps(1, 0, 256), AF.Sign, pk(1, 0, 256) + ["usum"], pk(1, 256, 512))
        tt(T.Cn[:], ps(1, 256, 512), T.Co[:], A.add, pk(1, 256, 512) + ["Co"], ["Cn"])
        if last:
            return
        tag("wm")
        op("v", lambda: V.transpose(T.TR[:], T.Cn[:]), ["Cn"], ["TR"], cost(256, 0.5))
        scan(T.sn[:], T.RST[:], T.TR[:], 0.0, A.add, A.max, ["TR", "RST"], ["sn"])
        ts(T.e16[:], T.sn[:, 15:256:16], 16.0, None, A.mult, r=["sn"], w=["e16"])
        ts(T.e16[:], T.e16[:], 15, None, A.bitwise_and, w=["e16"])
        ts(T.TB[:, 0:256:16], T.e16[:], -1.0, 15.0, A.mult, A.add, r=["e16"], w=["TB"])
        op("v", lambda: V.transpose(T.Mn[:], T.TB[:]), ["TB"], ["Mn"], cost(256, 0.5))
        put(T.M[:, 256:4864], 0, T.Mn, ["Mn"], Mk)
        if WRS:
            act(T.M[:, 4352:4608], T.M[:, 256:512], w=["M"])
            for k in range(1, 4):
                dma("y", T.M[k:128:16, 256:4352], T.M[0:128:16, 256 + OFF[k]:4352 + OFF[k]], "dm%d" % (r + 1), r=["M"], w=["Mrow%d" % k])
        else:
            for k in range(1, 4):
                dma("y", T.M[k:128:16, 256:4352 - OFF[k]], T.M[0:128:16, 256 + OFF[k]:4352], "dm%d" % (r + 1), r=["M"], w=["Mrow%d" % k])
            for k in range(1, 4):
                dma("y", T.M[k:128:16, 4352 - OFF[k]:4352], T.M[0:128:16, 256:256 + OFF[k]], "dm%d" % (r + 1), r=["M"], w=["Mwrap%d" % k])
        tag("wc")
        put(T.C[:], 0, T.Cn, ["Cn"], Ck)

    YCk = ["YC"]
    home_route(0)
    for r in range(RO):
        now[0] = r
        owner_values(r)
        if r == RO - 1:
            tag("yc")
            for k in range(8):
                mm([(ps(4, 0, 256), cb("Zy", 15 - j), T.C[:, 256 * j:256 * j + 256], j == 0, j == 15) for j in range(2 * k, 2 * k + 2)],
                   Ck + ["Zy"], pk(4), acc=k > 0)
            act(T.YK[:], ps(4, 0, 256), r=pk(4), w=["YK"])
            dma("y", T.YC[0:128:16, 0:4096], T.YK[:], "dyc", r=["YK"], w=YCk)
        train(r)
        home_update(r)
        if r < RO - 1:
            home_route(r + 1)
    tag("end")
    mm([(ps(6, 0, 256), cb("ycw"), T.Cn[:], True, True)], ["Cn", "ycw"], pk(6, 0, 256))
    act(T.ycn[:], ps(6, 0, 256), r=pk(6, 0, 256), w=["ycn"])
    put(T.YC[:], 0, T.ycn, ["ycn"], YCk)
    dma("y", T.yc[:], T.YC[0:128:16, 0:4096], "out", r=YCk, lat=2.6)
    dma("y", T.yf[:], T.F[:, 0:2048], "out", r=Fk, lat=3.2)
    act(T.xO[:], ps(3, 0, S), AF.Identity, pk(3) + ["KX"], ["xO"], bias=col(KX))
    mm(group(ps(4, 0, S), [(cb("I64"), T.sg[:, k, :]) for k in range(RO)] + [(I, T.yg[:, k, :]) for k in range(RO)]),
       ["sg%d" % k for k in range(RO)] + ["yg%d" % k for k in range(RO)] + ["I64", "IW"], pk(4, 0, S))
    act(T.ysO[:], ps(4, 0, S), AF.Identity, pk(4, 0, S), ["ysO"], bias=192.0)
    for e in range(4):
        dma("ys"[e % 2], T.yx[e:32:4, :], T.xO[4 * e:128:16, :], "out", r=["xO"])
    dma("s", T.ys[:], T.ysO[:], "out", r=["ysO"])
    if not ORDER:
        rng = np.random.default_rng(1)
        label = [(e["tag"] + e["q"], e["tag"]) for e in ops]
        names = sorted({a for a, _ in label}) + sorted({b for _, b in label})
        net = graph()
        brief.extend((e["c"], e["q"], e["lat"], e["x"]) for e in ops)
        marks.extend(i for i, e in enumerate(ops) if e["kind"] != "c")
        best = now_ = schedule(net, [-v for v in net[2]], True)
        for it in range(TRIES):
            wide = 1.5 * float(rng.random()) + 0.3
            move = {names[k]: wide * float(rng.standard_normal()) for k in rng.integers(0, len(names), int(rng.integers(1, MOVES)))}
            key = [t + move.get(a, 0.0) + move.get(b, 0.0) for t, (a, b) in zip(now_[1], label)]
            for i in rng.integers(0, len(ops), ONES):
                key[i] += wide * float(rng.standard_normal())
            got = schedule(net, key, it % BOTH == 0)
            if got[0] <= now_[0] + HEAT * (1.0 - it / TRIES) * float(rng.random()):
                now_ = got
            if got[0] <= best[0]:
                best = got
        ORDER.extend([best[2], sorted(range(len(ops)), key=lambda i: (best[1][i], i)), net, ops])
    for i in ORDER[1]:
        emit(ops[i])
    for sem, val in total.items():
        need("y", (sem, val))
